import numpy as np, ml_dtypes
CORES = [24,25,26,27,28,29,30,31]
N = 8
BF = ml_dtypes.bfloat16
def gentries(a):
    return np.ascontiguousarray(a.reshape(8, 16, -1).transpose(0, 2, 1)).reshape(8, -1)
def gtable(e):
    e = np.asarray(e); return np.ascontiguousarray(e.reshape(8, -1, 16).transpose(0, 2, 1)).reshape(128, -1).astype(np.int32)
W, LW, RO, E, LN = 2048, 11, 2, 2, 3
T = 3 * W // 4
def curves(rng):
    p = rng.choice(np.array([0.7, 1.0, 1.4], np.float32), (N, 8, 16, 1))
    return np.minimum((16 * rng.random((N, 8, 16, W), dtype=np.float32) ** p).astype(np.int64), 15)
def load(rng):
    return ((0.5 + 1.5 * rng.random((N, 128, W), dtype=np.float32)) * np.exp2(2 * rng.random((N, 1, W)) - 1).astype(np.float32)).astype(np.float32)
def roots(rng):
    return (0.875 + 0.25 * rng.random((N, 128, 5))).astype(np.float32)
def warp(rng, *lead):
    u = np.sort(rng.random(lead + (W,)), axis=-1); k = rng.integers(1, 4, lead + (1,)); a = rng.uniform(-0.9, 0.9, lead + (1,))
    w = np.clip(np.floor(W * (u + a * np.array([0.15915, 0.07957, 0.05305])[k - 1] * np.sin(6.283185307179586 * k * u))).astype(np.int64), 0, W - 1)
    back = rng.integers(1, 40, lead + (W // 16,)) * (rng.random(lead + (W // 16,)) < 0.15)
    turn = 7 * (rng.random(lead + (W // 8,)) < 0.1)
    i = np.maximum(np.arange(W) - np.repeat(back, 16, axis=-1), 0) ^ np.repeat(turn, 8, axis=-1)
    return np.take_along_axis(w, i, -1)
def cliffs(rng, *lead):
    j = np.arange(W); w = np.sort(rng.integers(0, W - 1, lead + (W,)), axis=-1)[..., np.minimum(4 * j // 3, W - 1)]; r = rng.random(lead + (W,))
    e = np.where(j < T, np.where(r < 0.45, w, 0), np.where(r < 0.6, W - 1, 0))
    e[..., 0] = 0; e[..., W - 1] = W - 1
    return e
def pack(x, v, rt, e, ga):
    return {"xs": np.ascontiguousarray(x.reshape(N, 128, W)).astype(np.float32).astype(BF), "pay": v.astype(BF), "rho": rt.astype(np.float32),
            "ew": np.stack([gtable(a.reshape(8, -1)) for a in e]), "gam": np.stack([gtable(a) for a in ga])}
def setup_inputs(rng):
    return pack(curves(rng), load(rng), roots(rng), warp(rng, N, 8, RO, E), warp(rng, N, 8))
def setup_inputs_spread(rng):
    p = np.exp2(rng.uniform(-2, 2, (N, 8, 1, W))).astype(np.float32)
    x = np.minimum((16 * rng.random((N, 8, 16, W), dtype=np.float32) ** p).astype(np.int64), 15)
    e = warp(rng, N, 8, RO, E); e[:, 1::2] = rng.integers(0, W, (N, 4, RO, E, W))
    return pack(x, load(rng), roots(rng), e, warp(rng, N, 8))
def setup_inputs_ends(rng):
    x = 15 * (rng.random((N, 8, 16, W)) < rng.choice(np.array([0.15, 0.5, 0.85]), (N, 8, 1, 1))).astype(np.int64)
    x[0, 0] = 15; x[0, 4] = 15; x[0, 7] = 15; x[N - 1, 7] = 0; x[2, 3] = 0
    x[1, 7] = 0; x[1, 7, 15, W - 1] = 15
    e = cliffs(rng, N, 8, RO, E); ga = cliffs(rng, N, 8)
    e[:, 2::3] = (W - 1) * rng.integers(0, 2, e[:, 2::3].shape)
    e[1, 7, 0, 1:, T:W - 1] = 0; e[1, 7, 0, 0, T:] = ga[2, 0, T:]
    h = T + int(np.argmax(e[1, 7, 0, 0, T:] == W - 1)); e[1, 7, 0, 0, h] = 0
    for q, g in ((N - 1, 6), (1, 3)):
        a = (q + 1) % N
        x[q, g] = 0; x[q, g, 15, W - 1] = 1
        ga[a, g + 1, W - 32:W - 1] = 0
        e[q, g, 0, 1:, T:W - 1] = 0; e[q, g, 0, 0, T:] = ga[a, g + 1, T:]; e[q, g, 0, 0, W - 1] = 0
    v = np.where(rng.random((N, 128, W)) < 0.7, 4.0, 0.25)
    rt = 0.875 + 0.25 * rng.integers(0, 2, (N, 128, 5))
    return pack(x, v.astype(np.float32), rt, e, ga)
def setup_inputs_corners(rng):
    j = np.arange(W)
    kinds = np.stack([j, W - 1 - j, 0 * j, 0 * j + W - 1, np.minimum(3 * j, W - 1), np.minimum(4 * j, W - 1), j >> 1, (5 * j) & (W - 1)])
    o = rng.permutation(8); k = o[(np.arange(N)[:, None] + np.arange(8)) % 8]
    ga = kinds[k]; e = kinds[rng.integers(0, 8, (N, 8, RO, E))]
    e = np.where(rng.random((N, 8, RO, E, 1)) < 0.3, rng.integers(0, W, e.shape), e)
    x = curves(rng); off = int(rng.integers(0, 8))
    for q in range(N):
        for g in range(8):
            m = (3 * q + g + off) % 8
            if m == 0: x[q, g] = 0
            elif m == 1: x[q, g] = 15
            elif m == 2: x[q, g] = rng.integers(0, 16, (16, 1))
            elif m == 3: x[q, g] = (16 * j) >> LW
            elif m == 4: x[q, g] = 0; x[q, g, :, W - 1] = 15
    return pack(x, load(rng), roots(rng), e, ga)
def setup_inputs_ties(rng):
    x = curves(rng); e = warp(rng, N, 8, RO, E); ga = warp(rng, N, 8); j = np.arange(W); a = int(rng.integers(0, N)); b = (a + 1) % N
    x[:, ::2] = np.where((j & 2) > 0, 15, np.minimum(x[:, ::2], 14))
    x[a, 1::2] = 15; x[b, 1::4] = rng.integers(0, 16, (2, 16, 1))
    base = (j & ~3) | 2
    e[:, ::2, 0, 0] = base + rng.integers(0, 2, (N, 4, W)); ga[:, 1::2] = base + rng.integers(0, 2, (N, 4, W))
    e[1::2, ::2, 0, 0, W - 1] = W - 4
    x[1::2, ::2, :, W - 4] = 15; x[1::2, ::2, int(rng.integers(0, 16)), W - 4] = 14
    x[0, 6] = np.where((j & 2) == 0, 15, np.minimum(x[0, 6], 14)); ga[1, 7] = (j & ~3) + 1; e[0, 6, 0] = warp(rng, E)
    return pack(x, load(rng), roots(rng), e, ga)
def check_ranges(d):
    bad = []
    for k, lo, hi in (("xs", 0, 15), ("pay", 0.25, 4), ("rho", 0.875, 1.125), ("ew", 0, W - 1), ("gam", 0, W - 1)):
        v = np.asarray(d[k]).astype(np.float64)
        if not (np.min(v) >= lo and np.max(v) <= hi): bad.append("range of " + k)
    v = np.asarray(d["xs"]).astype(np.float64)
    if not np.all(v == np.floor(v)): bad.append("xs is not whole")
    return bad
def pick(a, c):
    return np.take_along_axis(a, c[:, :, None, :], 3)
def inverse(w):
    w = w.reshape(-1, W); top = np.maximum.accumulate(w, axis=1)
    before = np.concatenate([np.full((len(w), 1), -1, np.int64), top[:, :-1]], axis=1)
    i, j = np.nonzero(w > before); t = np.zeros(w.shape, np.int64); t[i, w[i, j]] = j
    return np.maximum.accumulate(t, axis=1).reshape(N, 8, W)
def root(rt, c):
    s = np.concatenate([np.minimum(np.abs(c[..., 1:] - c[..., :-1]), 4), np.ones((N, 8, 1), np.int64)], axis=-1)
    return pick(rt, s)
def reference(xs, pay, rho, ew, gam):
    x = xs.astype(np.int64).reshape(N, 8, 16, W); p0 = pay.astype(np.float64).reshape(N, 8, 16, W); rt = rho.astype(np.float64).reshape(N, 8, 16, 5)
    e = np.stack([gentries(a) for a in ew]).astype(np.int64).reshape(N, 8, RO, E, W); ga = np.stack([gentries(a) for a in gam]).astype(np.int64)
    v = p0; m = np.maximum.reduce(x, axis=0)
    stay = np.broadcast_to(np.arange(W), (N, 8, W))
    for t in range(RO):
        gn = np.roll(np.roll(ga, -1, axis=0), -1, axis=1)
        tr = np.stack([stay] + [e[:, :, t, i] for i in range(E)] + [gn, inverse(gn)])
        mn = np.roll(m, -1, axis=0)[None]
        sc = np.stack([np.sum(np.abs(pick(x, c) - mn), axis=(2, 3)) for c in tr])
        b = np.argmin(sc, axis=0)
        c = np.take_along_axis(tr, b[None, :, :, None], 0)[0]
        x = pick(x, c); v = pick(v, c) * root(rt, c); ga = np.take_along_axis(ga, c, 2)
        mu = np.add.reduce(inverse(ga), axis=0) >> LN
        mu = np.broadcast_to(mu, (N, 8, W))
        x = pick(x, mu); v = pick(v, mu) * root(rt, mu); ga = np.take_along_axis(ga, mu, 2)
        m = np.maximum.reduce(x, axis=0)
        v = v + m * 0.03125
    u = v + x * 0.0625 + pick(p0, ga)
    y = (np.add.reduce(u, axis=0) * 0.125).reshape(128, W)
    n = W // N
    return {"y": np.stack([y[:, r * n:(r + 1) * n] for r in range(N)]).astype(np.float32)}

def check_inputs(d):
    bad = list(check_ranges(d))
    if not bad:
        for name, y in reference(**d).items():
            for q in range(N):
                v = np.abs(np.asarray(y[q], np.float64)); s = np.sqrt(np.mean(v * v))
                if v.max() > 3 * s or s < 2.0 ** 0: bad.append('%s of rank %d is uneven or too small' % (name, q))
    return bad

@@ -1,0 +1,597 @@
+from concourse.bass import DstId, RemoteDMATransfer
+from concourse.mybir import AluOpType as ALU, AxisListType as AX, ActivationFunctionType as AF
+
+W = 2048
+H = W // 2
+PW = 256
+KV = [64, 64, 54, 64]
+GV = (768, 1408)
+NVAL_V = 4
+TAIL = [2, 3, 2]
+MAGIC = 12582912.0
+
+SCRATCH = {}
+
+
+def _buf(where, dtype, cols, *names, rows=128):
+    for n in names:
+        SCRATCH[n] = (where, [rows, cols], dtype)
+
+
+_buf("sbuf", "bfloat16", W, "X0", "X1", "X2", "X3", "payS", "P3", "ENC", "G0", "G1", "G2", "G3", "IR", "M0", "M1",
+     "dA", "d2", "d3", "d4", "junk", "pc", "xq", "pq")
+_buf("sbuf", "bfloat16", W + 16, "TOP")
+_buf("sbuf", "float32", W, "VAL", "V1", "V2", "V3", "tmp", "U", "QM", "uq")
+for _n in range(2):
+    _buf("sbuf", "bfloat16", W + 112 + 16 * max(KV[_n::2]), "WV%d" % _n)
+    _buf("sbuf", "float32", W + 112 + 16 * (128 - min(KV[_n::2])), "WA%d" % _n)
+_buf("sbuf", "bfloat16", 3 * PW, "t3")
+_buf("sbuf", "bfloat16", H, "cB")
+_buf("sbuf", "int32", 128, "gamI")
+_buf("sbuf", "int32", 512, "ewI")
+_buf("sbuf", "uint16", 512, "ewU")
+_buf("sbuf", "uint16", 128, "gamU", "offU", "cU0", "cU1", "muU0", "muU1", "sU", "glU")
+_buf("sbuf", "uint16", 256, "nbS0", "nbS1", "nbR0", "nbR1")
+_buf("sbuf", "uint16", 8, "eo")
+_buf("sbuf", "float16", 128, "ivS0", "ivS1", "I8h", "cmu")
+_buf("sbuf", "float16", 7 * 128, "ivR0", "ivR1")
+_buf("sbuf", "int32", 2, "iP")
+_buf("sbuf", "int32", 4, "iC")
+_buf("sbuf", "float32", 8, "fC", "base5", "Tc", "acc1", "acc2", "acc3", "km", "rhoS")
+_buf("sbuf", "float32", 144, "iF", "Ts")
+_buf("sbuf", "float32", 128, "iG", "iF64", "Grp8", "E1", "E2", "E3", *["DD%d" % _k for _k in sorted(set(KV))])
+_buf("sbuf", "float16", 128, "c16", "I16", "S1", "S2", "D15", "C4")
+_buf("sbuf", "float32", 16, "EQ", "GT", "GT64")
+_buf("sbuf", "float32", 64, "R9")
+_buf("sbuf", "float32", 640, "Lall")
+_buf("sbuf", "bfloat16", 144, "Wd", "Wd2", "WdB")
+_buf("sbuf", "bfloat16", 128, "Ip", "In", "I8", "I32b", "I128b")
+_buf("sbuf", "bfloat16", PW, "qM", "qS")
+_buf("sbuf", "float32", PW, "qg", "ysb")
+_buf("dram", "bfloat16", PW, "dM0", "dM1", rows=8 * 128 + 16)
+_buf("psum", "float32", 1024, "pA", "pB")
+_buf("psum", "float32", 512, "pT", "pL", "pK", "pS")
+
+SEMAPHORES = (["qv", "qa", "qt", "qg", "sent", "lgam", "lxs", "lew", "lrho", "lpay", "own0", "own1", "fill0", "fill1",
+               "fill2", "fill3", "accm", "sty", "ax", "ap", "aqm"]
+              + ["%s%d" % (s, t) for s in ("rs", "ag", "ec", "nb", "mu") for t in range(2)]
+              + ["au%d" % k for k in range(len(TAIL))])
+QSEM = {"v": "qv", "a": "qa", "t": "qt", "g": "qg"}
+
+
+def _overlap(a, b):
+    if a[0] != b[0] or a[2] <= b[1] or b[2] <= a[1]:
+        return False
+    if a[3] > 1 and a[3] == b[3] and (a[1] - b[1]) % a[3]:
+        return False
+    return True
+
+
+def _emit(g, T, ops):
+    Q = {"v": g.vector, "a": g.scalar, "t": g.tensor, "g": g, "s": g.sync}
+    total = {}
+    for o in ops:
+        if o["sem"]:
+            total[o["sem"]] = total.get(o["sem"], 0) + o["inc"]
+    hist, known = {}, {q: {} for q in Q}
+    for n, o in enumerate(ops):
+        deps = set(o["after"])
+        for regs, wr in ((o["ins"], False), (o["outs"], True)):
+            for x in regs:
+                ps = SCRATCH.get(x[0], ("",))[0] == "psum"
+                for (m, y, w2) in hist.get(x[0], []):
+                    p = ops[m]
+                    if m == n or (p["q"] == "t" and o["q"] == "t"):
+                        continue
+                    if ps and p["q"] != o["q"]:
+                        if x[1] // 512 <= (y[2] - 1) // 512 and y[1] // 512 <= (x[2] - 1) // 512:
+                            deps.add(m)
+                    elif (wr or w2) and _overlap(x, y):
+                        deps.add(m)
+        for regs, wr in ((o["ins"], False), (o["outs"], True)):
+            for x in regs:
+                hist.setdefault(x[0], []).append((n, x, wr))
+        o["waits"] = []
+        if o["q"] is None:
+            o["know"] = {}
+            continue
+        k = known[o["q"]]
+        for m in sorted(deps, reverse=True):
+            p = ops[m]
+            key, val = (p["sem"], 1 << 30) if p["sem"] else (p["q"], m)
+            if p["sem"] == "sent":
+                raise ValueError("a source of a remote write is overwritten")
+            if p["sem"] and p["sem"] == o["sem"]:
+                continue
+            if k.get(key, -1) >= val:
+                continue
+            o["waits"].append(m)
+            p["need"] = True
+            k[key] = val
+            if not p["sem"]:
+                for kk, vv in p["know"].items():
+                    if k.get(kk, -1) < vv:
+                        k[kk] = vv
+        o["know"] = dict(k)
+    count, waited = {}, {}
+    for o in ops:
+        if o["q"] and not o["sem"] and o["need"]:
+            count[o["q"]] = count.get(o["q"], 0) + 1
+            o["val"] = count[o["q"]]
+    for o in ops:
+        if o["q"] is None:
+            continue
+        for m in o["waits"]:
+            p = ops[m]
+            s, v = (p["sem"], total[p["sem"]]) if p["sem"] else (QSEM[p["q"]], p["val"])
+            Q[o["q"]].wait_ge(T.sem[s], v)
+            waited[s] = max(waited.get(s, 0), v)
+        ins = o["fn"]()
+        if o["sem"] and o["sem"] != "sent":
+            ins.then_inc(T.sem[o["sem"]], 16)
+        elif not o["sem"] and o["need"]:
+            ins.then_inc(T.sem[QSEM[o["q"]]], 1)
+    for q, c in count.items():
+        total[QSEM[q]] = c
+    for s, v in total.items():
+        if waited.get(s, 0) < v:
+            (g.sync if s == "sty" else g).wait_ge(T.sem[s], v)
+
+
+def rank_program(g, core, T, topo):
+    me = T.rank_of(core)
+    if me is None:
+        return
+    cores = list(T.cores)
+    N = len(cores)
+    ops = []
+    V, A, PE = g.vector, g.scalar, g.tensor
+
+    def sides(s):
+        same = [r for r in range(N) if topo.die(cores[r]) == topo.die(cores[s])]
+        return same, [r for r in range(N) if r not in same]
+
+    def dest(s, k):
+        same, other = sides(s)
+        i = same.index(s)
+        if k < len(other):
+            return other[(i + k) % len(other)]
+        return same[(i + k - len(other) + 1) % len(same)]
+
+    def prv(s):
+        same = sides(s)[0]
+        return same[(same.index(s) - 1) % len(same)]
+
+    def did(r):
+        a = topo.addr(cores[r])
+        return DstId(rid=a[0], pnc=a[1])
+
+    def bits(es):
+        return sum(1 << e for e in es)
+
+    nfar = len(sides(me)[1])
+    dests = [dest(me, k) for k in range(N - 1)]
+    eng = topo.engines(core, cores[dests[0]])
+    allm = bits(eng)
+
+    def two(k):
+        j, o = (k, 0) if k < nfar else (k - nfar, 1)
+        return bits([eng[4 * j + o], eng[4 * j + o + 2]])
+
+    def r(name, lo=0, hi=None, step=1, p=None):
+        if hi is None:
+            hi = T[name].shape[1]
+        ps = slice(None) if p is None else slice(p[0], p[1])
+        ap = T[name][ps, lo:hi:step] if step > 1 else T[name][ps, lo:hi]
+        return (ap, [(name, lo, hi, step)], [])
+
+    def rows(name, a, b):
+        return (T[name][a:b, :], [(name, a, b, 1)], [])
+
+    def ind(win, off):
+        return (win[0].indirect(off[0]), win[1], off[1])
+
+    def op(q, fn, outs, ins, sem=None, inc=16, after=()):
+        o = {"q": q, "fn": fn, "sem": sem, "inc": inc, "need": False, "after": list(after), "outs": [], "ins": []}
+        for x in outs:
+            o["outs"] += x[1]
+            o["ins"] += x[2]
+        for x in ins:
+            if isinstance(x, tuple):
+                o["ins"] += x[1] + x[2]
+        ops.append(o)
+        return len(ops) - 1
+
+    def a_(x):
+        return x[0] if isinstance(x, tuple) else x
+
+    def cp(o, i):
+        return op("v", lambda: V.tensor_copy(o[0], i[0]), [o], [i])
+
+    def tt(o, a, b, alu):
+        return op("v", lambda: V.tensor_tensor(o[0], a[0], b[0], alu), [o], [a, b])
+
+    def ts(o, a, s1, o0, s2=None, o1=None):
+        if o1 is None:
+            return op("v", lambda: V.tensor_scalar(o[0], a[0], a_(s1), None, o0), [o], [a, s1])
+        return op("v", lambda: V.tensor_scalar(o[0], a[0], a_(s1), a_(s2), o0, o1), [o], [a, s1, s2])
+
+    def ms(o, c):
+        return op("v", lambda: V.memset(o[0], c), [o], [])
+
+    def scan(o, a, b, init):
+        return op("v", lambda: V.tensor_tensor_scan(o[0], a[0], b[0], a_(init), ALU.max, ALU.max), [o], [a, b, init])
+
+    def act(o, i, f=AF.Identity, scale=None, bias=None, acc=None):
+        kw = {}
+        if scale is not None:
+            kw["scale"] = a_(scale)
+        if bias is not None:
+            kw["bias"] = a_(bias)
+        if acc is not None:
+            kw["accum_out"] = acc[0]
+        return op("a", lambda: A.activation(o[0], i[0], f, **kw), [o] + ([acc] if acc else []), [i, scale, bias])
+
+    def mm(o, l, x, st, sp):
+        return op("t", lambda: PE.matmul(o[0], l[0], x[0], st, sp), [o], [l, x])
+
+    def dma(q, o, i, sem, after=(), **kw):
+        e = {"s": g.sync, "a": A, "g": g}[q]
+        return op(q, lambda: e.dma_start(o[0], i[0], **kw), [o], [i], sem=sem, after=after)
+
+    def send(trs):
+        def fn():
+            return g.remote_dma_fused([RemoteDMATransfer(
+                dst_ids=[did(d) for d, _ in ds], dma_engine_mask=m, remote_sem=T.sem[s], srcs=[x[0] for x in ss],
+                dsts=[x[0] for _, x in ds], alu_op=f) for ss, ds, m, s, f in trs], local_sem=T.sem["sent"])
+        return op("g", fn, [], [x for t in trs for x in t[0]], sem="sent", inc=sum(bin(t[2]).count("1") for t in trs))
+
+    def arrive(sem, n, places):
+        return op(None, None, places, [], sem=sem, inc=n)
+
+    def piece(name, o):
+        return r(name, PW * o, PW * o + PW)
+
+    def col(name, j):
+        return r(name, j, j + 1)
+
+    def conv_list(ps, lo, row, sel, c0, c1):
+        n = (c1 - c0) // 16
+        for i in range(16):
+            mm(r(ps, lo, lo + n), r(sel, 15 - i, 143 - i), r(row, c0 + i, c1, 16), i == 0, i == 15)
+
+    def conv_block():
+        for i in range(16):
+            mm(r("pT", 0, 129), r("WdB", 15 - i, 143 - i), r("TOP", 15 + 128 * i, 144 + 128 * i), i == 0, i == 15)
+
+    def top_part(row, lo, hi):
+        x = r(row, lo, hi)
+        scan(r("TOP", 16 + lo, 16 + hi), x, x, col("TOP", 15 + lo) if lo else 0.0)
+
+    def offsets(n):
+        tt(r("E1"), r("pT", 0, 128), r("DD%d" % KV[n]), ALU.add)
+        ts(r("Ts", 0, 128), r("pT", 1, 129), 1.0 / 4096, ALU.mult)
+        tt(r("E2"), r("E1"), r("pT", 1, 129), ALU.subtract)
+        tt(r("E3"), r("E2"), r("Ts", 0, 128), ALU.max)
+        cp(r("offU"), r("E3"))
+
+    def iota(o, pat, base, cm):
+        op("g", lambda: g.iota(o[0], pat, base, cm, allow_small_or_imprecise_dtypes=True), [o], [])
+
+    def dummies(k):
+        iota(r("DD%d" % k, 0, k), [[16, k]], W, 1)
+        iota(r("DD%d" % k, k, 128), [[16, 128 - k]], W, 1)
+
+    def scatter_v(n):
+        cp(ind(r("WV%d" % (n % 2)), r("offU", 0, KV[n])), r("VAL", 0, 16 * KV[n]))
+
+    def scatter_a(n):
+        act(ind(r("WA%d" % (n % 2)), r("offU", KV[n], 128)), r("VAL", 16 * KV[n], W), AF.Silu)
+
+    def merge(n, sel, out):
+        sc = 4.0 if n > 1 else 1.0
+        for h in range(2):
+            scan(r("IR", H * h, H * h + H), r("WV%d" % (n % 2), H * h, H * h + H), r("WA%d" % (n % 2), H * h, H * h + H),
+                 col("IR", H - 1) if h else 64.0 * sc)
+            conv_list("pL", 64 * h, "IR", sel, H * h, H * h + H)
+        return lambda: ts(out, r("pL", 0, 128), 1.0 / sc, ALU.mult, -1024.0, ALU.add)
+
+    def warp_top(new, old, lst):
+        gather_v(new, old, lst, 0, GV[0])
+        gather_a(new, old, lst, GV[0], GV[1])
+        gather_a(new, old, lst, GV[1], W)
+        top_part(new, 0, GV[0])
+        top_part(new, GV[0], GV[1])
+        top_part(new, GV[1], W)
+        conv_block()
+
+    def slopes_pe():
+        mm(r("pS", 0, 128), r("I16"), r("C4"), True, False)
+        mm(r("pS", 0, 127), r("S2"), r("c16", 1, 128), False, False)
+        mm(r("pS", 127, 128), r("D15"), r("c16", 127, 128), False, False)
+        mm(r("pS", 0, 128), r("S1"), r("c16"), False, True)
+
+    def slopes_v():
+        ts(r("sU"), r("pS", 0, 128), 0.0, ALU.max, 8.0, ALU.min)
+
+    def weigh(out, src, tab, lo, hi, olo=None):
+        olo = lo if olo is None else olo
+        return tt(r(out, olo, olo + hi - lo), ind(r("R9", 16 * tab, 16 * tab + 9), r("sU", lo // 16, hi // 16)),
+                  r(src, olo, olo + hi - lo), ALU.mult)
+
+    def gather_a(out, win, lst, lo, hi, base=0, olo=None):
+        olo = lo if olo is None else olo
+        return act(r(out, olo, olo + hi - lo), ind(r(win), r(lst, base + lo // 16, base + hi // 16)))
+
+    def gather_v(out, win, lst, lo, hi):
+        return cp(r(out, lo, hi), ind(r(win), r(lst, lo // 16, hi // 16)))
+
+    def template(t, x, between=None):
+        d, m = "dM%d" % t, "M%d" % t
+        send([([piece(x, q)], [(q, rows(d, 128 * (k + 1), 128 * (k + 2)))], two(k), "rs%d" % t, 0)
+              for k, q in enumerate(dests)])
+        if between:
+            between()
+        arrive("rs%d" % t, 2 * (N - 1), [rows(d, 128, 128 * N)])
+        send([([rows(d, 128 * k + 16, 128 * k + 144) for k in range(N)], [(q, piece(m, me)) for q in dests], allm,
+               "ag%d" % t, 2)])
+        arrive("ag%d" % t, len(eng) * (N - 1), [piece(m, q) for q in dests])
+        send([([piece(m, prv(me))], [(prv(me), piece(m, prv(me)))], allm, "ec%d" % t, 0)])
+        arrive("ec%d" % t, len(eng), [piece(m, me)])
+
+    def own_piece(t, x):
+        d = "dM%d" % t
+        dma("s", rows(d, 0, 128), piece(x, me), "own%d" % t)
+        dma("s", rows(d, 128 * N, 128 * N + 16), r(x, PW * me, PW * me + PW, p=(0, 16)), "own%d" % t)
+
+    def neighbour(t):
+        send([([r("nbS%d" % t)], [((me - 1) % N, r("nbR%d" % t))], allm, "nb%d" % t, 0)])
+        return arrive("nb%d" % t, len(eng), [r("nbR%d" % t)])
+
+    def score_pe(t, tr, src, us=(0, 1)):
+        m = "M%d" % t
+        for u in us:
+            h = 1 - u if PW * me < H else u
+            ps = "pA" if u == 0 else "pB"
+            for c in range(2):
+                lo = H * h + 512 * c
+                mm(r(ps, 512 * c, 512 * c + 512), r("Ip"), r(src, lo, lo + 512), True, False)
+                mm(r(ps, 512 * c, 512 * c + 512), r("In"), r(m, lo, lo + 512), False, True)
+            act(r("junk", H * u, H * u + H), r(ps), AF.Abs, acc=col("acc1" if u == 0 else "acc2", tr))
+
+    def scores(t, x, extra):
+        m, nb = "M%d" % t, "nbR%d" % t
+        score_pe(t, 0, x, (1,))
+        score_pe(t, 1, "dA")
+        tt(r("d2"), ind(r(x), r("ewU", 256 * t + 128, 256 * t + 256)), r(m), ALU.subtract)
+        act(r("d2"), r("d2"), AF.Abs, acc=col("acc1", 2))
+        tt(r("d3"), ind(r(x), r(nb, 0, 128)), r(m), ALU.subtract)
+        act(r("d3"), r("d3"), AF.Abs, acc=col("acc1", 3))
+        for lo, hi, ac in ((0, 1024, "acc1"), (1024, 1664, "acc2"), (1664, W, "acc3")):
+            tt(r("d4", lo, hi), ind(r(x), r(nb, 128 + lo // 16, 128 + hi // 16)), r(m, lo, hi), ALU.subtract)
+            act(r("d4", lo, hi), r("d4", lo, hi), AF.Abs, acc=col(ac, 4))
+        cp(r("Lall", 3, 640, 5), r(nb, 0, 128))
+        cp(r("Lall", 4, 640, 5), r(nb, 128, 256))
+        extra()
+        mm(r("pK", 0, 5), r("Grp8"), r("Tc", 0, 5), True, False)
+        for j, ac in enumerate(("acc1", "acc2", "acc3")):
+            mm(r("pK", 0, 5), r("Grp8"), r(ac, 0, 5), False, j == 2)
+            mm(r("pS", 0, 5), r("Grp8"), r(ac, 0, 5), j == 0, j == 2)
+        for j, ps in enumerate(("pK", "pS")):
+            o, i = col("km", 4 * j), r(ps, 0, 5)
+            op("v", lambda o=o, i=i: V.tensor_reduce(o[0], i[0], AX.X, ALU.min), [o], [i])
+        ts(r("eo"), r("base5"), col("km", 0), ALU.add, col("km", 4), ALU.subtract)
+        cp(r("cU%d" % t), ind(r("Lall"), r("eo")))
+
+    def mean_send(t):
+        send([([r("ivS%d" % t)], [(q, r("ivR%d" % t, 128 * k, 128 * k + 128)) for k, q in enumerate(dests)], allm,
+               "mu%d" % t, 0)])
+        arrive("mu%d" % t, len(eng) * (N - 1), [r("ivR%d" % t)])
+
+    def mean_sum(t):
+        mm(r("pT", 0, 128), r("I8h"), r("cmu"), True, False)
+        mm(r("pT", 0, 128), r("I8h"), r("ivS%d" % t), False, False)
+        for k in range(N - 1):
+            mm(r("pT", 0, 128), r("I8h"), r("ivR%d" % t, 128 * k, 128 * k + 128), False, k == N - 2)
+        ts(r("muU%d" % t), r("pT", 0, 128), MAGIC, ALU.add, MAGIC, ALU.subtract)
+
+    def mean_f32():
+        ts(r("c16"), r("pT", 0, 128), MAGIC, ALU.add, MAGIC, ALU.subtract)
+
+    dma("s", r("gamI"), r("gam"), "lgam")
+    dma("a", r("X0"), r("xs"), "lxs")
+    own_piece(0, "xs")
+    dma("s", r("ewI"), r("ew"), "lew")
+    op("g", lambda: g.iota(T["iP"][:, :], [[112, 2]], 0, 1), [r("iP")], [])
+    iota(r("iF"), [[1, 144]], 0, 0)
+    ms(r("cB"), 64.0)
+    for h in range(2):
+        dma("g", r("WA0", H * h, H * h + H), r("cB"), "fill0")
+        dma("s", r("WV0", H * h, H * h + H), r("cB"), "fill1")
+    dma("s", r("rhoS", 0, 5), r("rho"), "lrho")
+    act(r("iF64"), r("iF", 0, 128), AF.Silu, bias=64.0)
+    ts(col("iC", 0), col("iP", 0), 15, ALU.bitwise_and)
+    ts(r("iC", 1, 3), r("iP"), 112, ALU.bitwise_and)
+    cp(r("fC", 0, 3), r("iC", 0, 3))
+    ts(r("EQ"), r("iF", 0, 16), col("fC", 0), ALU.is_equal)
+    ts(r("GT"), r("iF", 0, 16), col("fC", 0), ALU.is_gt, 128.0, ALU.mult)
+    for a in range(16):
+        o = r("ENC", 128 * a, 128 * a + 128)
+        if a % 2:
+            act(o, r("iF", 0, 128), scale=col("EQ", a), bias=col("GT", a))
+        else:
+            ts(o, r("iF", 0, 128), col("EQ", a), ALU.mult, col("GT", a), ALU.add)
+    cp(r("gamU"), r("gamI"))
+    ms(col("TOP", 15), -0.0625)
+    ts(r("GT64"), r("EQ"), -64.0, ALU.mult, 64.0, ALU.add)
+    ts(r("Wd", 0, 143), r("iF", 0, 143), -15.0, ALU.add, col("fC", 1), ALU.is_equal)
+    tt(r("GT64"), r("GT64"), r("GT"), ALU.add)
+    ts(r("WdB", 0, 143), r("Wd", 0, 143), 4096.0, ALU.mult)
+    dummies(KV[0])
+    template(0, "X0", lambda: ([dummies(k) for k in sorted(set(KV) - {KV[0]})], iota(r("iG"), [[16, 8], [0, 16]], 0, 0)))
+
+    warp_top("G0", "ENC", "gamU")
+    for a in range(16):
+        o = r("VAL", a, W, 16)
+        if a < NVAL_V:
+            ts(o, r("iF64"), col("EQ", a), ALU.mult, col("GT64", a), ALU.add)
+        else:
+            act(o, r("iF64"), scale=col("EQ", a), bias=col("GT64", a))
+    ts(r("Wd2", 0, 143), r("iF", 0, 143), -15.0, ALU.add, col("fC", 2), ALU.is_equal)
+    offsets(0)
+    conv_list("pK", 0, "G0", "Wd2", 0, W)
+    scatter_a(0)
+    cp(r("ewU", 0, 256), r("ewI", 0, 256))
+    scatter_v(0)
+    cp(col("fC", 3), col("iP", 0))
+    cp(r("nbS0", 0, 128), r("pK", 0, 128))
+    ts(r("Ip"), r("iF", 0, 128), col("fC", 3), ALU.is_equal)
+    ts(r("In"), r("iF", 0, 128), col("fC", 3), ALU.is_equal, -1.0, ALU.mult)
+    gather_a("dA", "X0", "ewU", 0, W)
+    score_pe(0, 0, "X0", (0,))
+    fin = merge(0, "Wd2", r("nbS0", 128, 256))
+    ms(r("acc2", 2, 4), 0.0)
+    ms(r("acc3", 0, 4), 0.0)
+    ts(r("Lall", 0, 640, 5), r("iF", 0, 128), 16.0, ALU.mult, col("fC", 0), ALU.add)
+    fin()
+    mark = neighbour(0)
+    for h in range(2):
+        dma("g", r("WA1", H * h, H * h + H), r("cB"), "fill2")
+        dma("s", r("WV1", H * h, H * h + H), r("cB"), "fill3", [mark])
+    dma("s", r("payS"), r("pay"), "lpay")
+
+    def extra0():
+        ts(r("Grp8"), r("iG"), col("fC", 1), ALU.is_equal, 8.0, ALU.mult)
+        ts(r("Tc"), r("iF", 0, 8), 1.0 / 128, ALU.mult)
+        ts(r("base5"), r("Lall", 0, 40, 5), 5.0, ALU.mult)
+        cp(r("Lall", 1, 640, 5), r("ewI", 0, 128))
+        cp(r("Lall", 2, 640, 5), r("ewI", 128, 256))
+        ts(r("fC", 5, 6), col("fC", 3), -1.0, ALU.add)
+        ts(r("fC", 6, 7), col("fC", 3), 15.0, ALU.add)
+        ts(r("fC", 7, 8), col("EQ", 0), -1.0, ALU.mult, 1.0, ALU.add)
+
+    scores(0, "X0", extra0)
+    act(r("R9", 4, 9), r("rhoS", 0, 5))
+    for j in range(4):
+        act(col("R9", j), col("rhoS", 4 - j))
+    for tab, sc in ((1, 32.0), (2, 1.0 / 32), (3, 1.0 / N)):
+        act(r("R9", 16 * tab, 16 * tab + 9), r("R9", 0, 9), scale=sc)
+
+    warp_top("G1", "G0", "cU0")
+    gather_a("X1", "X0", "cU0", 0, W)
+    cp(r("I16"), r("Ip"))
+    ts(r("D15"), r("Ip"), col("EQ", 15), ALU.mult)
+    ms(r("C4", 0, 127), 4.0)
+    offsets(1)
+    scatter_a(1)
+    scatter_v(1)
+    gather_a("pc", "payS", "cU0", 0, H)
+    gather_a("pc", "payS", "cU0", H, W)
+    act(r("VAL"), r("VAL"), scale=4.0)
+    fin = merge(1, "Wd", r("ivS0"))
+    ts(r("S1"), r("iF", 0, 128), col("fC", 5), ALU.is_equal, col("fC", 7), ALU.mult)
+    ts(r("S2"), r("iF", 0, 128), col("fC", 6), ALU.is_equal, col("EQ", 0), ALU.mult)
+    ts(col("C4", 127), col("EQ", 15), 4.0, ALU.add)
+    fin()
+    mean_send(0)
+    cp(r("c16"), r("cU0"))
+    tt(r("S1"), r("S1"), r("I16"), ALU.subtract)
+    slopes_pe()
+    ts(r("I8h"), r("Ip"), 1.0 / N, ALU.mult)
+    ms(r("cmu"), -3.5)
+    cp(r("ewU", 256, 512), r("ewI", 256, 512))
+    slopes_v()
+    weigh("V1", "pc", 0, 0, H)
+    weigh("V1", "pc", 0, H, W)
+    mean_sum(0)
+
+    gather_a("X2", "X1", "muU0", 0, W)
+    own_piece(1, "X2")
+    template(1, "X2")
+    for h in range(2):
+        gather_v("G2", "G1", "muU0", H * h, H * h + H)
+        if h == 0:
+            mean_f32()
+        top_part("G2", H * h, H * h + H)
+    conv_block()
+    slopes_pe()
+    conv_list("pK", 0, "G2", "Wd2", 0, W)
+    gather_a("tmp", "V1", "muU0", 0, W)
+    offsets(2)
+    scatter_a(2)
+    scatter_v(2)
+    slopes_v()
+    cp(r("nbS1", 0, 128), r("pK", 0, 128))
+    weigh("V2", "tmp", 1, 0, W)
+    gather_a("dA", "X2", "ewU", 0, W, base=256)
+    score_pe(1, 0, "X2", (0,))
+    fin = merge(2, "Wd2", r("nbS1", 128, 256))
+    cp(r("Lall", 1, 640, 5), r("ewI", 256, 384))
+    cp(r("Lall", 2, 640, 5), r("ewI", 384, 512))
+    fin()
+    neighbour(1)
+    dma("g", r("V2", p=(16, 128)), r("M1", p=(0, 112)), "accm", accum_op=ALU.add)
+    dma("g", r("V2", p=(0, 16)), r("M1", p=(112, 128)), "accm", accum_op=ALU.add)
+    scores(1, "X2", lambda: (ts(r("I8"), r("Ip"), 1.0 / N, ALU.mult), ts(r("I32b"), r("Ip"), 1.0 / 32, ALU.mult),
+                             ts(r("I128b"), r("Ip"), 1.0 / (16 * N), ALU.mult)))
+
+    warp_top("G3", "G2", "cU1")
+    gather_a("X3", "X2", "cU1", 0, W)
+    cp(r("c16"), r("cU1"))
+    conv_list("pK", 0, "G3", "Wd", 0, W)
+    slopes_pe()
+    send([([piece("X3", q)], [(q, piece("xq", k))], two(k), "ax", 0) for k, q in enumerate(dests)])
+    arrive("ax", 2 * (N - 1), [r("xq", 0, PW * (N - 1))])
+    offsets(3)
+    scatter_a(3)
+    scatter_v(3)
+    cp(r("glU"), r("pK", 0, 128))
+    slopes_v()
+    gather_a("P3", "payS", "glU", 0, W)
+    gather_a("tmp", "V2", "cU1", 0, H)
+    gather_a("tmp", "V2", "cU1", H, W)
+    merge(3, "Wd", r("ivS1"))()
+    mean_send(1)
+    send([([piece("P3", q)], [(q, piece("pq", k))], two(k), "ap", 0) for k, q in enumerate(dests)])
+    arrive("ap", 2 * (N - 1), [r("pq", 0, PW * (N - 1))])
+    tt(r("t3"), r("xq", 0, 3 * PW), r("xq", 3 * PW, 6 * PW), ALU.max)
+    tt(r("qS"), piece("xq", 6), piece("X3", me), ALU.max)
+    tt(piece("t3", 0), piece("t3", 0), piece("t3", 1), ALU.max)
+    tt(r("qS"), r("qS"), piece("t3", 2), ALU.max)
+    tt(r("qM"), r("qS"), piece("t3", 0), ALU.max)
+    mm(r("pA", 0, PW), r("I128b"), piece("X3", me), True, False)
+    for k in range(N - 1):
+        mm(r("pA", 0, PW), r("I128b"), piece("xq", k), False, False)
+    mm(r("pA", 0, PW), r("I8"), piece("P3", me), False, False)
+    mm(r("pA", 0, PW), r("I32b"), r("qM"), False, False)
+    weigh("V3", "tmp", 2, 0, H)
+    weigh("V3", "tmp", 2, H, W)
+    mean_sum(1)
+    mean_f32()
+    slopes_pe()
+    for k in range(N - 1):
+        mm(r("pA", 0, PW), r("I8"), piece("pq", k), False, k == N - 2)
+    slopes_v()
+
+    k0 = 0
+    for c, n in enumerate(TAIL + [1]):
+        for k in range(k0, k0 + n):
+            q = dests[k] if k < N - 1 else me
+            gather_a("tmp", "V3", "muU1", PW * q, PW * q + PW, olo=PW * k)
+            tt(piece("U", k), ind(r("R9", 48, 57), r("sU", 16 * q, 16 * q + 16)), piece("tmp", k), ALU.mult)
+        if c < len(TAIL):
+            w = 4 if n > 2 else len(eng) // n
+            st = len(eng) // w
+            send([([piece("U", k)], [(dests[k], piece("uq", k))], bits(eng[k - k0::st]), "au%d" % c, 0)
+                  for k in range(k0, k0 + n)])
+            arrive("au%d" % c, w * n, [r("uq", PW * k0, PW * (k0 + n))])
+        if c == 0:
+            cp(piece("QM", me), r("pA", 0, PW))
+            send([([piece("QM", me)], [(q, piece("QM", me)) for q in dests], allm, "aqm", 0)])
+            arrive("aqm", len(eng) * (N - 1), [piece("QM", q) for q in dests])
+        k0 += n
+    for k in range(N - 1):
+        tt(r("qg") if k == N - 2 else r("pB", 0, PW), piece("U", N - 1) if k == 0 else r("pB", 0, PW), piece("uq", k), ALU.add)
+    tt(r("ysb"), ind(r("QM"), r("muU1", 16 * me, 16 * me + 16)), r("qg"), ALU.add)
+    dma("s", r("y"), r("ysb"), "sty")
+    _emit(g, T, ops)

@@ -4,10 +4,11 @@ from concourse.mybir import AluOpType as ALU, AxisListType as AX, ActivationFunc
 W = 2048
 H = W // 2
 PW = 256
-KV = [64, 64, 54, 64]
+KV = [64, 64, 72, 64]
 GV = (768, 1408)
-NVAL_V = 4
-TAIL = [2, 3, 2]
+NVAL_V = 7
+VC, VD = 1408, 1280
+TAIL = [2, 2, 2, 1]
 MAGIC = 12582912.0
 
 SCRATCH = {}
@@ -18,7 +19,7 @@ def _buf(where, dtype, cols, *names, rows=128):
         SCRATCH[n] = (where, [rows, cols], dtype)
 
 
-_buf("sbuf", "bfloat16", W, "X0", "X1", "X2", "X3", "payS", "P3", "ENC", "G0", "G1", "G2", "G3", "IR", "M0", "M1",
+_buf("sbuf", "bfloat16", W, "X0", "X1", "X2", "X3", "payS", "P3", "G0", "G1", "G2", "G3", "IR", "M0", "M1",
      "dA", "d2", "d3", "d4", "junk", "pc", "xq", "pq")
 _buf("sbuf", "bfloat16", W + 16, "TOP")
 _buf("sbuf", "float32", W, "VAL", "V1", "V2", "V3", "tmp", "U", "QM", "uq")
@@ -41,7 +42,8 @@ _buf("sbuf", "float32", 8, "fC", "base5", "Tc", "acc1", "acc2", "acc3", "km", "r
 _buf("sbuf", "float32", 144, "iF", "Ts")
 _buf("sbuf", "float32", 128, "iG", "iF64", "Grp8", "E1", "E2", "E3", *["DD%d" % _k for _k in sorted(set(KV))])
 _buf("sbuf", "float16", 128, "c16", "I16", "S1", "S2", "D15", "C4")
-_buf("sbuf", "float32", 16, "EQ", "GT", "GT64")
+_buf("sbuf", "float32", 16, "EQ", "GT", "GT64", "GTV")
+_buf("sbuf", "int32", 128, "gamH")
 _buf("sbuf", "float32", 64, "R9")
 _buf("sbuf", "float32", 640, "Lall")
 _buf("sbuf", "bfloat16", 144, "Wd", "Wd2", "WdB")
@@ -53,7 +55,7 @@ _buf("psum", "float32", 1024, "pA", "pB")
 _buf("psum", "float32", 512, "pT", "pL", "pK", "pS")
 
 SEMAPHORES = (["qv", "qa", "qt", "qg", "sent", "lgam", "lxs", "lew", "lrho", "lpay", "own0", "own1", "fill0", "fill1",
-               "fill2", "fill3", "accm", "sty", "ax", "ap", "aqm"]
+               "fill2", "fill3", "accm", "sty", "nbg", "ax", "aq", "ap", "aqm"]
               + ["%s%d" % (s, t) for s in ("rs", "ag", "ec", "nb", "mu") for t in range(2)]
               + ["au%d" % k for k in range(len(TAIL))])
 QSEM = {"v": "qv", "a": "qa", "t": "qt", "g": "qg"}
@@ -270,9 +272,9 @@ def rank_program(g, core, T, topo):
 
     def offsets(n):
         tt(r("E1"), r("pT", 0, 128), r("DD%d" % KV[n]), ALU.add)
-        ts(r("Ts", 0, 128), r("pT", 1, 129), 1.0 / 4096, ALU.mult)
-        tt(r("E2"), r("E1"), r("pT", 1, 129), ALU.subtract)
-        tt(r("E3"), r("E2"), r("Ts", 0, 128), ALU.max)
+        ts(r("Ts", 0, 128), r("pT", 1, 129), 1.0 / 4096, ALU.mult, -1024.0, ALU.add)
+        tt(r("pT", 256, 384), r("E1"), r("pT", 1, 129), ALU.subtract)
+        tt(r("E3"), r("pT", 256, 384), r("Ts", 0, 128), ALU.max)
         cp(r("offU"), r("E3"))
 
     def iota(o, pat, base, cm):
@@ -288,16 +290,20 @@ def rank_program(g, core, T, topo):
     def scatter_a(n):
         act(ind(r("WA%d" % (n % 2)), r("offU", KV[n], 128)), r("VAL", 16 * KV[n], W), AF.Silu)
 
-    def merge(n, sel, out):
+    def merge(n, sel, out, between=None):
         sc = 4.0 if n > 1 else 1.0
         for h in range(2):
             scan(r("IR", H * h, H * h + H), r("WV%d" % (n % 2), H * h, H * h + H), r("WA%d" % (n % 2), H * h, H * h + H),
                  col("IR", H - 1) if h else 64.0 * sc)
             conv_list("pL", 64 * h, "IR", sel, H * h, H * h + H)
+            if between and h == 0:
+                between()
         return lambda: ts(out, r("pL", 0, 128), 1.0 / sc, ALU.mult, -1024.0, ALU.add)
 
-    def warp_top(new, old, lst):
+    def warp_top(new, old, lst, between=None):
         gather_v(new, old, lst, 0, GV[0])
+        if between:
+            between()
         gather_a(new, old, lst, GV[0], GV[1])
         gather_a(new, old, lst, GV[1], W)
         top_part(new, 0, GV[0])
@@ -326,7 +332,7 @@ def rank_program(g, core, T, topo):
     def gather_v(out, win, lst, lo, hi):
         return cp(r(out, lo, hi), ind(r(win), r(lst, lo // 16, hi // 16)))
 
-    def template(t, x, between=None):
+    def template(t, x, between=None, later=None):
         d, m = "dM%d" % t, "M%d" % t
         send([([piece(x, q)], [(q, rows(d, 128 * (k + 1), 128 * (k + 2)))], two(k), "rs%d" % t, 0)
               for k, q in enumerate(dests)])
@@ -335,36 +341,57 @@ def rank_program(g, core, T, topo):
         arrive("rs%d" % t, 2 * (N - 1), [rows(d, 128, 128 * N)])
         send([([rows(d, 128 * k + 16, 128 * k + 144) for k in range(N)], [(q, piece(m, me)) for q in dests], allm,
                "ag%d" % t, 2)])
+        if later:
+            later()
         arrive("ag%d" % t, len(eng) * (N - 1), [piece(m, q) for q in dests])
-        send([([piece(m, prv(me))], [(prv(me), piece(m, prv(me)))], allm, "ec%d" % t, 0)])
-        arrive("ec%d" % t, len(eng), [piece(m, me)])
+        return lambda: (send([([piece(m, prv(me))], [(prv(me), piece(m, prv(me)))], allm, "ec%d" % t, 0)]),
+                        arrive("ec%d" % t, len(eng), [piece(m, me)]))
 
     def own_piece(t, x):
         d = "dM%d" % t
         dma("s", rows(d, 0, 128), piece(x, me), "own%d" % t)
         dma("s", rows(d, 128 * N, 128 * N + 16), r(x, PW * me, PW * me + PW, p=(0, 16)), "own%d" % t)
 
-    def neighbour(t):
-        send([([r("nbS%d" % t)], [((me - 1) % N, r("nbR%d" % t))], allm, "nb%d" % t, 0)])
-        return arrive("nb%d" % t, len(eng), [r("nbR%d" % t)])
+    def neighbour(t, lo=0):
+        send([([r("nbS%d" % t, lo)], [((me - 1) % N, r("nbR%d" % t, lo))], allm, "nb%d" % t, 0)])
+        return arrive("nb%d" % t, len(eng), [r("nbR%d" % t, lo)])
 
-    def score_pe(t, tr, src, us=(0, 1)):
+    def score_pe(t, tr, src, us=(0, 1), bank=None):
         m = "M%d" % t
         for u in us:
             h = 1 - u if PW * me < H else u
-            ps = "pA" if u == 0 else "pB"
+            ps = bank or ("pA" if u == 0 else "pB")
             for c in range(2):
                 lo = H * h + 512 * c
                 mm(r(ps, 512 * c, 512 * c + 512), r("Ip"), r(src, lo, lo + 512), True, False)
                 mm(r(ps, 512 * c, 512 * c + 512), r("In"), r(m, lo, lo + 512), False, True)
-            act(r("junk", H * u, H * u + H), r(ps), AF.Abs, acc=col("acc1" if u == 0 else "acc2", tr))
+            j = H if ps == "pB" else 0
+            act(r("junk", j, j + H), r(ps), AF.Abs, acc=col("acc1" if u == 0 else "acc2", tr))
+
+    others = [(lo, hi) for lo, hi in ((0, PW * me), (PW * me + PW, W)) if hi > lo]
+
+    late = 0 if PW * me < H else H
+    early = H - late
+
+    def trial2(t, x):
+        b = 256 * t + 128
+        for lo, hi in ((early, early + H), (late, late + H))[:1 + t]:
+            tt(r("d2", lo, hi), ind(r(x), r("ewU", b + lo // 16, b + hi // 16)), r("M%d" % t, lo, hi), ALU.subtract)
 
     def scores(t, x, extra):
         m, nb = "M%d" % t, "nbR%d" % t
-        score_pe(t, 0, x, (1,))
-        score_pe(t, 1, "dA")
-        tt(r("d2"), ind(r(x), r("ewU", 256 * t + 128, 256 * t + 256)), r(m), ALU.subtract)
-        act(r("d2"), r("d2"), AF.Abs, acc=col("acc1", 2))
+        if t:
+            score_pe(t, 0, x, (1,))
+            score_pe(t, 1, "dA")
+        else:
+            score_pe(t, 0, x, (1,), "pA")
+            score_pe(t, 1, "dA", (1,))
+        trial2(t, x)
+        act(r("d2", early, early + H), r("d2", early, early + H), AF.Abs, acc=col("acc1", 2))
+        if t:
+            act(r("d2", late, late + H), r("d2", late, late + H), AF.Abs, acc=col("acc2", 2))
+        else:
+            score_pe(t, 2, "d2", (1,), "pA")
         tt(r("d3"), ind(r(x), r(nb, 0, 128)), r(m), ALU.subtract)
         act(r("d3"), r("d3"), AF.Abs, acc=col("acc1", 3))
         for lo, hi, ac in ((0, 1024, "acc1"), (1024, 1664, "acc2"), (1664, W, "acc3")):
@@ -393,6 +420,8 @@ def rank_program(g, core, T, topo):
         mm(r("pT", 0, 128), r("I8h"), r("ivS%d" % t), False, False)
         for k in range(N - 1):
             mm(r("pT", 0, 128), r("I8h"), r("ivR%d" % t, 128 * k, 128 * k + 128), False, k == N - 2)
+        if t:
+            mean_f32()
         ts(r("muU%d" % t), r("pT", 0, 128), MAGIC, ALU.add, MAGIC, ALU.subtract)
 
     def mean_f32():
@@ -404,9 +433,8 @@ def rank_program(g, core, T, topo):
     dma("s", r("ewI"), r("ew"), "lew")
     op("g", lambda: g.iota(T["iP"][:, :], [[112, 2]], 0, 1), [r("iP")], [])
     iota(r("iF"), [[1, 144]], 0, 0)
-    ms(r("cB"), 64.0)
+    iota(r("cB"), [[0, H]], 64, 0)
     for h in range(2):
-        dma("g", r("WA0", H * h, H * h + H), r("cB"), "fill0")
         dma("s", r("WV0", H * h, H * h + H), r("cB"), "fill1")
     dma("s", r("rhoS", 0, 5), r("rho"), "lrho")
     act(r("iF64"), r("iF", 0, 128), AF.Silu, bias=64.0)
@@ -415,62 +443,77 @@ def rank_program(g, core, T, topo):
     cp(r("fC", 0, 3), r("iC", 0, 3))
     ts(r("EQ"), r("iF", 0, 16), col("fC", 0), ALU.is_equal)
     ts(r("GT"), r("iF", 0, 16), col("fC", 0), ALU.is_gt, 128.0, ALU.mult)
-    for a in range(16):
-        o = r("ENC", 128 * a, 128 * a + 128)
-        if a % 2:
-            act(o, r("iF", 0, 128), scale=col("EQ", a), bias=col("GT", a))
-        else:
-            ts(o, r("iF", 0, 128), col("EQ", a), ALU.mult, col("GT", a), ALU.add)
-    cp(r("gamU"), r("gamI"))
-    ms(col("TOP", 15), -0.0625)
     ts(r("GT64"), r("EQ"), -64.0, ALU.mult, 64.0, ALU.add)
-    ts(r("Wd", 0, 143), r("iF", 0, 143), -15.0, ALU.add, col("fC", 1), ALU.is_equal)
+    ts(r("GTV"), r("GT"), 64.0, ALU.add)
     tt(r("GT64"), r("GT64"), r("GT"), ALU.add)
-    ts(r("WdB", 0, 143), r("Wd", 0, 143), 4096.0, ALU.mult)
-    dummies(KV[0])
-    template(0, "X0", lambda: ([dummies(k) for k in sorted(set(KV) - {KV[0]})], iota(r("iG"), [[16, 8], [0, 16]], 0, 0)))
-
-    warp_top("G0", "ENC", "gamU")
     for a in range(16):
         o = r("VAL", a, W, 16)
         if a < NVAL_V:
-            ts(o, r("iF64"), col("EQ", a), ALU.mult, col("GT64", a), ALU.add)
+            ts(o, r("iF", 0, 128), col("EQ", a), ALU.mult, col("GTV", a), ALU.add)
         else:
             act(o, r("iF64"), scale=col("EQ", a), bias=col("GT64", a))
+    ts(r("gamH"), r("gamI"), 7, ALU.arith_shift_right)
+    ts(col("TOP", 15), col("EQ", 0), -1.0, ALU.mult, 64.0, ALU.add)
+    ts(r("pT", 256, 384), r("gamH"), -2047.0 / 16, ALU.mult)
+    ts(r("Wd", 0, 143), r("iF", 0, 143), -15.0, ALU.add, col("fC", 1), ALU.is_equal)
+    tt(r("E3"), r("pT", 256, 384), r("gamI"), ALU.add)
+    ts(r("WdB", 0, 143), r("Wd", 0, 143), 4096.0, ALU.mult)
+    ts(r("gamU"), r("E3"), 16.0, ALU.mult)
+
+    def ident(o, i):
+        op("g", lambda: g.affine_select(o[0], i[0], [[-1, 128]], ALU.is_equal, 0.0, 0, 1), [o], [i])
+
+    def after_pieces():
+        for h in range(2):
+            dma("g", r("WA0", H * h, H * h + H), r("cB"), "fill0")
+        dummies(KV[0])
+        iota(r("iG"), [[16, 8], [0, 16]], 0, 0)
+
+    def after_fold():
+        iota(r("I8"), [[0, 128]], 1, 0)
+        iota(r("I32b"), [[0, 128]], -1, 0)
+        ident(r("Ip"), r("I8"))
+        ident(r("In"), r("I32b"))
+
+    echo = template(0, "X0", after_pieces, after_fold)
+
+    def first_consts():
+        cp(r("ewU", 0, 256), r("ewI", 0, 256))
+
+    warp_top("G0", "VAL", "gamU", first_consts)
+    gather_a("dA", "X0", "ewU", 0, W)
     ts(r("Wd2", 0, 143), r("iF", 0, 143), -15.0, ALU.add, col("fC", 2), ALU.is_equal)
+    ms(r("acc2", 3, 4), 0.0)
+    ms(r("acc3", 0, 4), 0.0)
+    ts(r("Grp8"), r("iG"), col("fC", 1), ALU.is_equal, 8.0, ALU.mult)
+    act(r("Lall", 0, 640, 5), r("iF", 0, 128), scale=16.0, bias=col("fC", 0))
+    act(r("Tc"), r("iF", 0, 8), scale=1.0 / 128)
+    act(r("base5"), r("Lall", 0, 40, 5), scale=5.0)
     offsets(0)
     conv_list("pK", 0, "G0", "Wd2", 0, W)
     scatter_a(0)
-    cp(r("ewU", 0, 256), r("ewI", 0, 256))
     scatter_v(0)
-    cp(col("fC", 3), col("iP", 0))
-    cp(r("nbS0", 0, 128), r("pK", 0, 128))
-    ts(r("Ip"), r("iF", 0, 128), col("fC", 3), ALU.is_equal)
-    ts(r("In"), r("iF", 0, 128), col("fC", 3), ALU.is_equal, -1.0, ALU.mult)
-    gather_a("dA", "X0", "ewU", 0, W)
+    echo()
+    ts(r("nbS0", 0, 128), r("pK", 0, 128), -1024.0, ALU.add)
+    send([([r("nbS0", 0, 128)], [((me - 1) % N, r("nbR0", 0, 128))], allm, "nbg", 0)])
+    arrive("nbg", len(eng), [r("nbR0", 0, 128)])
+    gather_a("d2", "X0", "ewU", late, late + H, base=128)
     score_pe(0, 0, "X0", (0,))
+    score_pe(0, 1, "dA", (0,), "pB")
     fin = merge(0, "Wd2", r("nbS0", 128, 256))
-    ms(r("acc2", 2, 4), 0.0)
-    ms(r("acc3", 0, 4), 0.0)
-    ts(r("Lall", 0, 640, 5), r("iF", 0, 128), 16.0, ALU.mult, col("fC", 0), ALU.add)
+    cp(r("Lall", 1, 640, 5), r("ewI", 0, 128))
+    cp(r("Lall", 2, 640, 5), r("ewI", 128, 256))
+    cp(col("fC", 3), col("iP", 0))
     fin()
-    mark = neighbour(0)
+    mark = neighbour(0, 128)
     for h in range(2):
         dma("g", r("WA1", H * h, H * h + H), r("cB"), "fill2")
         dma("s", r("WV1", H * h, H * h + H), r("cB"), "fill3", [mark])
     dma("s", r("payS"), r("pay"), "lpay")
+    for k in sorted(set(KV) - {KV[0]}):
+        dummies(k)
 
-    def extra0():
-        ts(r("Grp8"), r("iG"), col("fC", 1), ALU.is_equal, 8.0, ALU.mult)
-        ts(r("Tc"), r("iF", 0, 8), 1.0 / 128, ALU.mult)
-        ts(r("base5"), r("Lall", 0, 40, 5), 5.0, ALU.mult)
-        cp(r("Lall", 1, 640, 5), r("ewI", 0, 128))
-        cp(r("Lall", 2, 640, 5), r("ewI", 128, 256))
-        ts(r("fC", 5, 6), col("fC", 3), -1.0, ALU.add)
-        ts(r("fC", 6, 7), col("fC", 3), 15.0, ALU.add)
-        ts(r("fC", 7, 8), col("EQ", 0), -1.0, ALU.mult, 1.0, ALU.add)
-
-    scores(0, "X0", extra0)
+    scores(0, "X0", lambda: None)
     act(r("R9", 4, 9), r("rhoS", 0, 5))
     for j in range(4):
         act(col("R9", j), col("rhoS", 4 - j))
@@ -479,8 +522,9 @@ def rank_program(g, core, T, topo):
 
     warp_top("G1", "G0", "cU0")
     gather_a("X1", "X0", "cU0", 0, W)
-    cp(r("I16"), r("Ip"))
-    ts(r("D15"), r("Ip"), col("EQ", 15), ALU.mult)
+    ts(r("fC", 5, 6), col("fC", 3), -1.0, ALU.add)
+    ts(r("fC", 6, 7), col("fC", 3), 15.0, ALU.add)
+    ts(r("fC", 7, 8), col("EQ", 0), -1.0, ALU.mult, 1.0, ALU.add)
     ms(r("C4", 0, 127), 4.0)
     offsets(1)
     scatter_a(1)
@@ -495,6 +539,8 @@ def rank_program(g, core, T, topo):
     fin()
     mean_send(0)
     cp(r("c16"), r("cU0"))
+    cp(r("I16"), r("Ip"))
+    ts(r("D15"), r("Ip"), col("EQ", 15), ALU.mult)
     tt(r("S1"), r("S1"), r("I16"), ALU.subtract)
     slopes_pe()
     ts(r("I8h"), r("Ip"), 1.0 / N, ALU.mult)
@@ -502,75 +548,75 @@ def rank_program(g, core, T, topo):
     cp(r("ewU", 256, 512), r("ewI", 256, 512))
     slopes_v()
     weigh("V1", "pc", 0, 0, H)
-    weigh("V1", "pc", 0, H, W)
+    weigh("V1", "pc", 0, H, VC)
     mean_sum(0)
 
-    gather_a("X2", "X1", "muU0", 0, W)
+    warp_top("G2", "G1", "muU0", mean_f32)
+    gather_a("X2", "X1", "muU0", PW * me, PW * me + PW)
     own_piece(1, "X2")
-    template(1, "X2")
-    for h in range(2):
-        gather_v("G2", "G1", "muU0", H * h, H * h + H)
-        if h == 0:
-            mean_f32()
-        top_part("G2", H * h, H * h + H)
-    conv_block()
+    for lo, hi in others:
+        gather_a("X2", "X1", "muU0", lo, hi)
+    template(1, "X2")()
+    weigh("V1", "pc", 0, VC, W)
     slopes_pe()
     conv_list("pK", 0, "G2", "Wd2", 0, W)
-    gather_a("tmp", "V1", "muU0", 0, W)
     offsets(2)
     scatter_a(2)
     scatter_v(2)
     slopes_v()
-    cp(r("nbS1", 0, 128), r("pK", 0, 128))
-    weigh("V2", "tmp", 1, 0, W)
-    gather_a("dA", "X2", "ewU", 0, W, base=256)
-    score_pe(1, 0, "X2", (0,))
+    ts(r("nbS1", 0, 128), r("pK", 0, 128), -1024.0, ALU.add)
+    gather_a("tmp", "V1", "muU0", 0, W)
+    gather_a("dA", "X2", "ewU", 0, W, base=16 * 16)
     fin = merge(2, "Wd2", r("nbS1", 128, 256))
+    score_pe(1, 0, "X2", (0,))
     cp(r("Lall", 1, 640, 5), r("ewI", 256, 384))
     cp(r("Lall", 2, 640, 5), r("ewI", 384, 512))
     fin()
     neighbour(1)
+    weigh("V2", "tmp", 1, 0, VD)
+    scores(1, "X2", lambda: weigh("V2", "tmp", 1, VD, W))
     dma("g", r("V2", p=(16, 128)), r("M1", p=(0, 112)), "accm", accum_op=ALU.add)
     dma("g", r("V2", p=(0, 16)), r("M1", p=(112, 128)), "accm", accum_op=ALU.add)
-    scores(1, "X2", lambda: (ts(r("I8"), r("Ip"), 1.0 / N, ALU.mult), ts(r("I32b"), r("Ip"), 1.0 / 32, ALU.mult),
-                             ts(r("I128b"), r("Ip"), 1.0 / (16 * N), ALU.mult)))
 
     warp_top("G3", "G2", "cU1")
     gather_a("X3", "X2", "cU1", 0, W)
     cp(r("c16"), r("cU1"))
     conv_list("pK", 0, "G3", "Wd", 0, W)
     slopes_pe()
-    send([([piece("X3", q)], [(q, piece("xq", k))], two(k), "ax", 0) for k, q in enumerate(dests)])
+    send([([piece("X3", prv(q))], [(q, piece("xq", k))], two(k), "ax", 0) for k, q in enumerate(dests)])
     arrive("ax", 2 * (N - 1), [r("xq", 0, PW * (N - 1))])
+    srcs = [piece("xq", k) for k in range(N - 1)] + [piece("X3", prv(me))]
+    send([(srcs, [(prv(me), r("qM"))], bits(eng[0::2]), "aq", 2), (srcs, [(prv(me), r("qS"))], bits(eng[1::2]), "aq", 1)])
+    arrive("aq", len(eng), [r("qM"), r("qS")])
+    ts(r("I8"), r("Ip"), 1.0 / N, ALU.mult)
     offsets(3)
     scatter_a(3)
     scatter_v(3)
-    cp(r("glU"), r("pK", 0, 128))
+    ts(r("glU"), r("pK", 0, 128), -1024.0, ALU.add)
     slopes_v()
     gather_a("P3", "payS", "glU", 0, W)
-    gather_a("tmp", "V2", "cU1", 0, H)
-    gather_a("tmp", "V2", "cU1", H, W)
-    merge(3, "Wd", r("ivS1"))()
-    mean_send(1)
+    cuts = (0, 384, 1024, 1664, W)
+    for c in range(4):
+        gather_a("tmp", "V2", "cU1", cuts[c], cuts[c + 1])
+    fin = merge(3, "Wd", r("ivS1"))
+    ts(r("I32b"), r("Ip"), 1.0 / 32, ALU.mult)
+    ts(r("I128b"), r("Ip"), 1.0 / (16 * N), ALU.mult)
+    fin()
     send([([piece("P3", q)], [(q, piece("pq", k))], two(k), "ap", 0) for k, q in enumerate(dests)])
     arrive("ap", 2 * (N - 1), [r("pq", 0, PW * (N - 1))])
-    tt(r("t3"), r("xq", 0, 3 * PW), r("xq", 3 * PW, 6 * PW), ALU.max)
-    tt(r("qS"), piece("xq", 6), piece("X3", me), ALU.max)
-    tt(piece("t3", 0), piece("t3", 0), piece("t3", 1), ALU.max)
-    tt(r("qS"), r("qS"), piece("t3", 2), ALU.max)
-    tt(r("qM"), r("qS"), piece("t3", 0), ALU.max)
-    mm(r("pA", 0, PW), r("I128b"), piece("X3", me), True, False)
-    for k in range(N - 1):
-        mm(r("pA", 0, PW), r("I128b"), piece("xq", k), False, False)
-    mm(r("pA", 0, PW), r("I8"), piece("P3", me), False, False)
+    mean_send(1)
+    mm(r("pA", 0, PW), r("I8"), piece("P3", me), True, False)
+    mm(r("pA", 0, PW), r("I128b"), r("qS"), False, False)
     mm(r("pA", 0, PW), r("I32b"), r("qM"), False, False)
-    weigh("V3", "tmp", 2, 0, H)
-    weigh("V3", "tmp", 2, H, W)
-    mean_sum(1)
-    mean_f32()
-    slopes_pe()
+    for c in range(4):
+        weigh("V3", "tmp", 2, cuts[c], cuts[c + 1])
     for k in range(N - 1):
         mm(r("pA", 0, PW), r("I8"), piece("pq", k), False, k == N - 2)
+    act(piece("QM", me), r("pA", 0, PW))
+    send([([piece("QM", me)], [(q, piece("QM", me)) for q in dests], allm, "aqm", 0)])
+    arrive("aqm", len(eng) * (N - 1), [piece("QM", q) for q in dests])
+    mean_sum(1)
+    slopes_pe()
     slopes_v()
 
     k0 = 0
@@ -585,13 +631,15 @@ def rank_program(g, core, T, topo):
             send([([piece("U", k)], [(dests[k], piece("uq", k))], bits(eng[k - k0::st]), "au%d" % c, 0)
                   for k in range(k0, k0 + n)])
             arrive("au%d" % c, w * n, [r("uq", PW * k0, PW * (k0 + n))])
-        if c == 0:
-            cp(piece("QM", me), r("pA", 0, PW))
-            send([([piece("QM", me)], [(q, piece("QM", me)) for q in dests], allm, "aqm", 0)])
-            arrive("aqm", len(eng) * (N - 1), [piece("QM", q) for q in dests])
         k0 += n
-    for k in range(N - 1):
-        tt(r("qg") if k == N - 2 else r("pB", 0, PW), piece("U", N - 1) if k == 0 else r("pB", 0, PW), piece("uq", k), ALU.add)
-    tt(r("ysb"), ind(r("QM"), r("muU1", 16 * me, 16 * me + 16)), r("qg"), ALU.add)
+    tt(r("qg"), ind(r("QM"), r("muU1", 16 * me, 16 * me + 16)), piece("U", N - 1), ALU.add)
+    p1, p2 = r("pB", 0, PW), r("pB", 512, 512 + PW)
+    tt(p1, r("qg"), piece("uq", 0), ALU.add)
+    tt(p2, piece("uq", 1), piece("uq", 2), ALU.add)
+    tt(p1, p1, piece("uq", 3), ALU.add)
+    tt(p2, p2, piece("uq", 4), ALU.add)
+    tt(r("qg"), p1, piece("uq", 5), ALU.add)
+    tt(p2, p2, r("qg"), ALU.add)
+    tt(r("ysb"), p2, piece("uq", 6), ALU.add)
     dma("s", r("y"), r("ysb"), "sty")
     _emit(g, T, ops)

@@ -4,12 +4,17 @@ from concourse.mybir import AluOpType as ALU, AxisListType as AX, ActivationFunc
 W = 2048
 H = W // 2
 PW = 256
-KV = [64, 64, 72, 64]
 GV = (768, 1408)
-NVAL_V = 7
-VC, VD = 1408, 1280
-TAIL = [2, 2, 2, 1]
+NVAL_V = 10
+TAIL = [(0, 1), (2,), (4, 5), (6,)]
+QC = 2
 MAGIC = 12582912.0
+UNIT = 8192.0
+USES = [(2.0, -256.0), (1.0, -256.0), (1.0, 128.0), (2.0, 128.0)]
+LOW = -5.0e6
+WAITS = (0, 320, 416, 480, 576, 736, 800, 896)
+UC = (896, 1376, 1792, W)
+LAST = ((128, 256), (832, 1536))
 
 SCRATCH = {}
 
@@ -19,43 +24,43 @@ def _buf(where, dtype, cols, *names, rows=128):
         SCRATCH[n] = (where, [rows, cols], dtype)
 
 
-_buf("sbuf", "bfloat16", W, "X0", "X1", "X2", "X3", "payS", "P3", "G0", "G1", "G2", "G3", "IR", "M0", "M1",
-     "dA", "d2", "d3", "d4", "junk", "pc", "xq", "pq")
+_buf("sbuf", "bfloat16", W, "X0", "X1", "X2", "X3", "payS", "P3", "G0", "G1", "G2", "G3", "IR", "M0", "M1", "MP",
+     "dA", "d2", "d3", "d4", "junk", "pc", "xq", "pq", "VAL", "st1", "st2")
 _buf("sbuf", "bfloat16", W + 16, "TOP")
-_buf("sbuf", "float32", W, "VAL", "V1", "V2", "V3", "tmp", "U", "QM", "uq")
-for _n in range(2):
-    _buf("sbuf", "bfloat16", W + 112 + 16 * max(KV[_n::2]), "WV%d" % _n)
-    _buf("sbuf", "float32", W + 112 + 16 * (128 - min(KV[_n::2])), "WA%d" % _n)
-_buf("sbuf", "bfloat16", 3 * PW, "t3")
-_buf("sbuf", "bfloat16", H, "cB")
-_buf("sbuf", "int32", 128, "gamI")
+_buf("sbuf", "float32", W, "V1", "V2", "V3", "tmp", "U", "QM", "uq")
+_buf("sbuf", "float32", W + 264, "WIN")
+_buf("sbuf", "int32", 128, "gamI", "nbI")
 _buf("sbuf", "int32", 512, "ewI")
 _buf("sbuf", "uint16", 512, "ewU")
-_buf("sbuf", "uint16", 128, "gamU", "offU", "cU0", "cU1", "muU0", "muU1", "sU", "glU")
+_buf("sbuf", "uint16", 128, "gamU", "cU0", "cU1", "muU0", "muU1", "muS", "sU0", "sU1", "sU2", "sU3", "glU")
 _buf("sbuf", "uint16", 256, "nbS0", "nbS1", "nbR0", "nbR1")
-_buf("sbuf", "uint16", 8, "eo")
-_buf("sbuf", "float16", 128, "ivS0", "ivS1", "I8h", "cmu")
+_buf("sbuf", "uint16", 8, "eo", "offU")
+_buf("sbuf", "float16", 128, "ivS0", "ivS1", "cmu", "FM", "DN", "c16", "C4", "gl16", "iv16")
 _buf("sbuf", "float16", 7 * 128, "ivR0", "ivR1")
+_buf("sbuf", "float16", 256, "A2", "B2", "N2")
+SCRATCH["N3"] = ("sbuf", [128, 8, 32], "float16")
+SCRATCH["C3"] = ("sbuf", [128, 8, 32], "bfloat16")
 _buf("sbuf", "int32", 2, "iP")
 _buf("sbuf", "int32", 4, "iC")
-_buf("sbuf", "float32", 8, "fC", "base5", "Tc", "acc1", "acc2", "acc3", "km", "rhoS")
-_buf("sbuf", "float32", 144, "iF", "Ts")
-_buf("sbuf", "float32", 128, "iG", "iF64", "Grp8", "E1", "E2", "E3", *["DD%d" % _k for _k in sorted(set(KV))])
-_buf("sbuf", "float16", 128, "c16", "I16", "S1", "S2", "D15", "C4")
-_buf("sbuf", "float32", 16, "EQ", "GT", "GT64", "GTV")
-_buf("sbuf", "int32", 128, "gamH")
+_buf("sbuf", "float32", 8, "fC", "fD", "base5", "Tc", "km", "rhoS")
+_buf("sbuf", "float32", 40, "acc")
+_buf("sbuf", "float32", 144, "iF")
+_buf("sbuf", "float32", 128, "iG", "iA", "Grp8", "SRC")
+_buf("sbuf", "float32", 16, "EQ", "GT")
 _buf("sbuf", "float32", 64, "R9")
 _buf("sbuf", "float32", 640, "Lall")
-_buf("sbuf", "bfloat16", 144, "Wd", "Wd2", "WdB")
-_buf("sbuf", "bfloat16", 128, "Ip", "In", "I8", "I32b", "I128b")
+_buf("sbuf", "bfloat16", 8, "sel", "sel2")
+_buf("sbuf", "bfloat16", 128, "iB", "one", "neg", "Kd", "lane", "Ip", "In", "I8", "I32b", "I128b", "Sh", "S1",
+     "S2", "D15")
 _buf("sbuf", "bfloat16", PW, "qM", "qS")
-_buf("sbuf", "float32", PW, "qg", "ysb")
+_buf("sbuf", "float32", PW, "qg", "qg2", "ysb")
 _buf("dram", "bfloat16", PW, "dM0", "dM1", rows=8 * 128 + 16)
-_buf("psum", "float32", 1024, "pA", "pB")
-_buf("psum", "float32", 512, "pT", "pL", "pK", "pS")
+_buf("dram", "int32", 128, "dG", rows=128 + 16)
+_buf("psum", "float32", 1024, "pA", "pB", "pC")
+_buf("psum", "float32", 512, "pT", "pL")
 
-SEMAPHORES = (["qv", "qa", "qt", "qg", "sent", "lgam", "lxs", "lew", "lrho", "lpay", "own0", "own1", "fill0", "fill1",
-               "fill2", "fill3", "accm", "sty", "nbg", "ax", "aq", "ap", "aqm"]
+SEMAPHORES = (["qv", "qa", "qt", "qg", "sent", "lgam", "lxs", "lew", "lrho", "lpay", "own0", "own1", "fill",
+               "ldg", "accm0", "accm1", "sty", "nbg0", "nbg1", "ax0", "ax1", "aq", "ap0", "ap1", "aqm", "aqf", "auf"]
               + ["%s%d" % (s, t) for s in ("rs", "ag", "ec", "nb", "mu") for t in range(2)]
               + ["au%d" % k for k in range(len(TAIL))])
 QSEM = {"v": "qv", "a": "qa", "t": "qt", "g": "qg"}
@@ -171,8 +176,22 @@ def rank_program(g, core, T, topo):
     def bits(es):
         return sum(1 << e for e in es)
 
-    nfar = len(sides(me)[1])
+    def runs(ranks):
+        out = []
+        for q in sorted(ranks):
+            if out and out[-1][1] == PW * q:
+                out[-1][1] += PW
+            else:
+                out.append([PW * q, PW * q + PW])
+        return out
+
+    near, far = sides(me)
+    nfar = len(far)
+    mine = near.index(me)
+    mate = far[mine]
     dests = [dest(me, k) for k in range(N - 1)]
+    served = [mate] + dests[nfar:]
+    halves = (range(nfar), range(nfar, N - 1))
     eng = topo.engines(core, cores[dests[0]])
     allm = bits(eng)
 
@@ -186,6 +205,9 @@ def rank_program(g, core, T, topo):
         ps = slice(None) if p is None else slice(p[0], p[1])
         ap = T[name][ps, lo:hi:step] if step > 1 else T[name][ps, lo:hi]
         return (ap, [(name, lo, hi, step)], [])
+
+    def r3(name, lo=0, hi=32):
+        return (T[name][:, :, lo:hi], [(name, lo, hi, 1)], [])
 
     def rows(name, a, b):
         return (T[name][a:b, :], [(name, a, b, 1)], [])
@@ -221,8 +243,8 @@ def rank_program(g, core, T, topo):
     def ms(o, c):
         return op("v", lambda: V.memset(o[0], c), [o], [])
 
-    def scan(o, a, b, init):
-        return op("v", lambda: V.tensor_tensor_scan(o[0], a[0], b[0], a_(init), ALU.max, ALU.max), [o], [a, b, init])
+    def scan(o, a, b, init, o0=ALU.max, o1=ALU.max):
+        return op("v", lambda: V.tensor_tensor_scan(o[0], a[0], b[0], a_(init), o0, o1), [o], [a, b, init])
 
     def act(o, i, f=AF.Identity, scale=None, bias=None, acc=None):
         kw = {}
@@ -251,79 +273,28 @@ def rank_program(g, core, T, topo):
     def arrive(sem, n, places):
         return op(None, None, places, [], sem=sem, inc=n)
 
-    def piece(name, o):
-        return r(name, PW * o, PW * o + PW)
+    def piece(name, o, w=PW):
+        return r(name, w * o, w * o + w)
 
     def col(name, j):
         return r(name, j, j + 1)
 
-    def conv_list(ps, lo, row, sel, c0, c1):
-        n = (c1 - c0) // 16
-        for i in range(16):
-            mm(r(ps, lo, lo + n), r(sel, 15 - i, 143 - i), r(row, c0 + i, c1, 16), i == 0, i == 15)
+    def iota(o, pat, base, cm):
+        op("g", lambda: g.iota(o[0], pat, base, cm, allow_small_or_imprecise_dtypes=True), [o], [])
 
-    def conv_block():
+    def ident(o, i):
+        op("g", lambda: g.affine_select(o[0], i[0], [[-1, 128]], ALU.is_equal, 0.0, 0, 1), [o], [i])
+
+    def conv_turned(ps, lo, row, sel):
         for i in range(16):
-            mm(r("pT", 0, 129), r("WdB", 15 - i, 143 - i), r("TOP", 15 + 128 * i, 144 + 128 * i), i == 0, i == 15)
+            mm(r(ps, lo + i, lo + 128, 16), r(row, i, W, 16), r(sel), True, True)
+
+    def turn_back(src, ps, at):
+        mm(r(ps, at, at + 128), r(src), r("Ip"), True, True)
 
     def top_part(row, lo, hi):
         x = r(row, lo, hi)
         scan(r("TOP", 16 + lo, 16 + hi), x, x, col("TOP", 15 + lo) if lo else 0.0)
-
-    def offsets(n):
-        tt(r("E1"), r("pT", 0, 128), r("DD%d" % KV[n]), ALU.add)
-        ts(r("Ts", 0, 128), r("pT", 1, 129), 1.0 / 4096, ALU.mult, -1024.0, ALU.add)
-        tt(r("pT", 256, 384), r("E1"), r("pT", 1, 129), ALU.subtract)
-        tt(r("E3"), r("pT", 256, 384), r("Ts", 0, 128), ALU.max)
-        cp(r("offU"), r("E3"))
-
-    def iota(o, pat, base, cm):
-        op("g", lambda: g.iota(o[0], pat, base, cm, allow_small_or_imprecise_dtypes=True), [o], [])
-
-    def dummies(k):
-        iota(r("DD%d" % k, 0, k), [[16, k]], W, 1)
-        iota(r("DD%d" % k, k, 128), [[16, 128 - k]], W, 1)
-
-    def scatter_v(n):
-        cp(ind(r("WV%d" % (n % 2)), r("offU", 0, KV[n])), r("VAL", 0, 16 * KV[n]))
-
-    def scatter_a(n):
-        act(ind(r("WA%d" % (n % 2)), r("offU", KV[n], 128)), r("VAL", 16 * KV[n], W), AF.Silu)
-
-    def merge(n, sel, out, between=None):
-        sc = 4.0 if n > 1 else 1.0
-        for h in range(2):
-            scan(r("IR", H * h, H * h + H), r("WV%d" % (n % 2), H * h, H * h + H), r("WA%d" % (n % 2), H * h, H * h + H),
-                 col("IR", H - 1) if h else 64.0 * sc)
-            conv_list("pL", 64 * h, "IR", sel, H * h, H * h + H)
-            if between and h == 0:
-                between()
-        return lambda: ts(out, r("pL", 0, 128), 1.0 / sc, ALU.mult, -1024.0, ALU.add)
-
-    def warp_top(new, old, lst, between=None):
-        gather_v(new, old, lst, 0, GV[0])
-        if between:
-            between()
-        gather_a(new, old, lst, GV[0], GV[1])
-        gather_a(new, old, lst, GV[1], W)
-        top_part(new, 0, GV[0])
-        top_part(new, GV[0], GV[1])
-        top_part(new, GV[1], W)
-        conv_block()
-
-    def slopes_pe():
-        mm(r("pS", 0, 128), r("I16"), r("C4"), True, False)
-        mm(r("pS", 0, 127), r("S2"), r("c16", 1, 128), False, False)
-        mm(r("pS", 127, 128), r("D15"), r("c16", 127, 128), False, False)
-        mm(r("pS", 0, 128), r("S1"), r("c16"), False, True)
-
-    def slopes_v():
-        ts(r("sU"), r("pS", 0, 128), 0.0, ALU.max, 8.0, ALU.min)
-
-    def weigh(out, src, tab, lo, hi, olo=None):
-        olo = lo if olo is None else olo
-        return tt(r(out, olo, olo + hi - lo), ind(r("R9", 16 * tab, 16 * tab + 9), r("sU", lo // 16, hi // 16)),
-                  r(src, olo, olo + hi - lo), ALU.mult)
 
     def gather_a(out, win, lst, lo, hi, base=0, olo=None):
         olo = lo if olo is None else olo
@@ -332,314 +303,426 @@ def rank_program(g, core, T, topo):
     def gather_v(out, win, lst, lo, hi):
         return cp(r(out, lo, hi), ind(r(win), r(lst, lo // 16, hi // 16)))
 
-    def template(t, x, between=None, later=None):
-        d, m = "dM%d" % t, "M%d" % t
+    def nothing():
+        return None
+
+    def filler(calls):
+        calls = list(calls)
+        return lambda: calls.pop(0)() if calls else None
+
+    def parts(out, win, lst):
+        return [lambda lo=lo, hi=hi: gather_v(out, win, lst, lo, hi) for lo, hi in zip(WAITS[:-1], WAITS[1:])]
+
+    def warp_top(new, old, lst, calls=(), sel=None):
+        fill = filler(calls)
+        gather_v(new, old, lst, 0, GV[0])
+        gather_a(new, old, lst, GV[0], GV[1])
+        gather_a(new, old, lst, GV[1], W)
+        for lo, hi in ((0, GV[0]), GV, (GV[1], W)):
+            fill()
+            top_part(new, lo, hi)
+        if sel:
+            conv_turned("pC", 0, new, sel)
+        for c in range(17):
+            mm(r("pT", c + 1, 256, 32), r("TOP", 31 - c, 31 - c + W - 15, 16), r("sel"), True, True)
+        if sel:
+            cp(r("gl16"), r("pC", 0, 128))
+            turn_back("gl16", "pC", 512)
+
+    def blocks(n, calls=()):
+        sc, base = USES[n]
+        fill = filler(calls)
+        tt(r("A2"), r("pT", 0, 256), r3("C3"), ALU.min)
+        fill()
+        tt(r("B2"), r("A2"), r("pT", 1, 257), ALU.is_le)
+        fill()
+        scan(r("N2"), r("B2"), r("A2"), 0.0, ALU.mult, ALU.max)
+        fill()
+        cp(r3("N3"), r("N2"))
+        fill()
+        mm(r("pL", 0, 128), r("one"), r("Kd"), True, False)
+        tt(r("FM"), r3("N3", 16, 32), r("lane"), ALU.mult)
+        mm(r("pT", 264, 272), r("FM"), r("sel"), True, True)
+        tt(r("DN"), r3("N3", 16, 32), r3("N3", 0, 16), ALU.subtract)
+        mm(r("pL", 0, 128), r("DN"), r("Ip"), False, True)
+        fill()
+        cp(r("offU"), r("pT", 264, 272))
+        ts(r("SRC"), r("pL", 0, 128), sc, ALU.mult, sc * (UNIT * (base + 0.5) - 0.5), ALU.add)
+        fill()
+        cp(ind(r("WIN"), r("offU")), r("SRC"))
+        fill()
+        scan(r("IR"), r("WIN", 0, W), r("st%d" % int(sc)), sc * UNIT * (base - (0.1875 if base > 0 else 0.375)),
+             ALU.max, ALU.add)
+
+    def counted(n, out, lo):
+        sc, base = USES[n]
+        ts(out, r("pL", lo, lo + 128), 1.0 / (sc * UNIT), ALU.mult, -16.0 * base, ALU.add)
+
+    def slopes_pe():
+        mm(r("pL", 256, 384), r("Ip"), r("C4"), True, False)
+        mm(r("pL", 256, 383), r("S2"), r("c16", 1, 128), False, False)
+        mm(r("pL", 383, 384), r("D15"), r("c16", 127, 128), False, False)
+        mm(r("pL", 256, 384), r("S1"), r("c16"), False, True)
+
+    def slopes_v(n):
+        ts(r("sU%d" % n), r("pL", 256, 384), 0.0, ALU.max, 8.0, ALU.min)
+
+    def weigh(out, src, n, lo, hi):
+        return tt(r(out, lo, hi), ind(r("R9", 16 * n, 16 * n + 9), r("sU%d" % n, lo // 16, hi // 16)), r(src, lo, hi),
+                  ALU.mult)
+
+    def template(t, x, m, between=nothing):
+        d = "dM%d" % t
         send([([piece(x, q)], [(q, rows(d, 128 * (k + 1), 128 * (k + 2)))], two(k), "rs%d" % t, 0)
               for k, q in enumerate(dests)])
-        if between:
-            between()
+        between()
         arrive("rs%d" % t, 2 * (N - 1), [rows(d, 128, 128 * N)])
-        send([([rows(d, 128 * k + 16, 128 * k + 144) for k in range(N)], [(q, piece(m, me)) for q in dests], allm,
-               "ag%d" % t, 2)])
-        if later:
-            later()
-        arrive("ag%d" % t, len(eng) * (N - 1), [piece(m, q) for q in dests])
-        return lambda: (send([([piece(m, prv(me))], [(prv(me), piece(m, prv(me)))], allm, "ec%d" % t, 0)]),
-                        arrive("ec%d" % t, len(eng), [piece(m, me)]))
+
+        def fold():
+            send([([rows(d, 128 * k + 16, 128 * k + 144) for k in range(N)], [(q, piece(m, me)) for q in dests], allm,
+                   "ag%d" % t, 2)])
+            arrive("ag%d" % t, len(eng) * (N - 1), [piece(m, q) for q in dests])
+
+        def echo():
+            send([([piece(m, prv(me))], [(prv(me), piece(m, prv(me)))], allm, "ec%d" % t, 0)])
+            arrive("ec%d" % t, len(eng), [piece(m, me)])
+        return fold, echo
 
     def own_piece(t, x):
         d = "dM%d" % t
         dma("s", rows(d, 0, 128), piece(x, me), "own%d" % t)
         dma("s", rows(d, 128 * N, 128 * N + 16), r(x, PW * me, PW * me + PW, p=(0, 16)), "own%d" % t)
 
-    def neighbour(t, lo=0):
-        send([([r("nbS%d" % t, lo)], [((me - 1) % N, r("nbR%d" % t, lo))], allm, "nb%d" % t, 0)])
-        return arrive("nb%d" % t, len(eng), [r("nbR%d" % t, lo)])
+    def neighbour(t, lo, sem):
+        send([([r("nbS%d" % t, lo, lo + 128)], [((me - 1) % N, r("nbR%d" % t, lo, lo + 128))], allm, sem, 0)])
+        return arrive(sem, len(eng), [r("nbR%d" % t, lo, lo + 128)])
 
-    def score_pe(t, tr, src, us=(0, 1), bank=None):
-        m = "M%d" % t
-        for u in us:
-            h = 1 - u if PW * me < H else u
-            ps = bank or ("pA" if u == 0 else "pB")
-            for c in range(2):
-                lo = H * h + 512 * c
-                mm(r(ps, 512 * c, 512 * c + 512), r("Ip"), r(src, lo, lo + 512), True, False)
-                mm(r(ps, 512 * c, 512 * c + 512), r("In"), r(m, lo, lo + 512), False, True)
-            j = H if ps == "pB" else 0
-            act(r("junk", j, j + H), r(ps), AF.Abs, acc=col("acc1" if u == 0 else "acc2", tr))
+    def acc(t, slot, tr):
+        return col("acc", 20 * t + 5 * slot + tr)
 
-    others = [(lo, hi) for lo, hi in ((0, PW * me), (PW * me + PW, W)) if hi > lo]
+    def diff_pe(t, src, lo, ps, first=True, second=True):
+        for c in range(2):
+            a = lo + 512 * c
+            if first:
+                mm(r(ps, 512 * c, 512 * c + 512), r("Ip"), r(src, a, a + 512), True, False)
+            if second:
+                mm(r(ps, 512 * c, 512 * c + 512), r("In"), r("M%d" % t, a, a + 512), False, True)
 
-    late = 0 if PW * me < H else H
-    early = H - late
+    turn = [0]
 
-    def trial2(t, x):
-        b = 256 * t + 128
-        for lo, hi in ((early, early + H), (late, late + H))[:1 + t]:
-            tt(r("d2", lo, hi), ind(r(x), r("ewU", b + lo // 16, b + hi // 16)), r("M%d" % t, lo, hi), ALU.subtract)
+    def size_a(t, slot, tr, ps):
+        turn[0] = H - turn[0]
+        act(r("junk", turn[0], turn[0] + H), r(ps), AF.Abs, acc=acc(t, slot, tr))
 
-    def scores(t, x, extra):
-        m, nb = "M%d" % t, "nbR%d" % t
-        if t:
-            score_pe(t, 0, x, (1,))
-            score_pe(t, 1, "dA")
-        else:
-            score_pe(t, 0, x, (1,), "pA")
-            score_pe(t, 1, "dA", (1,))
-        trial2(t, x)
-        act(r("d2", early, early + H), r("d2", early, early + H), AF.Abs, acc=col("acc1", 2))
-        if t:
-            act(r("d2", late, late + H), r("d2", late, late + H), AF.Abs, acc=col("acc2", 2))
-        else:
-            score_pe(t, 2, "d2", (1,), "pA")
-        tt(r("d3"), ind(r(x), r(nb, 0, 128)), r(m), ALU.subtract)
-        act(r("d3"), r("d3"), AF.Abs, acc=col("acc1", 3))
-        for lo, hi, ac in ((0, 1024, "acc1"), (1024, 1664, "acc2"), (1664, W, "acc3")):
-            tt(r("d4", lo, hi), ind(r(x), r(nb, 128 + lo // 16, 128 + hi // 16)), r(m, lo, hi), ALU.subtract)
-            act(r("d4", lo, hi), r("d4", lo, hi), AF.Abs, acc=col(ac, 4))
-        cp(r("Lall", 3, 640, 5), r(nb, 0, 128))
-        cp(r("Lall", 4, 640, 5), r(nb, 128, 256))
-        extra()
-        mm(r("pK", 0, 5), r("Grp8"), r("Tc", 0, 5), True, False)
-        for j, ac in enumerate(("acc1", "acc2", "acc3")):
-            mm(r("pK", 0, 5), r("Grp8"), r(ac, 0, 5), False, j == 2)
-            mm(r("pS", 0, 5), r("Grp8"), r(ac, 0, 5), j == 0, j == 2)
-        for j, ps in enumerate(("pK", "pS")):
-            o, i = col("km", 4 * j), r(ps, 0, 5)
+    def size_v(t, slot, tr, x):
+        o = acc(t, slot, tr)
+        op("v", lambda: V.tensor_reduce(o[0], x[0], AX.X, ALU.add, apply_absolute_value=True), [o], [x])
+
+    def diff_v(t, d, x, lst, base, lo, hi):
+        tt(r(d, lo, hi), ind(r(x), r(lst, base + lo // 16, base + hi // 16)), r("M%d" % t, lo, hi), ALU.subtract)
+
+    def size_s(t, slot, tr, d, lo, hi):
+        act(r(d, lo, hi), r(d, lo, hi), AF.Abs, acc=acc(t, slot, tr))
+
+    def elect(t):
+        keys, sums = r("pT", 272, 277), r("pL", 0, 5)
+        mm(keys, r("Grp8"), r("Tc", 0, 5), True, False)
+        for j in range(3):
+            x = r("acc", 20 * t + 5 * j, 20 * t + 5 * j + 5)
+            mm(keys, r("Grp8"), x, False, j == 2)
+            mm(sums, r("Grp8"), x, j == 0, j == 2)
+        for j, i in enumerate((keys, sums)):
+            o = col("km", 4 * j)
             op("v", lambda o=o, i=i: V.tensor_reduce(o[0], i[0], AX.X, ALU.min), [o], [i])
         ts(r("eo"), r("base5"), col("km", 0), ALU.add, col("km", 4), ALU.subtract)
         cp(r("cU%d" % t), ind(r("Lall"), r("eo")))
 
+    def last_trial(t, x):
+        nb = "nbR%d" % t
+        cuts = (0,) + LAST[t] + (W,)
+        for j in range(3):
+            diff_v(t, "d4", x, nb, 128, cuts[j], cuts[j + 1])
+            if j < 2:
+                size_s(t, j, 4, "d4", cuts[j], cuts[j + 1])
+        lall(4, nb, 128)()
+        size_v(t, 2, 4, r("d4", cuts[2], W))
+
+    def lall(tr, name, lo):
+        return lambda: cp(r("Lall", tr, 640, 5), r(name, lo, lo + 128))
+
     def mean_send(t):
-        send([([r("ivS%d" % t)], [(q, r("ivR%d" % t, 128 * k, 128 * k + 128)) for k, q in enumerate(dests)], allm,
-               "mu%d" % t, 0)])
-        arrive("mu%d" % t, len(eng) * (N - 1), [r("ivR%d" % t)])
+        to = [(q, r("ivR%d" % t, 128 * k, 128 * k + 128)) for k, q in enumerate(dests)]
+        send([([r("ivS%d" % t)], x, bits(eng[j::2]), "mu%d" % t, 0) for j, x in enumerate((to[:nfar], to[nfar:]))])
+        arrive("mu%d" % t, len(eng) // 2 * (N - 1), [r("ivR%d" % t)])
 
     def mean_sum(t):
-        mm(r("pT", 0, 128), r("I8h"), r("cmu"), True, False)
-        mm(r("pT", 0, 128), r("I8h"), r("ivS%d" % t), False, False)
+        o = r("pT", 384, 512)
+        mm(o, r("I8"), r("cmu"), True, False)
+        mm(o, r("ivS%d" % t), r("I8"), False, False)
         for k in range(N - 1):
-            mm(r("pT", 0, 128), r("I8h"), r("ivR%d" % t, 128 * k, 128 * k + 128), False, k == N - 2)
+            mm(o, r("ivR%d" % t, 128 * k, 128 * k + 128), r("I8"), False, k == N - 2)
         if t:
-            mean_f32()
-        ts(r("muU%d" % t), r("pT", 0, 128), MAGIC, ALU.add, MAGIC, ALU.subtract)
+            mean_f16()
+        ts(r("muU%d" % t), o, MAGIC, ALU.add, MAGIC, ALU.subtract)
 
-    def mean_f32():
-        ts(r("c16"), r("pT", 0, 128), MAGIC, ALU.add, MAGIC, ALU.subtract)
+    def mean_f16():
+        ts(r("c16"), r("pT", 384, 512), MAGIC, ALU.add, MAGIC, ALU.subtract)
 
+    def add_template(lo, hi):
+        dma("g", r("V2", lo, hi, p=(16, 128)), r("M1", lo, hi, p=(0, 112)), "accm%d" % (lo > 0), accum_op=ALU.add)
+        dma("g", r("V2", lo, hi, p=(0, 16)), r("M1", lo, hi, p=(112, 128)), "accm%d" % (lo > 0), accum_op=ALU.add)
+
+    dma("s", rows("dG", 0, 128), r("gam"), "ldg")
+    dma("a", rows("dG", 128, 144), r("gam", p=(0, 16)), "ldg")
     dma("s", r("gamI"), r("gam"), "lgam")
     dma("a", r("X0"), r("xs"), "lxs")
-    own_piece(0, "xs")
     dma("s", r("ewI"), r("ew"), "lew")
+    own_piece(0, "xs")
     op("g", lambda: g.iota(T["iP"][:, :], [[112, 2]], 0, 1), [r("iP")], [])
     iota(r("iF"), [[1, 144]], 0, 0)
-    iota(r("cB"), [[0, H]], 64, 0)
-    for h in range(2):
-        dma("s", r("WV0", H * h, H * h + H), r("cB"), "fill1")
-    dma("s", r("rhoS", 0, 5), r("rho"), "lrho")
-    act(r("iF64"), r("iF", 0, 128), AF.Silu, bias=64.0)
+    iota(r("iB"), [[1, 128]], 0, 0)
+    iota(col("fD", 1), [[0, 1]], 2050, 2)
+    iota(r3("C3", 0, 18), [[0, 144]], 4096, 0)
+    act(r("pT", 0, 128), r("iF", 0, 128), scale=0.0, bias=4096.0)
+    act(r("pT", 128, 257), r("iF", 0, 129), scale=0.0, bias=4096.0)
+    act(r("pT", 0, 256, 32), r("iF", 0, 8), scale=0.0, bias=col("fD", 1))
+    send([([rows("dG", 16, 144)], [((me - 1) % N, r("nbI"))], allm, "nbg0", 0)])
+    arrive("nbg0", len(eng), [r("nbI")])
+    ms(r("WIN", 0, 256), LOW)
     ts(col("iC", 0), col("iP", 0), 15, ALU.bitwise_and)
     ts(r("iC", 1, 3), r("iP"), 112, ALU.bitwise_and)
+    ms(r("WIN", 256, 512), LOW)
     cp(r("fC", 0, 3), r("iC", 0, 3))
+    ms(r("st2", 0, 512), 2.0)
     ts(r("EQ"), r("iF", 0, 16), col("fC", 0), ALU.is_equal)
     ts(r("GT"), r("iF", 0, 16), col("fC", 0), ALU.is_gt, 128.0, ALU.mult)
-    ts(r("GT64"), r("EQ"), -64.0, ALU.mult, 64.0, ALU.add)
-    ts(r("GTV"), r("GT"), 64.0, ALU.add)
-    tt(r("GT64"), r("GT64"), r("GT"), ALU.add)
+    ms(r("st2", 512, H), 2.0)
+    for h in range(1, 4):
+        dma("s", piece("WIN", h, 512), r("WIN", 0, 512), "fill")
+    dma("s", r("rhoS", 0, 5), r("rho"), "lrho")
     for a in range(16):
-        o = r("VAL", a, W, 16)
+        o = r("VAL", 128 * a, 128 * a + 128)
         if a < NVAL_V:
-            ts(o, r("iF", 0, 128), col("EQ", a), ALU.mult, col("GTV", a), ALU.add)
+            ts(o, r("iB"), col("EQ", a), ALU.mult, col("GT", a), ALU.add)
         else:
-            act(o, r("iF64"), scale=col("EQ", a), bias=col("GT64", a))
-    ts(r("gamH"), r("gamI"), 7, ALU.arith_shift_right)
-    ts(col("TOP", 15), col("EQ", 0), -1.0, ALU.mult, 64.0, ALU.add)
-    ts(r("pT", 256, 384), r("gamH"), -2047.0 / 16, ALU.mult)
-    ts(r("Wd", 0, 143), r("iF", 0, 143), -15.0, ALU.add, col("fC", 1), ALU.is_equal)
-    tt(r("E3"), r("pT", 256, 384), r("gamI"), ALU.add)
-    ts(r("WdB", 0, 143), r("Wd", 0, 143), 4096.0, ALU.mult)
-    ts(r("gamU"), r("E3"), 16.0, ALU.mult)
-
-    def ident(o, i):
-        op("g", lambda: g.affine_select(o[0], i[0], [[-1, 128]], ALU.is_equal, 0.0, 0, 1), [o], [i])
+            act(o, r("iF", 0, 128), scale=col("EQ", a), bias=col("GT", a))
+    cp(r("gamU"), r("gamI"))
+    ts(col("TOP", 15), col("EQ", 0), -1.0, ALU.mult)
+    ts(r("sel"), r("iF", 0, 128, 16), col("fC", 1), ALU.is_equal)
 
     def after_pieces():
-        for h in range(2):
-            dma("g", r("WA0", H * h, H * h + H), r("cB"), "fill0")
-        dummies(KV[0])
-        iota(r("iG"), [[16, 8], [0, 16]], 0, 0)
+        iota(r3("C3", 18, 32), [[0, 112]], 0, 0)
+        iota(r("fD", 5, 6), [[0, 1]], 0, 1)
+        iota(r("fD", 6, 7), [[0, 1]], 0, int(UNIT))
+        iota(r("iA"), [[0, 8], [1, 16]], 0, 0)
+        iota(r("one"), [[0, 128]], 1, 0)
+        iota(r("st2", H, 1664), [[0, 1664 - H]], 2, 0)
 
-    def after_fold():
-        iota(r("I8"), [[0, 128]], 1, 0)
-        iota(r("I32b"), [[0, 128]], -1, 0)
-        ident(r("Ip"), r("I8"))
-        ident(r("In"), r("I32b"))
+    fold, echo = template(0, "X0", "M0", after_pieces)
+    fold()
+    iota(r("st2", 1664, W), [[0, W - 1664]], 2, 0)
+    iota(r("neg"), [[0, 128]], -1, 0)
+    ident(r("In"), r("neg"))
+    iota(r("acc"), [[0, 40]], 0, 0)
+    iota(r("iG"), [[16, 8], [0, 16]], 0, 0)
+    iota(r("fD", 2, 4), [[16, 2]], -1, 1)
+    echo()
+    late = 0 if PW * me < H else H
+    early = H - late
 
-    echo = template(0, "X0", after_pieces, after_fold)
-
-    def first_consts():
-        cp(r("ewU", 0, 256), r("ewI", 0, 256))
-
-    warp_top("G0", "VAL", "gamU", first_consts)
+    warp_top("G0", "VAL", "gamU", [lambda: cp(r("ewU", 0, 256), r("ewI", 0, 256)),
+                                   lambda: ts(r("sel2"), r("iF", 0, 128, 16), col("fC", 2), ALU.is_equal),
+                                   lall(1, "ewI", 0)])
     gather_a("dA", "X0", "ewU", 0, W)
-    ts(r("Wd2", 0, 143), r("iF", 0, 143), -15.0, ALU.add, col("fC", 2), ALU.is_equal)
-    ms(r("acc2", 3, 4), 0.0)
-    ms(r("acc3", 0, 4), 0.0)
-    ts(r("Grp8"), r("iG"), col("fC", 1), ALU.is_equal, 8.0, ALU.mult)
+    ts(r("Kd"), r("iB"), col("fD", 5), ALU.is_equal, col("fD", 6), ALU.mult)
+    ts(r("Ip"), r("iB"), col("fD", 5), ALU.is_equal)
+    ts(r("lane"), r("iA"), col("fC", 0), ALU.is_equal)
+    lall(2, "ewI", 128)()
+    blocks(0, [lambda: cp(r("nbR0", 0, 128), r("nbI")), lall(3, "nbI", 0),
+               lambda: ts(col("iC", 3), col("iP", 1), 127, ALU.bitwise_and),
+               lambda: ts(r("fD", 4, 5), col("EQ", 0), -1.0, ALU.mult, 1.0, ALU.add),
+               lambda: (cp(col("fC", 3), col("iC", 3)), ms(r("C4", 0, 127), 4.0)),
+               lambda: ms(r("cmu"), -3.5),
+               lambda: ts(col("C4", 127), col("EQ", 15), 4.0, ALU.add)])
+    diff_pe(0, "X0", early, "pA", second=False)
+    diff_pe(0, "dA", early, "pC", second=False)
+    diff_pe(0, "X0", late, "pB", second=False)
+    gather_a("d2", "X0", "ewU", 0, W, base=128)
     act(r("Lall", 0, 640, 5), r("iF", 0, 128), scale=16.0, bias=col("fC", 0))
     act(r("Tc"), r("iF", 0, 8), scale=1.0 / 128)
     act(r("base5"), r("Lall", 0, 40, 5), scale=5.0)
-    offsets(0)
-    conv_list("pK", 0, "G0", "Wd2", 0, W)
-    scatter_a(0)
-    scatter_v(0)
-    echo()
-    ts(r("nbS0", 0, 128), r("pK", 0, 128), -1024.0, ALU.add)
-    send([([r("nbS0", 0, 128)], [((me - 1) % N, r("nbR0", 0, 128))], allm, "nbg", 0)])
-    arrive("nbg", len(eng), [r("nbR0", 0, 128)])
-    gather_a("d2", "X0", "ewU", late, late + H, base=128)
-    score_pe(0, 0, "X0", (0,))
-    score_pe(0, 1, "dA", (0,), "pB")
-    fin = merge(0, "Wd2", r("nbS0", 128, 256))
-    cp(r("Lall", 1, 640, 5), r("ewI", 0, 128))
-    cp(r("Lall", 2, 640, 5), r("ewI", 128, 256))
-    cp(col("fC", 3), col("iP", 0))
-    fin()
-    mark = neighbour(0, 128)
-    for h in range(2):
-        dma("g", r("WA1", H * h, H * h + H), r("cB"), "fill2")
-        dma("s", r("WV1", H * h, H * h + H), r("cB"), "fill3", [mark])
-    dma("s", r("payS"), r("pay"), "lpay")
-    for k in sorted(set(KV) - {KV[0]}):
-        dummies(k)
+    diff_pe(0, "dA", early, "pC", first=False)
+    size_a(0, 0, 1, "pC")
+    diff_pe(0, "X0", early, "pA", first=False)
+    size_a(0, 0, 0, "pA")
+    conv_turned("pL", 128, "IR", "sel2")
+    diff_v(0, "d3", "X0", "nbR0", 0, early, early + 512)
+    counted(0, r("iv16"), 128)
+    turn_back("iv16", "pL", 384)
+    ts(r("Grp8"), r("iG"), col("fC", 1), ALU.is_equal, 8.0, ALU.mult)
+    ts(r("Sh"), r("iB"), col("fC", 3), ALU.is_equal)
+    cp(r("nbS0", 128, 256), r("pL", 384, 512))
+    dma("s", r("payS"), r("pay"), "lpay", [neighbour(0, 128, "nb0")])
+    iota(r("st1"), [[0, W]], 1, 0)
+    diff_pe(0, "X0", late, "pB", first=False)
+    diff_pe(0, "d2", early, "pC")
+    diff_v(0, "d3", "X0", "nbR0", 0, early + 512, early + H)
+    size_a(0, 1, 0, "pB")
+    diff_pe(0, "dA", late, "pA")
+    size_a(0, 0, 2, "pC")
+    diff_v(0, "d3", "X0", "nbR0", 0, late, late + H)
+    diff_pe(0, "d2", late, "pB")
+    size_a(0, 1, 1, "pA")
+    size_a(0, 1, 2, "pB")
+    size_s(0, 0, 3, "d3", 0, W)
+    last_trial(0, "X0")
+    elect(0)
 
-    scores(0, "X0", lambda: None)
+    warp_top("G1", "G0", "cU0", [lambda: cp(r("c16"), r("cU0")),
+                                 lambda: ts(r("S1"), r("iB"), col("fD", 2), ALU.is_equal, col("fD", 4), ALU.mult),
+                                 lambda: ts(r("S2"), r("iB"), col("fD", 3), ALU.is_equal, col("EQ", 0), ALU.mult)])
+    gather_a("X1", "X0", "cU0", 0, W)
+    own_piece(1, "X1")
+    fold, echo = template(1, "X1", "MP")
+    ts(r("D15"), r("Ip"), col("EQ", 15), ALU.mult)
+    tt(r("S1"), r("S1"), r("Ip"), ALU.subtract)
+    cp(r("ewU", 256, 512), r("ewI", 256, 512))
+    slopes_pe()
+    blocks(1, [lambda: slopes_v(0), lall(1, "ewI", 256), lall(2, "ewI", 384)])
+    conv_turned("pL", 128, "IR", "sel")
     act(r("R9", 4, 9), r("rhoS", 0, 5))
     for j in range(4):
         act(col("R9", j), col("rhoS", 4 - j))
-    for tab, sc in ((1, 32.0), (2, 1.0 / 32), (3, 1.0 / N)):
-        act(r("R9", 16 * tab, 16 * tab + 9), r("R9", 0, 9), scale=sc)
-
-    warp_top("G1", "G0", "cU0")
-    gather_a("X1", "X0", "cU0", 0, W)
-    ts(r("fC", 5, 6), col("fC", 3), -1.0, ALU.add)
-    ts(r("fC", 6, 7), col("fC", 3), 15.0, ALU.add)
-    ts(r("fC", 7, 8), col("EQ", 0), -1.0, ALU.mult, 1.0, ALU.add)
-    ms(r("C4", 0, 127), 4.0)
-    offsets(1)
-    scatter_a(1)
-    scatter_v(1)
     gather_a("pc", "payS", "cU0", 0, H)
     gather_a("pc", "payS", "cU0", H, W)
-    act(r("VAL"), r("VAL"), scale=4.0)
-    fin = merge(1, "Wd", r("ivS0"))
-    ts(r("S1"), r("iF", 0, 128), col("fC", 5), ALU.is_equal, col("fC", 7), ALU.mult)
-    ts(r("S2"), r("iF", 0, 128), col("fC", 6), ALU.is_equal, col("EQ", 0), ALU.mult)
-    ts(col("C4", 127), col("EQ", 15), 4.0, ALU.add)
-    fin()
+    act(r("I8"), r("Ip"), scale=1.0 / N)
+    for tab, sc in ((1, 32.0), (2, 1.0 / 32), (3, 1.0 / N)):
+        act(r("R9", 16 * tab, 16 * tab + 9), r("R9", 0, 9), scale=sc)
+    act(r("I32b"), r("Ip"), scale=1.0 / 32)
+    act(r("I128b"), r("Ip"), scale=1.0 / (16 * N))
+    weigh("V1", "pc", 0, 0, 512)
+    counted(1, r("ivS0"), 128)
     mean_send(0)
-    cp(r("c16"), r("cU0"))
-    cp(r("I16"), r("Ip"))
-    ts(r("D15"), r("Ip"), col("EQ", 15), ALU.mult)
-    tt(r("S1"), r("S1"), r("I16"), ALU.subtract)
-    slopes_pe()
-    ts(r("I8h"), r("Ip"), 1.0 / N, ALU.mult)
-    ms(r("cmu"), -3.5)
-    cp(r("ewU", 256, 512), r("ewI", 256, 512))
-    slopes_v()
-    weigh("V1", "pc", 0, 0, H)
-    weigh("V1", "pc", 0, H, VC)
+    fold()
+    echo()
+    weigh("V1", "pc", 0, 512, W)
     mean_sum(0)
 
-    warp_top("G2", "G1", "muU0", mean_f32)
-    gather_a("X2", "X1", "muU0", PW * me, PW * me + PW)
-    own_piece(1, "X2")
-    for lo, hi in others:
-        gather_a("X2", "X1", "muU0", lo, hi)
-    template(1, "X2")()
-    weigh("V1", "pc", 0, VC, W)
-    slopes_pe()
-    conv_list("pK", 0, "G2", "Wd2", 0, W)
-    offsets(2)
-    scatter_a(2)
-    scatter_v(2)
-    slopes_v()
-    ts(r("nbS1", 0, 128), r("pK", 0, 128), -1024.0, ALU.add)
-    gather_a("tmp", "V1", "muU0", 0, W)
-    gather_a("dA", "X2", "ewU", 0, W, base=16 * 16)
-    fin = merge(2, "Wd2", r("nbS1", 128, 256))
-    score_pe(1, 0, "X2", (0,))
-    cp(r("Lall", 1, 640, 5), r("ewI", 256, 384))
-    cp(r("Lall", 2, 640, 5), r("ewI", 384, 512))
-    fin()
-    neighbour(1)
-    weigh("V2", "tmp", 1, 0, VD)
-    scores(1, "X2", lambda: weigh("V2", "tmp", 1, VD, W))
-    dma("g", r("V2", p=(16, 128)), r("M1", p=(0, 112)), "accm", accum_op=ALU.add)
-    dma("g", r("V2", p=(0, 16)), r("M1", p=(112, 128)), "accm", accum_op=ALU.add)
+    def shifted():
+        mean_f16()
+        mm(r("pL", 384, 512), r("Sh"), r("c16"), True, True)
+        slopes_pe()
 
-    warp_top("G3", "G2", "cU1")
-    gather_a("X3", "X2", "cU1", 0, W)
-    cp(r("c16"), r("cU1"))
-    conv_list("pK", 0, "G3", "Wd", 0, W)
-    slopes_pe()
-    send([([piece("X3", prv(q))], [(q, piece("xq", k))], two(k), "ax", 0) for k, q in enumerate(dests)])
-    arrive("ax", 2 * (N - 1), [r("xq", 0, PW * (N - 1))])
-    srcs = [piece("xq", k) for k in range(N - 1)] + [piece("X3", prv(me))]
-    send([(srcs, [(prv(me), r("qM"))], bits(eng[0::2]), "aq", 2), (srcs, [(prv(me), r("qS"))], bits(eng[1::2]), "aq", 1)])
-    arrive("aq", len(eng), [r("qM"), r("qS")])
-    ts(r("I8"), r("Ip"), 1.0 / N, ALU.mult)
-    offsets(3)
-    scatter_a(3)
-    scatter_v(3)
-    ts(r("glU"), r("pK", 0, 128), -1024.0, ALU.add)
-    slopes_v()
-    gather_a("P3", "payS", "glU", 0, W)
-    cuts = (0, 384, 1024, 1664, W)
-    for c in range(4):
-        gather_a("tmp", "V2", "cU1", cuts[c], cuts[c + 1])
-    fin = merge(3, "Wd", r("ivS1"))
-    ts(r("I32b"), r("Ip"), 1.0 / 32, ALU.mult)
-    ts(r("I128b"), r("Ip"), 1.0 / (16 * N), ALU.mult)
-    fin()
-    send([([piece("P3", q)], [(q, piece("pq", k))], two(k), "ap", 0) for k, q in enumerate(dests)])
-    arrive("ap", 2 * (N - 1), [r("pq", 0, PW * (N - 1))])
+    warp_top("G2", "G1", "muU0", [shifted, lambda: cp(r("muS"), r("pL", 384, 512)), lambda: slopes_v(1)], "sel2")
+    gather_a("X2", "X1", "muU0", 0, W)
+    gather_a("M1", "MP", "muS", H, W)
+    calls = parts("M1", "MP", "muS")
+    calls[0]()
+    blocks(2, [lambda: cp(r("nbS1", 0, 128), r("pC", 512, 640))] + calls[1:])
+    neighbour(1, 0, "nbg1")
+    diff_pe(1, "X2", H, "pA")
+    diff_pe(1, "X2", 0, "pB", second=False)
+    conv_turned("pL", 128, "IR", "sel2")
+    gather_v("M1", "MP", "muS", WAITS[-1], H)
+    diff_v(1, "d2", "X2", "ewU", 384, H, H + 384)
+    counted(2, r("iv16"), 128)
+    turn_back("iv16", "pL", 384)
+    diff_v(1, "d2", "X2", "ewU", 384, H + 384, H + 640)
+    cp(r("nbS1", 128, 256), r("pL", 384, 512))
+    neighbour(1, 128, "nb1")
+    gather_a("dA", "X2", "ewU", 0, W, base=256)
+    size_a(1, 1, 0, "pA")
+    diff_pe(1, "X2", 0, "pB", first=False)
+    diff_v(1, "d2", "X2", "ewU", 384, H + 640, W)
+    size_v(1, 0, 0, r("pB"))
+    gather_a("tmp", "V1", "muU0", 0, H)
+    diff_pe(1, "dA", 0, "pC")
+    diff_pe(1, "dA", H, "pA")
+    diff_v(1, "d3", "X2", "nbR1", 0, 0, H)
+    gather_a("d2", "X2", "ewU", 0, H, base=384)
+    weigh("V2", "tmp", 1, 0, H)
+    add_template(0, H)
+    size_a(1, 0, 1, "pC")
+    diff_pe(1, "d2", 0, "pB")
+    diff_v(1, "d3", "X2", "nbR1", 0, H, W)
+    size_a(1, 1, 1, "pA")
+    gather_a("tmp", "V1", "muU0", H, W)
+    size_s(1, 1, 2, "d2", H, W)
+    lall(3, "nbR1", 0)()
+    weigh("V2", "tmp", 1, H, W)
+    add_template(H, W)
+    size_a(1, 0, 2, "pB")
+    size_s(1, 0, 3, "d3", 0, W)
+    last_trial(1, "X2")
+    elect(1)
+
+    def slopes_3():
+        cp(r("c16"), r("cU1"))
+        slopes_pe()
+
+    warp_top("G3", "G2", "cU1", [slopes_3, nothing, lambda: slopes_v(2)], "sel")
+    calls = parts("U", "V2", "cU1")
+    calls[0]()
+    for c, ks in enumerate(halves):
+        for lo, hi in runs((far, near)[c]):
+            gather_a("X3", "X2", "cU1", lo, hi)
+        send([([piece("X3", prv(dests[k]))], [(dests[k], piece("xq", k))], bits(eng[k + 1 - nfar::nfar]) if c else two(k),
+               "ax%d" % c, 0) for k in ks])
+        arrive("ax%d" % c, 2 * (c + 1) * len(ks), [piece("xq", k) for k in ks])
+    blocks(3, [lambda: cp(r("glU"), r("pC", 512, 640))] + calls[1:])
+    conv_turned("pL", 128, "IR", "sel")
+    for c, ks in enumerate(halves):
+        for k in ks:
+            gather_a("P3", "payS", "glU", PW * dests[k], PW * dests[k] + PW)
+        send([([piece("P3", dests[k])], [(dests[k], piece("pq", k))], two(k), "ap%d" % c, 0) for k in ks])
+        arrive("ap%d" % c, 2 * len(ks), [piece("pq", k) for k in ks])
+        if c == 0:
+            srcs = [piece("xq", k) for k in range(N - 1)] + [piece("X3", prv(me))]
+            send([(srcs, [(prv(me), r(x))], bits(eng[j::2]), "aq", 2 - j) for j, x in enumerate(("qM", "qS"))])
+            arrive("aq", len(eng), [r("qM"), r("qS")])
+    gather_a("P3", "payS", "glU", PW * me, PW * me + PW)
+    weigh("V3", "U", 2, 0, 512)
+    counted(3, r("ivS1"), 128)
     mean_send(1)
+    weigh("V3", "U", 2, 512, UC[0])
+    for lo, hi in zip(UC[:-1], UC[1:]):
+        gather_a("U", "V2", "cU1", lo, hi)
+        weigh("V3", "U", 2, lo, hi)
     mm(r("pA", 0, PW), r("I8"), piece("P3", me), True, False)
+    for k in halves[0]:
+        mm(r("pA", 0, PW), r("I8"), piece("pq", k), False, False)
     mm(r("pA", 0, PW), r("I128b"), r("qS"), False, False)
     mm(r("pA", 0, PW), r("I32b"), r("qM"), False, False)
-    for c in range(4):
-        weigh("V3", "tmp", 2, cuts[c], cuts[c + 1])
-    for k in range(N - 1):
+    for k in halves[1]:
         mm(r("pA", 0, PW), r("I8"), piece("pq", k), False, k == N - 2)
     act(piece("QM", me), r("pA", 0, PW))
-    send([([piece("QM", me)], [(q, piece("QM", me)) for q in dests], allm, "aqm", 0)])
-    arrive("aqm", len(eng) * (N - 1), [piece("QM", q) for q in dests])
+    send([([piece("QM", me)], [(q, piece("QM", me))], bits(eng[j::nfar]), "aqm" if j else "aqf", 0)
+          for j, q in enumerate(served)])
+    arrive("aqf", len(eng) // nfar, [piece("QM", mate)])
     mean_sum(1)
     slopes_pe()
-    slopes_v()
+    slopes_v(3)
 
-    k0 = 0
-    for c, n in enumerate(TAIL + [1]):
-        for k in range(k0, k0 + n):
-            q = dests[k] if k < N - 1 else me
-            gather_a("tmp", "V3", "muU1", PW * q, PW * q + PW, olo=PW * k)
-            tt(piece("U", k), ind(r("R9", 48, 57), r("sU", 16 * q, 16 * q + 16)), piece("tmp", k), ALU.mult)
-        if c < len(TAIL):
-            w = 4 if n > 2 else len(eng) // n
-            st = len(eng) // w
-            send([([piece("U", k)], [(dests[k], piece("uq", k))], bits(eng[k - k0::st]), "au%d" % c, 0)
-                  for k in range(k0, k0 + n)])
-            arrive("au%d" % c, w * n, [r("uq", PW * k0, PW * (k0 + n))])
-        k0 += n
-    tt(r("qg"), ind(r("QM"), r("muU1", 16 * me, 16 * me + 16)), piece("U", N - 1), ALU.add)
-    p1, p2 = r("pB", 0, PW), r("pB", 512, 512 + PW)
-    tt(p1, r("qg"), piece("uq", 0), ALU.add)
-    tt(p2, piece("uq", 1), piece("uq", 2), ALU.add)
-    tt(p1, p1, piece("uq", 3), ALU.add)
-    tt(p2, p2, piece("uq", 4), ALU.add)
-    tt(r("qg"), p1, piece("uq", 5), ALU.add)
-    tt(p2, p2, r("qg"), ALU.add)
-    tt(r("ysb"), p2, piece("uq", 6), ALU.add)
+    order = [far[(mine + j) % nfar] for j in range(1, nfar)] + served + [me]
+    for k, q in enumerate(order):
+        gather_a("tmp", "V3", "muU1", PW * q, PW * q + PW, olo=PW * k)
+        tt(piece("U", k), ind(r("R9", 48, 57), r("sU3", 16 * q, 16 * q + 16)), piece("tmp", k), ALU.mult)
+        for c, ks in enumerate(TAIL):
+            if k == ks[-1]:
+                send([([piece("U", i)], [(served[1 + i % nfar], piece("uq", i))], bits(eng[j::len(ks)]), "au%d" % c, 0)
+                      for j, i in enumerate(ks)])
+                arrive("au%d" % c, len(eng), [piece("uq", i) for i in ks])
+        if k == QC:
+            send([([piece("QM", mate)], [(q2, piece("QM", mate)) for q2 in served[1:]], allm, "aqm", 0)])
+            arrive("aqm", (len(eng) // nfar + len(eng)) * (nfar - 1), [piece("QM", q2) for q2 in dests if q2 != mate])
+    send([([piece("uq", i) for i in range(nfar - 1)] + [piece("U", nfar - 1)], [(mate, piece("uq", nfar - 1))], allm,
+           "auf", 1)])
+    arrive("auf", len(eng), [piece("uq", nfar - 1)])
+    run = r("pC", 0, PW)
+    tt(r("qg2"), ind(r("QM"), r("muU1", 16 * me, 16 * me + 16)), piece("U", N - 1), ALU.add)
+    tt(run, r("qg2"), piece("uq", nfar), ALU.add)
+    tt(run, run, piece("uq", nfar + 1), ALU.add)
+    tt(run, run, piece("uq", nfar + 2), ALU.add)
+    tt(r("ysb"), run, piece("uq", nfar - 1), ALU.add)
     dma("s", r("y"), r("ysb"), "sty")
     _emit(g, T, ops)

@@ -7,14 +7,14 @@ PW = 256
 GV = (768, 1408)
 NVAL_V = 10
 TAIL = [(0, 1), (2,), (4, 5), (6,)]
-QC = 2
 MAGIC = 12582912.0
 UNIT = 8192.0
 USES = [(2.0, -256.0), (1.0, -256.0), (1.0, 128.0), (2.0, 128.0)]
 LOW = -5.0e6
-WAITS = (0, 320, 416, 480, 576, 736, 800, 896)
-UC = (896, 1376, 1792, W)
-LAST = ((128, 256), (832, 1536))
+WAITS = (0, 96, 160, 256, 416, 480, 576)
+UC = (0, 512, 1024, 1536, W)
+LAST = ((512, 896), (1024, 1536))
+LAND = ("X0", "G0")
 
 SCRATCH = {}
 
@@ -25,7 +25,7 @@ def _buf(where, dtype, cols, *names, rows=128):
 
 
 _buf("sbuf", "bfloat16", W, "X0", "X1", "X2", "X3", "payS", "P3", "G0", "G1", "G2", "G3", "IR", "M0", "M1", "MP",
-     "dA", "d2", "d3", "d4", "junk", "pc", "xq", "pq", "VAL", "st1", "st2")
+     "dA", "d2", "d3", "d4", "dP", "junk", "pc", "xq", "pq", "VAL", "st1", "st2")
 _buf("sbuf", "bfloat16", W + 16, "TOP")
 _buf("sbuf", "float32", W, "V1", "V2", "V3", "tmp", "U", "QM", "uq")
 _buf("sbuf", "float32", W + 264, "WIN")
@@ -42,26 +42,28 @@ SCRATCH["N3"] = ("sbuf", [128, 8, 32], "float16")
 SCRATCH["C3"] = ("sbuf", [128, 8, 32], "bfloat16")
 _buf("sbuf", "int32", 2, "iP")
 _buf("sbuf", "int32", 4, "iC")
-_buf("sbuf", "float32", 8, "fC", "fD", "base5", "Tc", "km", "rhoS")
+_buf("sbuf", "float32", 8, "fC", "fD", "base5", "Tc", "km", "rhoS", "accn", "eight")
 _buf("sbuf", "float32", 40, "acc")
 _buf("sbuf", "float32", 144, "iF")
-_buf("sbuf", "float32", 128, "iG", "iA", "Grp8", "SRC")
+_buf("sbuf", "float32", 128, "iG", "iA", "Grp8", "Grp8n", "SRC", "S3", "Sm")
+_buf("sbuf", "float32", 256, "So", "Si")
 _buf("sbuf", "float32", 16, "EQ", "GT")
 _buf("sbuf", "float32", 64, "R9")
 _buf("sbuf", "float32", 640, "Lall")
 _buf("sbuf", "bfloat16", 8, "sel", "sel2")
 _buf("sbuf", "bfloat16", 128, "iB", "one", "neg", "Kd", "lane", "Ip", "In", "I8", "I32b", "I128b", "Sh", "S1",
-     "S2", "D15")
-_buf("sbuf", "bfloat16", PW, "qM", "qS")
-_buf("sbuf", "float32", PW, "qg", "qg2", "ysb")
+     "S2", "D15", "Gp", "Gn")
+_buf("sbuf", "bfloat16", PW, "qM", "qS", "qSs")
+_buf("sbuf", "float32", PW, "qg", "ysb")
 _buf("dram", "bfloat16", PW, "dM0", "dM1", rows=8 * 128 + 16)
 _buf("dram", "int32", 128, "dG", rows=128 + 16)
 _buf("psum", "float32", 1024, "pA", "pB", "pC")
 _buf("psum", "float32", 512, "pT", "pL")
 
-SEMAPHORES = (["qv", "qa", "qt", "qg", "sent", "lgam", "lxs", "lew", "lrho", "lpay", "own0", "own1", "fill",
-               "ldg", "accm0", "accm1", "sty", "nbg0", "nbg1", "ax0", "ax1", "aq", "ap0", "ap1", "aqm", "aqf", "auf"]
-              + ["%s%d" % (s, t) for s in ("rs", "ag", "ec", "nb", "mu") for t in range(2)]
+SEMAPHORES = (["qv", "qa", "qt", "qg", "sent", "lgam", "lxs", "lew", "lrho", "lpay", "fill", "ldg", "sty", "aq", "am",
+               "as", "aqm", "auf"]
+              + ["%s%d" % (s, t) for s in ("own", "accm", "rs", "ag", "ec", "nbg", "nb", "mu", "ax", "ap", "fx", "fb")
+                 for t in range(2)]
               + ["au%d" % k for k in range(len(TAIL))])
 QSEM = {"v": "qv", "a": "qa", "t": "qt", "g": "qg"}
 
@@ -189,6 +191,7 @@ def rank_program(g, core, T, topo):
     nfar = len(far)
     mine = near.index(me)
     mate = far[mine]
+    nxt = near[(mine + 1) % nfar]
     dests = [dest(me, k) for k in range(N - 1)]
     served = [mate] + dests[nfar:]
     halves = (range(nfar), range(nfar, N - 1))
@@ -198,6 +201,9 @@ def rank_program(g, core, T, topo):
     def two(k):
         j, o = (k, 0) if k < nfar else (k - nfar, 1)
         return bits([eng[4 * j + o], eng[4 * j + o + 2]])
+
+    def four(k):
+        return bits(eng[k + 1 - nfar::nfar])
 
     def r(name, lo=0, hi=None, step=1, p=None):
         if hi is None:
@@ -285,6 +291,11 @@ def rank_program(g, core, T, topo):
     def ident(o, i):
         op("g", lambda: g.affine_select(o[0], i[0], [[-1, 128]], ALU.is_equal, 0.0, 0, 1), [o], [i])
 
+    def to_all(name, sem):
+        send([([piece(name, me)], [(dests[k], piece(name, me)) for k in ks], bits(eng[c::2]), sem, 0)
+              for c, ks in enumerate(halves)])
+        arrive(sem, len(eng) // 2 * (N - 1), [piece(name, q) for q in dests])
+
     def conv_turned(ps, lo, row, sel):
         for i in range(16):
             mm(r(ps, lo + i, lo + 128, 16), r(row, i, W, 16), r(sel), True, True)
@@ -296,12 +307,12 @@ def rank_program(g, core, T, topo):
         x = r(row, lo, hi)
         scan(r("TOP", 16 + lo, 16 + hi), x, x, col("TOP", 15 + lo) if lo else 0.0)
 
-    def gather_a(out, win, lst, lo, hi, base=0, olo=None):
+    def gather_a(out, win, lst, lo, hi, base=0, olo=None, acc=None):
         olo = lo if olo is None else olo
-        return act(r(out, olo, olo + hi - lo), ind(r(win), r(lst, base + lo // 16, base + hi // 16)))
+        return act(r(out, olo, olo + hi - lo), ind(r(win), r(lst, base + lo // 16, base + hi // 16)), acc=acc)
 
-    def gather_v(out, win, lst, lo, hi):
-        return cp(r(out, lo, hi), ind(r(win), r(lst, lo // 16, hi // 16)))
+    def gather_v(out, win, lst, lo, hi, base=0):
+        return cp(r(out, lo, hi), ind(r(win), r(lst, base + lo // 16, base + hi // 16)))
 
     def nothing():
         return None
@@ -309,9 +320,6 @@ def rank_program(g, core, T, topo):
     def filler(calls):
         calls = list(calls)
         return lambda: calls.pop(0)() if calls else None
-
-    def parts(out, win, lst):
-        return [lambda lo=lo, hi=hi: gather_v(out, win, lst, lo, hi) for lo, hi in zip(WAITS[:-1], WAITS[1:])]
 
     def warp_top(new, old, lst, calls=(), sel=None):
         fill = filler(calls)
@@ -371,22 +379,18 @@ def rank_program(g, core, T, topo):
         return tt(r(out, lo, hi), ind(r("R9", 16 * n, 16 * n + 9), r("sU%d" % n, lo // 16, hi // 16)), r(src, lo, hi),
                   ALU.mult)
 
-    def template(t, x, m, between=nothing):
+    def slot(t, k):
+        return rows("dM%d" % t, 128 * (k + 1), 128 * (k + 2))
+
+    def fold(t, m):
         d = "dM%d" % t
-        send([([piece(x, q)], [(q, rows(d, 128 * (k + 1), 128 * (k + 2)))], two(k), "rs%d" % t, 0)
-              for k, q in enumerate(dests)])
-        between()
-        arrive("rs%d" % t, 2 * (N - 1), [rows(d, 128, 128 * N)])
+        send([([rows(d, 128 * k + 16, 128 * k + 144) for k in range(N)], [(q, piece(m, me)) for q in dests], allm,
+               "ag%d" % t, 2)])
+        arrive("ag%d" % t, len(eng) * (N - 1), [piece(m, q) for q in dests])
 
-        def fold():
-            send([([rows(d, 128 * k + 16, 128 * k + 144) for k in range(N)], [(q, piece(m, me)) for q in dests], allm,
-                   "ag%d" % t, 2)])
-            arrive("ag%d" % t, len(eng) * (N - 1), [piece(m, q) for q in dests])
-
-        def echo():
-            send([([piece(m, prv(me))], [(prv(me), piece(m, prv(me)))], allm, "ec%d" % t, 0)])
-            arrive("ec%d" % t, len(eng), [piece(m, me)])
-        return fold, echo
+    def echo(t, m):
+        send([([piece(m, prv(me))], [(prv(me), piece(m, prv(me)))], allm, "ec%d" % t, 0)])
+        arrive("ec%d" % t, len(eng), [piece(m, me)])
 
     def own_piece(t, x):
         d = "dM%d" % t
@@ -397,11 +401,11 @@ def rank_program(g, core, T, topo):
         send([([r("nbS%d" % t, lo, lo + 128)], [((me - 1) % N, r("nbR%d" % t, lo, lo + 128))], allm, sem, 0)])
         return arrive(sem, len(eng), [r("nbR%d" % t, lo, lo + 128)])
 
-    def acc(t, slot, tr):
-        return col("acc", 20 * t + 5 * slot + tr)
+    def acc(t, j, tr):
+        return col("acc", 20 * t + 5 * j + tr)
 
-    def diff_pe(t, src, lo, ps, first=True, second=True):
-        for c in range(2):
+    def diff_pe(t, src, lo, ps, first=True, second=True, cols=H):
+        for c in range(cols // 512):
             a = lo + 512 * c
             if first:
                 mm(r(ps, 512 * c, 512 * c + 512), r("Ip"), r(src, a, a + 512), True, False)
@@ -410,40 +414,72 @@ def rank_program(g, core, T, topo):
 
     turn = [0]
 
-    def size_a(t, slot, tr, ps):
+    def size_a(t, j, tr, ps, cols=H):
         turn[0] = H - turn[0]
-        act(r("junk", turn[0], turn[0] + H), r(ps), AF.Abs, acc=acc(t, slot, tr))
+        act(r("junk", turn[0], turn[0] + cols), r(ps, 0, cols), AF.Abs, acc=acc(t, j, tr))
 
-    def size_v(t, slot, tr, x):
-        o = acc(t, slot, tr)
+    def size_v(t, j, tr, x):
+        o = acc(t, j, tr)
         op("v", lambda: V.tensor_reduce(o[0], x[0], AX.X, ALU.add, apply_absolute_value=True), [o], [x])
 
     def diff_v(t, d, x, lst, base, lo, hi):
         tt(r(d, lo, hi), ind(r(x), r(lst, base + lo // 16, base + hi // 16)), r("M%d" % t, lo, hi), ALU.subtract)
 
-    def size_s(t, slot, tr, d, lo, hi):
-        act(r(d, lo, hi), r(d, lo, hi), AF.Abs, acc=acc(t, slot, tr))
+    def size_s(t, j, tr, d, lo, hi):
+        act(r(d, lo, hi), r(d, lo, hi), AF.Abs, acc=acc(t, j, tr))
+
+    def size_pe(d, lo, hi, first, last):
+        ts(r("dP", lo, hi), r(d, lo, hi), 0.0, ALU.max)
+        for a in range(lo, hi, 128):
+            mm(r("pL", 128, 256), r(d, a, a + 128), r("Gn"), first and a == lo, False)
+            mm(r("pL", 128, 256), r("dP", a, a + 128), r("Gp"), False, last and a == hi - 128)
+
+    def row_sums(ps, row, weights):
+        for a in range(0, W, 128):
+            mm(ps, r(row, a, a + 128), r(weights), a == 0, a == W - 128)
+
+    def greater(tr, x):
+        send([([r(x), r("M1")], [(nxt, r(LAND[tr]))], allm, "fx%d" % tr, 2)])
+        arrive("fx%d" % tr, len(eng), [r(LAND[tr])])
+
+    def greater_back(tr, ps):
+        act(piece("So", tr, 128), ps)
+        send([([piece("So", tr, 128)], [(prv(me), piece("Si", tr, 128))], allm, "fb%d" % tr, 0)])
+        arrive("fb%d" % tr, len(eng), [piece("Si", tr, 128)])
 
     def elect(t):
-        keys, sums = r("pT", 272, 277), r("pL", 0, 5)
+        both = (("pT", 272), ("pB", 0))
+        keys, sums = [r(ps, lo, lo + 5) for ps, lo in both]
         mm(keys, r("Grp8"), r("Tc", 0, 5), True, False)
+        mm(sums, r("Grp8"), r("acc", 15, 20), True, False)
+        parts = [(3, r("S3"))]
+        if t:
+            parts = [(0, piece("Si", 0, 128))] + parts + [(1, piece("Si", 1, 128))]
+            for ps, lo in both:
+                mm(r(ps, lo, lo + 2), r("Grp8n"), r("accn", 0, 2), False, False)
+                mm(r(ps, lo, lo + 2), r("Sm"), r("eight", 0, 2), False, False)
+        for tr, x in parts:
+            for ps, lo in both:
+                mm(r(ps, lo + tr, lo + tr + 1), x, col("eight", 0), False, False)
         for j in range(3):
             x = r("acc", 20 * t + 5 * j, 20 * t + 5 * j + 5)
             mm(keys, r("Grp8"), x, False, j == 2)
-            mm(sums, r("Grp8"), x, j == 0, j == 2)
+            mm(sums, r("Grp8"), x, False, j == 2)
         for j, i in enumerate((keys, sums)):
             o = col("km", 4 * j)
             op("v", lambda o=o, i=i: V.tensor_reduce(o[0], i[0], AX.X, ALU.min), [o], [i])
         ts(r("eo"), r("base5"), col("km", 0), ALU.add, col("km", 4), ALU.subtract)
         cp(r("cU%d" % t), ind(r("Lall"), r("eo")))
 
-    def last_trial(t, x):
+    def last_trial(t, x, between=nothing):
         nb = "nbR%d" % t
         cuts = (0,) + LAST[t] + (W,)
         for j in range(3):
             diff_v(t, "d4", x, nb, 128, cuts[j], cuts[j + 1])
             if j < 2:
                 size_s(t, j, 4, "d4", cuts[j], cuts[j + 1])
+            if j == 0:
+                between()
         lall(4, nb, 128)()
         size_v(t, 2, 4, r("d4", cuts[2], W))
 
@@ -471,6 +507,8 @@ def rank_program(g, core, T, topo):
     def add_template(lo, hi):
         dma("g", r("V2", lo, hi, p=(16, 128)), r("M1", lo, hi, p=(0, 112)), "accm%d" % (lo > 0), accum_op=ALU.add)
         dma("g", r("V2", lo, hi, p=(0, 16)), r("M1", lo, hi, p=(112, 128)), "accm%d" % (lo > 0), accum_op=ALU.add)
+
+    waits = list(zip(WAITS[:-1], WAITS[1:]))
 
     dma("s", rows("dG", 0, 128), r("gam"), "ldg")
     dma("a", rows("dG", 128, 144), r("gam", p=(0, 16)), "ldg")
@@ -509,24 +547,22 @@ def rank_program(g, core, T, topo):
     cp(r("gamU"), r("gamI"))
     ts(col("TOP", 15), col("EQ", 0), -1.0, ALU.mult)
     ts(r("sel"), r("iF", 0, 128, 16), col("fC", 1), ALU.is_equal)
-
-    def after_pieces():
-        iota(r3("C3", 18, 32), [[0, 112]], 0, 0)
-        iota(r("fD", 5, 6), [[0, 1]], 0, 1)
-        iota(r("fD", 6, 7), [[0, 1]], 0, int(UNIT))
-        iota(r("iA"), [[0, 8], [1, 16]], 0, 0)
-        iota(r("one"), [[0, 128]], 1, 0)
-        iota(r("st2", H, 1664), [[0, 1664 - H]], 2, 0)
-
-    fold, echo = template(0, "X0", "M0", after_pieces)
-    fold()
+    send([([piece("X0", q)], [(q, slot(0, k))], two(k), "rs0", 0) for k, q in enumerate(dests)])
+    arrive("rs0", 2 * (N - 1), [rows("dM0", 128, 128 * N)])
+    iota(r3("C3", 18, 32), [[0, 112]], 0, 0)
+    iota(r("fD", 5, 6), [[0, 1]], 0, 1)
+    iota(r("fD", 6, 7), [[0, 1]], 0, int(UNIT))
+    iota(r("iA"), [[0, 8], [1, 16]], 0, 0)
+    iota(r("one"), [[0, 128]], 1, 0)
+    iota(r("st2", H, 1664), [[0, 1664 - H]], 2, 0)
+    fold(0, "M0")
     iota(r("st2", 1664, W), [[0, W - 1664]], 2, 0)
     iota(r("neg"), [[0, 128]], -1, 0)
     ident(r("In"), r("neg"))
     iota(r("acc"), [[0, 40]], 0, 0)
     iota(r("iG"), [[16, 8], [0, 16]], 0, 0)
     iota(r("fD", 2, 4), [[16, 2]], -1, 1)
-    echo()
+    echo(0, "M0")
     late = 0 if PW * me < H else H
     early = H - late
 
@@ -538,16 +574,14 @@ def rank_program(g, core, T, topo):
     ts(r("Ip"), r("iB"), col("fD", 5), ALU.is_equal)
     ts(r("lane"), r("iA"), col("fC", 0), ALU.is_equal)
     lall(2, "ewI", 128)()
-    blocks(0, [lambda: cp(r("nbR0", 0, 128), r("nbI")), lall(3, "nbI", 0),
-               lambda: ts(col("iC", 3), col("iP", 1), 127, ALU.bitwise_and),
-               lambda: ts(r("fD", 4, 5), col("EQ", 0), -1.0, ALU.mult, 1.0, ALU.add),
-               lambda: (cp(col("fC", 3), col("iC", 3)), ms(r("C4", 0, 127), 4.0)),
-               lambda: ms(r("cmu"), -3.5),
-               lambda: ts(col("C4", 127), col("EQ", 15), 4.0, ALU.add)])
+    blocks(0, [lambda: cp(r("nbR0", 0, 128), r("nbI")), lall(3, "nbI", 0)]
+           + [lambda lo=lo, hi=hi: gather_v("d2", "X0", "ewU", lo, hi, 128) for lo, hi in waits[1:]])
     diff_pe(0, "X0", early, "pA", second=False)
     diff_pe(0, "dA", early, "pC", second=False)
     diff_pe(0, "X0", late, "pB", second=False)
-    gather_a("d2", "X0", "ewU", 0, W, base=128)
+    gather_a("d2", "X0", "ewU", 0, WAITS[1], base=128)
+    gather_a("d2", "X0", "ewU", WAITS[-1], W, base=128)
+    gather_a("d3", "X0", "nbR0", late, late + 512)
     act(r("Lall", 0, 640, 5), r("iF", 0, 128), scale=16.0, bias=col("fC", 0))
     act(r("Tc"), r("iF", 0, 8), scale=1.0 / 128)
     act(r("base5"), r("Lall", 0, 40, 5), scale=5.0)
@@ -560,51 +594,65 @@ def rank_program(g, core, T, topo):
     counted(0, r("iv16"), 128)
     turn_back("iv16", "pL", 384)
     ts(r("Grp8"), r("iG"), col("fC", 1), ALU.is_equal, 8.0, ALU.mult)
-    ts(r("Sh"), r("iB"), col("fC", 3), ALU.is_equal)
     cp(r("nbS0", 128, 256), r("pL", 384, 512))
     dma("s", r("payS"), r("pay"), "lpay", [neighbour(0, 128, "nb0")])
+    iota(r("eight"), [[0, 8]], 8, 0)
     iota(r("st1"), [[0, W]], 1, 0)
+    act(r("Gp"), r("Grp8"), scale=0.25)
+    act(r("Gn"), r("Grp8"), scale=-0.125)
     diff_pe(0, "X0", late, "pB", first=False)
     diff_pe(0, "d2", early, "pC")
     diff_v(0, "d3", "X0", "nbR0", 0, early + 512, early + H)
     size_a(0, 1, 0, "pB")
     diff_pe(0, "dA", late, "pA")
     size_a(0, 0, 2, "pC")
-    diff_v(0, "d3", "X0", "nbR0", 0, late, late + H)
+    diff_v(0, "d3", "X0", "nbR0", 0, late + 512, late + H)
     diff_pe(0, "d2", late, "pB")
     size_a(0, 1, 1, "pA")
+    diff_pe(0, "d3", late, "pC", cols=512)
     size_a(0, 1, 2, "pB")
-    size_s(0, 0, 3, "d3", 0, W)
-    last_trial(0, "X0")
-    elect(0)
-
-    warp_top("G1", "G0", "cU0", [lambda: cp(r("c16"), r("cU0")),
-                                 lambda: ts(r("S1"), r("iB"), col("fD", 2), ALU.is_equal, col("fD", 4), ALU.mult),
-                                 lambda: ts(r("S2"), r("iB"), col("fD", 3), ALU.is_equal, col("EQ", 0), ALU.mult)])
-    gather_a("X1", "X0", "cU0", 0, W)
-    own_piece(1, "X1")
-    fold, echo = template(1, "X1", "MP")
-    ts(r("D15"), r("Ip"), col("EQ", 15), ALU.mult)
-    tt(r("S1"), r("S1"), r("Ip"), ALU.subtract)
-    cp(r("ewU", 256, 512), r("ewI", 256, 512))
-    slopes_pe()
-    blocks(1, [lambda: slopes_v(0), lall(1, "ewI", 256), lall(2, "ewI", 384)])
-    conv_turned("pL", 128, "IR", "sel")
+    size_pe("d3", early, early + H, True, False)
+    size_pe("d3", late + 512, late + H, False, True)
+    size_a(0, 1, 3, "pC", 512)
+    last_trial(0, "X0", lambda: act(r("S3"), r("pL", 128, 256)))
     act(r("R9", 4, 9), r("rhoS", 0, 5))
     for j in range(4):
         act(col("R9", j), col("rhoS", 4 - j))
-    gather_a("pc", "payS", "cU0", 0, H)
-    gather_a("pc", "payS", "cU0", H, W)
     act(r("I8"), r("Ip"), scale=1.0 / N)
     for tab, sc in ((1, 32.0), (2, 1.0 / 32), (3, 1.0 / N)):
         act(r("R9", 16 * tab, 16 * tab + 9), r("R9", 0, 9), scale=sc)
+    elect(0)
+
+    warp_top("G1", "G0", "cU0", [lambda: ts(r("fD", 4, 5), col("EQ", 0), -1.0, ALU.mult, 1.0, ALU.add),
+                                 lambda: ts(r("S1"), r("iB"), col("fD", 2), ALU.is_equal, col("fD", 4), ALU.mult),
+                                 lambda: ts(r("S2"), r("iB"), col("fD", 3), ALU.is_equal, col("EQ", 0), ALU.mult)])
+    for c, ks in enumerate(halves):
+        for lo, hi in runs((far, near)[c]):
+            gather_a("X1", "X0", "cU0", lo, hi)
+        send([([piece("X1", dests[k])], [(dests[k], slot(1, k))], (two, four)[c](k), "rs1", 0) for k in ks])
+    own_piece(1, "X1")
+    arrive("rs1", 2 * nfar + 4 * (nfar - 1), [rows("dM1", 128, 128 * N)])
+    ts(r("D15"), r("Ip"), col("EQ", 15), ALU.mult)
+    tt(r("S1"), r("S1"), r("Ip"), ALU.subtract)
+    cp(r("c16"), r("cU0"))
+    ms(r("C4", 0, 127), 4.0)
+    ts(col("C4", 127), col("EQ", 15), 4.0, ALU.add)
+    slopes_pe()
+    blocks(1, [lambda: ts(col("iC", 3), col("iP", 1), 127, ALU.bitwise_and), lall(1, "ewI", 256), lall(2, "ewI", 384),
+               lambda: slopes_v(0), lambda: cp(r("ewU", 256, 512), r("ewI", 256, 512)),
+               lambda: cp(col("fC", 3), col("iC", 3)), lambda: ms(r("cmu"), -3.5)])
+    ts(r("Sh"), r("iB"), col("fC", 3), ALU.is_equal)
+    conv_turned("pL", 128, "IR", "sel")
+    gather_a("pc", "payS", "cU0", 0, H)
+    gather_a("pc", "payS", "cU0", H, W)
+    act(r("Grp8n"), r("Grp8"), scale=-1.0)
     act(r("I32b"), r("Ip"), scale=1.0 / 32)
     act(r("I128b"), r("Ip"), scale=1.0 / (16 * N))
     weigh("V1", "pc", 0, 0, 512)
     counted(1, r("ivS0"), 128)
     mean_send(0)
-    fold()
-    echo()
+    fold(1, "MP")
+    echo(1, "MP")
     weigh("V1", "pc", 0, 512, W)
     mean_sum(0)
 
@@ -613,46 +661,49 @@ def rank_program(g, core, T, topo):
         mm(r("pL", 384, 512), r("Sh"), r("c16"), True, True)
         slopes_pe()
 
-    warp_top("G2", "G1", "muU0", [shifted, lambda: cp(r("muS"), r("pL", 384, 512)), lambda: slopes_v(1)], "sel2")
-    gather_a("X2", "X1", "muU0", 0, W)
-    gather_a("M1", "MP", "muS", H, W)
-    calls = parts("M1", "MP", "muS")
-    calls[0]()
-    blocks(2, [lambda: cp(r("nbS1", 0, 128), r("pC", 512, 640))] + calls[1:])
-    neighbour(1, 0, "nbg1")
-    diff_pe(1, "X2", H, "pA")
-    diff_pe(1, "X2", 0, "pB", second=False)
+    def warp_out():
+        cp(r("nbS1", 0, 128), r("pC", 512, 640))
+        neighbour(1, 0, "nbg1")
+
+    warp_top("G2", "G1", "muU0", [shifted, nothing, lambda: cp(r("muS"), r("pL", 384, 512))], "sel2")
+    slopes_v(1)
+    gather_a("tmp", "V1", "muU0", 0, H)
+    gather_a("X2", "X1", "muU0", 0, W, acc=col("accn", 0))
+    gather_v("M1", "MP", "muS", PW * me, PW * me + PW)
+    to_all("M1", "am")
+    blocks(2, [warp_out] + [lambda lo=lo, hi=hi: weigh("V2", "tmp", 1, lo, hi) for lo, hi in waits])
+    gather_a("dA", "X2", "ewU", 0, W, base=256, acc=col("accn", 1))
+    sums = [r("pC", 0, 128), r("pC", 512, 640)]
     conv_turned("pL", 128, "IR", "sel2")
-    gather_v("M1", "MP", "muS", WAITS[-1], H)
-    diff_v(1, "d2", "X2", "ewU", 384, H, H + 384)
+    greater(0, "X2")
+    greater(1, "dA")
+    weigh("V2", "tmp", 1, WAITS[-1], H)
     counted(2, r("iv16"), 128)
     turn_back("iv16", "pL", 384)
-    diff_v(1, "d2", "X2", "ewU", 384, H + 384, H + 640)
+    diff_v(1, "d3", "X2", "nbR1", 0, 0, 256)
     cp(r("nbS1", 128, 256), r("pL", 384, 512))
     neighbour(1, 128, "nb1")
-    gather_a("dA", "X2", "ewU", 0, W, base=256)
-    size_a(1, 1, 0, "pA")
-    diff_pe(1, "X2", 0, "pB", first=False)
-    diff_v(1, "d2", "X2", "ewU", 384, H + 640, W)
-    size_v(1, 0, 0, r("pB"))
-    gather_a("tmp", "V1", "muU0", 0, H)
-    diff_pe(1, "dA", 0, "pC")
-    diff_pe(1, "dA", H, "pA")
-    diff_v(1, "d3", "X2", "nbR1", 0, 0, H)
-    gather_a("d2", "X2", "ewU", 0, H, base=384)
-    weigh("V2", "tmp", 1, 0, H)
-    add_template(0, H)
-    size_a(1, 0, 1, "pC")
-    diff_pe(1, "d2", 0, "pB")
-    diff_v(1, "d3", "X2", "nbR1", 0, H, W)
-    size_a(1, 1, 1, "pA")
+    row_sums(r("pT", 384, 512), "M1", "Gn")
     gather_a("tmp", "V1", "muU0", H, W)
-    size_s(1, 1, 2, "d2", H, W)
-    lall(3, "nbR1", 0)()
+    gather_a("d2", "X2", "ewU", 0, H, base=384)
+    act(r("Sm"), r("pT", 384, 512))
+    gather_a("d2", "X2", "ewU", H, W, base=384)
+    diff_v(1, "d3", "X2", "nbR1", 0, 256, W)
+    diff_pe(1, "d2", 0, "pA")
+    row_sums(sums[0], LAND[0], "Gp")
+    diff_pe(1, "d2", H, "pB")
+    size_a(1, 0, 2, "pA")
+    size_s(1, 0, 3, "d3", 0, H)
+    greater_back(0, sums[0])
     weigh("V2", "tmp", 1, H, W)
+    row_sums(sums[1], LAND[1], "Gp")
+    lall(3, "nbR1", 0)()
+    size_pe("d3", H, W, True, True)
+    size_a(1, 1, 2, "pB")
+    greater_back(1, sums[1])
+    add_template(0, H)
     add_template(H, W)
-    size_a(1, 0, 2, "pB")
-    size_s(1, 0, 3, "d3", 0, W)
+    act(r("S3"), r("pL", 128, 256))
     last_trial(1, "X2")
     elect(1)
 
@@ -661,33 +712,38 @@ def rank_program(g, core, T, topo):
         slopes_pe()
 
     warp_top("G3", "G2", "cU1", [slopes_3, nothing, lambda: slopes_v(2)], "sel")
-    calls = parts("U", "V2", "cU1")
-    calls[0]()
+    gather_v("X3", "X2", "cU1", PW * prv(me), PW * prv(me) + PW)
     for c, ks in enumerate(halves):
-        for lo, hi in runs((far, near)[c]):
+        for lo, hi in runs([prv(dests[k]) for k in ks]):
             gather_a("X3", "X2", "cU1", lo, hi)
-        send([([piece("X3", prv(dests[k]))], [(dests[k], piece("xq", k))], bits(eng[k + 1 - nfar::nfar]) if c else two(k),
-               "ax%d" % c, 0) for k in ks])
+        send([([piece("X3", prv(dests[k]))], [(dests[k], piece("xq", k))], (two, four)[c](k), "ax%d" % c, 0) for k in ks])
         arrive("ax%d" % c, 2 * (c + 1) * len(ks), [piece("xq", k) for k in ks])
-    blocks(3, [lambda: cp(r("glU"), r("pC", 512, 640))] + calls[1:])
-    conv_turned("pL", 128, "IR", "sel")
+    last, own = PW * dests[-1], PW * me
+    cuts = [(last, last + 96), (last + 96, last + 160), (last + 160, last + PW), (own, own + 160), (own + 160, own + PW)]
+    blocks(3, [lambda: cp(r("glU"), r("pC", 512, 640))]
+           + [lambda lo=lo, hi=hi: gather_v("P3", "payS", "glU", lo, hi) for lo, hi in cuts])
     for c, ks in enumerate(halves):
         for k in ks:
-            gather_a("P3", "payS", "glU", PW * dests[k], PW * dests[k] + PW)
+            if k < N - 2:
+                gather_a("P3", "payS", "glU", PW * dests[k], PW * dests[k] + PW)
         send([([piece("P3", dests[k])], [(dests[k], piece("pq", k))], two(k), "ap%d" % c, 0) for k in ks])
         arrive("ap%d" % c, 2 * len(ks), [piece("pq", k) for k in ks])
         if c == 0:
             srcs = [piece("xq", k) for k in range(N - 1)] + [piece("X3", prv(me))]
-            send([(srcs, [(prv(me), r(x))], bits(eng[j::2]), "aq", 2 - j) for j, x in enumerate(("qM", "qS"))])
-            arrive("aq", len(eng), [r("qM"), r("qS")])
-    gather_a("P3", "payS", "glU", PW * me, PW * me + PW)
-    weigh("V3", "U", 2, 0, 512)
-    counted(3, r("ivS1"), 128)
-    mean_send(1)
-    weigh("V3", "U", 2, 512, UC[0])
+            send([(srcs, [(prv(me), r("qM"))], allm, "aq", 2)])
+            arrive("aq", len(eng), [r("qM")])
+            for k, x in enumerate(srcs):
+                mm(r("pB", 0, PW), r("Ip"), x, k == 0, k == N - 1)
+    conv_turned("pL", 128, "IR", "sel")
     for lo, hi in zip(UC[:-1], UC[1:]):
         gather_a("U", "V2", "cU1", lo, hi)
         weigh("V3", "U", 2, lo, hi)
+        if lo == 0:
+            counted(3, r("ivS1"), 128)
+            act(r("qSs"), r("pB", 0, PW))
+            send([([r("qSs")], [(prv(me), r("qS"))], allm, "as", 0)])
+            arrive("as", len(eng), [r("qS")])
+            mean_send(1)
     mm(r("pA", 0, PW), r("I8"), piece("P3", me), True, False)
     for k in halves[0]:
         mm(r("pA", 0, PW), r("I8"), piece("pq", k), False, False)
@@ -696,9 +752,7 @@ def rank_program(g, core, T, topo):
     for k in halves[1]:
         mm(r("pA", 0, PW), r("I8"), piece("pq", k), False, k == N - 2)
     act(piece("QM", me), r("pA", 0, PW))
-    send([([piece("QM", me)], [(q, piece("QM", me))], bits(eng[j::nfar]), "aqm" if j else "aqf", 0)
-          for j, q in enumerate(served)])
-    arrive("aqf", len(eng) // nfar, [piece("QM", mate)])
+    to_all("QM", "aqm")
     mean_sum(1)
     slopes_pe()
     slopes_v(3)
@@ -712,15 +766,12 @@ def rank_program(g, core, T, topo):
                 send([([piece("U", i)], [(served[1 + i % nfar], piece("uq", i))], bits(eng[j::len(ks)]), "au%d" % c, 0)
                       for j, i in enumerate(ks)])
                 arrive("au%d" % c, len(eng), [piece("uq", i) for i in ks])
-        if k == QC:
-            send([([piece("QM", mate)], [(q2, piece("QM", mate)) for q2 in served[1:]], allm, "aqm", 0)])
-            arrive("aqm", (len(eng) // nfar + len(eng)) * (nfar - 1), [piece("QM", q2) for q2 in dests if q2 != mate])
     send([([piece("uq", i) for i in range(nfar - 1)] + [piece("U", nfar - 1)], [(mate, piece("uq", nfar - 1))], allm,
            "auf", 1)])
     arrive("auf", len(eng), [piece("uq", nfar - 1)])
     run = r("pC", 0, PW)
-    tt(r("qg2"), ind(r("QM"), r("muU1", 16 * me, 16 * me + 16)), piece("U", N - 1), ALU.add)
-    tt(run, r("qg2"), piece("uq", nfar), ALU.add)
+    tt(r("qg"), ind(r("QM"), r("muU1", 16 * me, 16 * me + 16)), piece("U", N - 1), ALU.add)
+    tt(run, r("qg"), piece("uq", nfar), ALU.add)
     tt(run, run, piece("uq", nfar + 1), ALU.add)
     tt(run, run, piece("uq", nfar + 2), ALU.add)
     tt(r("ysb"), run, piece("uq", nfar - 1), ALU.add)

from concourse.bass import DstId, RemoteDMATransfer
from concourse.mybir import AluOpType as ALU, AxisListType as AX, ActivationFunctionType as AF

W = 2048
H = W // 2
PW = 256
GV = (768, 1408)
NVAL_V = 10
TAIL = [(0, 1), (2,), (4, 5), (6,)]
MAGIC = 12582912.0
UNIT = 8192.0
USES = [(2.0, -256.0), (1.0, -256.0), (1.0, 128.0), (2.0, 128.0)]
LOW = -5.0e6
WAITS = (0, 96, 160, 256, 416, 480, 576)
UC = (0, 512, 1024, 1536, W)
LAST = ((512, 896), (1024, 1536))
LAND = ("X0", "G0")

SCRATCH = {}


def _buf(where, dtype, cols, *names, rows=128):
    for n in names:
        SCRATCH[n] = (where, [rows, cols], dtype)


_buf("sbuf", "bfloat16", W, "X0", "X1", "X2", "X3", "payS", "P3", "G0", "G1", "G2", "G3", "IR", "M0", "M1", "MP",
     "dA", "d2", "d3", "d4", "dP", "junk", "pc", "xq", "pq", "VAL", "st1", "st2")
_buf("sbuf", "bfloat16", W + 16, "TOP")
_buf("sbuf", "float32", W, "V1", "V2", "V3", "tmp", "U", "QM", "uq")
_buf("sbuf", "float32", W + 264, "WIN")
_buf("sbuf", "int32", 128, "gamI", "nbI")
_buf("sbuf", "int32", 512, "ewI")
_buf("sbuf", "uint16", 512, "ewU")
_buf("sbuf", "uint16", 128, "gamU", "cU0", "cU1", "muU0", "muU1", "muS", "sU0", "sU1", "sU2", "sU3", "glU")
_buf("sbuf", "uint16", 256, "nbS0", "nbS1", "nbR0", "nbR1")
_buf("sbuf", "uint16", 8, "eo", "offU")
_buf("sbuf", "float16", 128, "ivS0", "ivS1", "cmu", "FM", "DN", "c16", "C4", "gl16", "iv16")
_buf("sbuf", "float16", 7 * 128, "ivR0", "ivR1")
_buf("sbuf", "float16", 256, "A2", "B2", "N2")
SCRATCH["N3"] = ("sbuf", [128, 8, 32], "float16")
SCRATCH["C3"] = ("sbuf", [128, 8, 32], "bfloat16")
_buf("sbuf", "int32", 2, "iP")
_buf("sbuf", "int32", 4, "iC")
_buf("sbuf", "float32", 8, "fC", "fD", "base5", "Tc", "km", "rhoS", "accn", "eight")
_buf("sbuf", "float32", 40, "acc")
_buf("sbuf", "float32", 144, "iF")
_buf("sbuf", "float32", 128, "iG", "iA", "Grp8", "Grp8n", "SRC", "S3", "Sm")
_buf("sbuf", "float32", 256, "So", "Si")
_buf("sbuf", "float32", 16, "EQ", "GT")
_buf("sbuf", "float32", 64, "R9")
_buf("sbuf", "float32", 640, "Lall")
_buf("sbuf", "bfloat16", 8, "sel", "sel2")
_buf("sbuf", "bfloat16", 128, "iB", "one", "neg", "Kd", "lane", "Ip", "In", "I8", "I32b", "I128b", "Sh", "S1",
     "S2", "D15", "Gp", "Gn")
_buf("sbuf", "bfloat16", PW, "qM", "qS", "qSs")
_buf("sbuf", "float32", PW, "qg", "ysb")
_buf("dram", "bfloat16", PW, "dM0", "dM1", rows=8 * 128 + 16)
_buf("dram", "int32", 128, "dG", rows=128 + 16)
_buf("psum", "float32", 1024, "pA", "pB", "pC")
_buf("psum", "float32", 512, "pT", "pL")

SEMAPHORES = (["qv", "qa", "qt", "qg", "sent", "lgam", "lxs", "lew", "lrho", "lpay", "fill", "ldg", "sty", "aq", "am",
               "as", "aqm", "auf"]
              + ["%s%d" % (s, t) for s in ("own", "accm", "rs", "ag", "ec", "nbg", "nb", "mu", "ax", "ap", "fx", "fb")
                 for t in range(2)]
              + ["au%d" % k for k in range(len(TAIL))])
QSEM = {"v": "qv", "a": "qa", "t": "qt", "g": "qg"}


def _overlap(a, b):
    if a[0] != b[0] or a[2] <= b[1] or b[2] <= a[1]:
        return False
    if a[3] > 1 and a[3] == b[3] and (a[1] - b[1]) % a[3]:
        return False
    return True


def _emit(g, T, ops):
    Q = {"v": g.vector, "a": g.scalar, "t": g.tensor, "g": g, "s": g.sync}
    total = {}
    for o in ops:
        if o["sem"]:
            total[o["sem"]] = total.get(o["sem"], 0) + o["inc"]
    hist, known = {}, {q: {} for q in Q}
    for n, o in enumerate(ops):
        deps = set(o["after"])
        for regs, wr in ((o["ins"], False), (o["outs"], True)):
            for x in regs:
                ps = SCRATCH.get(x[0], ("",))[0] == "psum"
                for (m, y, w2) in hist.get(x[0], []):
                    p = ops[m]
                    if m == n or (p["q"] == "t" and o["q"] == "t"):
                        continue
                    if ps and p["q"] != o["q"]:
                        if x[1] // 512 <= (y[2] - 1) // 512 and y[1] // 512 <= (x[2] - 1) // 512:
                            deps.add(m)
                    elif (wr or w2) and _overlap(x, y):
                        deps.add(m)
        for regs, wr in ((o["ins"], False), (o["outs"], True)):
            for x in regs:
                hist.setdefault(x[0], []).append((n, x, wr))
        o["waits"] = []
        if o["q"] is None:
            o["know"] = {}
            continue
        k = known[o["q"]]
        for m in sorted(deps, reverse=True):
            p = ops[m]
            key, val = (p["sem"], 1 << 30) if p["sem"] else (p["q"], m)
            if p["sem"] == "sent":
                raise ValueError("a source of a remote write is overwritten")
            if p["sem"] and p["sem"] == o["sem"]:
                continue
            if k.get(key, -1) >= val:
                continue
            o["waits"].append(m)
            p["need"] = True
            k[key] = val
            if not p["sem"]:
                for kk, vv in p["know"].items():
                    if k.get(kk, -1) < vv:
                        k[kk] = vv
        o["know"] = dict(k)
    count, waited = {}, {}
    for o in ops:
        if o["q"] and not o["sem"] and o["need"]:
            count[o["q"]] = count.get(o["q"], 0) + 1
            o["val"] = count[o["q"]]
    for o in ops:
        if o["q"] is None:
            continue
        for m in o["waits"]:
            p = ops[m]
            s, v = (p["sem"], total[p["sem"]]) if p["sem"] else (QSEM[p["q"]], p["val"])
            Q[o["q"]].wait_ge(T.sem[s], v)
            waited[s] = max(waited.get(s, 0), v)
        ins = o["fn"]()
        if o["sem"] and o["sem"] != "sent":
            ins.then_inc(T.sem[o["sem"]], 16)
        elif not o["sem"] and o["need"]:
            ins.then_inc(T.sem[QSEM[o["q"]]], 1)
    for q, c in count.items():
        total[QSEM[q]] = c
    for s, v in total.items():
        if waited.get(s, 0) < v:
            (g.sync if s == "sty" else g).wait_ge(T.sem[s], v)


def rank_program(g, core, T, topo):
    me = T.rank_of(core)
    if me is None:
        return
    cores = list(T.cores)
    N = len(cores)
    ops = []
    V, A, PE = g.vector, g.scalar, g.tensor

    def sides(s):
        same = [r for r in range(N) if topo.die(cores[r]) == topo.die(cores[s])]
        return same, [r for r in range(N) if r not in same]

    def dest(s, k):
        same, other = sides(s)
        i = same.index(s)
        if k < len(other):
            return other[(i + k) % len(other)]
        return same[(i + k - len(other) + 1) % len(same)]

    def prv(s):
        same = sides(s)[0]
        return same[(same.index(s) - 1) % len(same)]

    def did(r):
        a = topo.addr(cores[r])
        return DstId(rid=a[0], pnc=a[1])

    def bits(es):
        return sum(1 << e for e in es)

    def runs(ranks):
        out = []
        for q in sorted(ranks):
            if out and out[-1][1] == PW * q:
                out[-1][1] += PW
            else:
                out.append([PW * q, PW * q + PW])
        return out

    near, far = sides(me)
    nfar = len(far)
    mine = near.index(me)
    mate = far[mine]
    nxt = near[(mine + 1) % nfar]
    dests = [dest(me, k) for k in range(N - 1)]
    served = [mate] + dests[nfar:]
    halves = (range(nfar), range(nfar, N - 1))
    eng = topo.engines(core, cores[dests[0]])
    allm = bits(eng)

    def two(k):
        j, o = (k, 0) if k < nfar else (k - nfar, 1)
        return bits([eng[4 * j + o], eng[4 * j + o + 2]])

    def four(k):
        return bits(eng[k + 1 - nfar::nfar])

    def r(name, lo=0, hi=None, step=1, p=None):
        if hi is None:
            hi = T[name].shape[1]
        ps = slice(None) if p is None else slice(p[0], p[1])
        ap = T[name][ps, lo:hi:step] if step > 1 else T[name][ps, lo:hi]
        return (ap, [(name, lo, hi, step)], [])

    def r3(name, lo=0, hi=32):
        return (T[name][:, :, lo:hi], [(name, lo, hi, 1)], [])

    def rows(name, a, b):
        return (T[name][a:b, :], [(name, a, b, 1)], [])

    def ind(win, off):
        return (win[0].indirect(off[0]), win[1], off[1])

    def op(q, fn, outs, ins, sem=None, inc=16, after=()):
        o = {"q": q, "fn": fn, "sem": sem, "inc": inc, "need": False, "after": list(after), "outs": [], "ins": []}
        for x in outs:
            o["outs"] += x[1]
            o["ins"] += x[2]
        for x in ins:
            if isinstance(x, tuple):
                o["ins"] += x[1] + x[2]
        ops.append(o)
        return len(ops) - 1

    def a_(x):
        return x[0] if isinstance(x, tuple) else x

    def cp(o, i):
        return op("v", lambda: V.tensor_copy(o[0], i[0]), [o], [i])

    def tt(o, a, b, alu):
        return op("v", lambda: V.tensor_tensor(o[0], a[0], b[0], alu), [o], [a, b])

    def ts(o, a, s1, o0, s2=None, o1=None):
        if o1 is None:
            return op("v", lambda: V.tensor_scalar(o[0], a[0], a_(s1), None, o0), [o], [a, s1])
        return op("v", lambda: V.tensor_scalar(o[0], a[0], a_(s1), a_(s2), o0, o1), [o], [a, s1, s2])

    def ms(o, c):
        return op("v", lambda: V.memset(o[0], c), [o], [])

    def scan(o, a, b, init, o0=ALU.max, o1=ALU.max):
        return op("v", lambda: V.tensor_tensor_scan(o[0], a[0], b[0], a_(init), o0, o1), [o], [a, b, init])

    def act(o, i, f=AF.Identity, scale=None, bias=None, acc=None):
        kw = {}
        if scale is not None:
            kw["scale"] = a_(scale)
        if bias is not None:
            kw["bias"] = a_(bias)
        if acc is not None:
            kw["accum_out"] = acc[0]
        return op("a", lambda: A.activation(o[0], i[0], f, **kw), [o] + ([acc] if acc else []), [i, scale, bias])

    def mm(o, l, x, st, sp):
        return op("t", lambda: PE.matmul(o[0], l[0], x[0], st, sp), [o], [l, x])

    def dma(q, o, i, sem, after=(), **kw):
        e = {"s": g.sync, "a": A, "g": g}[q]
        return op(q, lambda: e.dma_start(o[0], i[0], **kw), [o], [i], sem=sem, after=after)

    def send(trs):
        def fn():
            return g.remote_dma_fused([RemoteDMATransfer(
                dst_ids=[did(d) for d, _ in ds], dma_engine_mask=m, remote_sem=T.sem[s], srcs=[x[0] for x in ss],
                dsts=[x[0] for _, x in ds], alu_op=f) for ss, ds, m, s, f in trs], local_sem=T.sem["sent"])
        return op("g", fn, [], [x for t in trs for x in t[0]], sem="sent", inc=sum(bin(t[2]).count("1") for t in trs))

    def arrive(sem, n, places):
        return op(None, None, places, [], sem=sem, inc=n)

    def piece(name, o, w=PW):
        return r(name, w * o, w * o + w)

    def col(name, j):
        return r(name, j, j + 1)

    def iota(o, pat, base, cm):
        op("g", lambda: g.iota(o[0], pat, base, cm, allow_small_or_imprecise_dtypes=True), [o], [])

    def ident(o, i):
        op("g", lambda: g.affine_select(o[0], i[0], [[-1, 128]], ALU.is_equal, 0.0, 0, 1), [o], [i])

    def to_all(name, sem):
        send([([piece(name, me)], [(dests[k], piece(name, me)) for k in ks], bits(eng[c::2]), sem, 0)
              for c, ks in enumerate(halves)])
        arrive(sem, len(eng) // 2 * (N - 1), [piece(name, q) for q in dests])

    def conv_turned(ps, lo, row, sel):
        for i in range(16):
            mm(r(ps, lo + i, lo + 128, 16), r(row, i, W, 16), r(sel), True, True)

    def turn_back(src, ps, at):
        mm(r(ps, at, at + 128), r(src), r("Ip"), True, True)

    def top_part(row, lo, hi):
        x = r(row, lo, hi)
        scan(r("TOP", 16 + lo, 16 + hi), x, x, col("TOP", 15 + lo) if lo else 0.0)

    def gather_a(out, win, lst, lo, hi, base=0, olo=None, acc=None):
        olo = lo if olo is None else olo
        return act(r(out, olo, olo + hi - lo), ind(r(win), r(lst, base + lo // 16, base + hi // 16)), acc=acc)

    def gather_v(out, win, lst, lo, hi, base=0):
        return cp(r(out, lo, hi), ind(r(win), r(lst, base + lo // 16, base + hi // 16)))

    def nothing():
        return None

    def filler(calls):
        calls = list(calls)
        return lambda: calls.pop(0)() if calls else None

    def warp_top(new, old, lst, calls=(), sel=None):
        fill = filler(calls)
        gather_v(new, old, lst, 0, GV[0])
        gather_a(new, old, lst, GV[0], GV[1])
        gather_a(new, old, lst, GV[1], W)
        for lo, hi in ((0, GV[0]), GV, (GV[1], W)):
            fill()
            top_part(new, lo, hi)
        if sel:
            conv_turned("pC", 0, new, sel)
        for c in range(17):
            mm(r("pT", c + 1, 256, 32), r("TOP", 31 - c, 31 - c + W - 15, 16), r("sel"), True, True)
        if sel:
            cp(r("gl16"), r("pC", 0, 128))
            turn_back("gl16", "pC", 512)

    def blocks(n, calls=()):
        sc, base = USES[n]
        fill = filler(calls)
        tt(r("A2"), r("pT", 0, 256), r3("C3"), ALU.min)
        fill()
        tt(r("B2"), r("A2"), r("pT", 1, 257), ALU.is_le)
        fill()
        scan(r("N2"), r("B2"), r("A2"), 0.0, ALU.mult, ALU.max)
        fill()
        cp(r3("N3"), r("N2"))
        fill()
        mm(r("pL", 0, 128), r("one"), r("Kd"), True, False)
        tt(r("FM"), r3("N3", 16, 32), r("lane"), ALU.mult)
        mm(r("pT", 264, 272), r("FM"), r("sel"), True, True)
        tt(r("DN"), r3("N3", 16, 32), r3("N3", 0, 16), ALU.subtract)
        mm(r("pL", 0, 128), r("DN"), r("Ip"), False, True)
        fill()
        cp(r("offU"), r("pT", 264, 272))
        ts(r("SRC"), r("pL", 0, 128), sc, ALU.mult, sc * (UNIT * (base + 0.5) - 0.5), ALU.add)
        fill()
        cp(ind(r("WIN"), r("offU")), r("SRC"))
        fill()
        scan(r("IR"), r("WIN", 0, W), r("st%d" % int(sc)), sc * UNIT * (base - (0.1875 if base > 0 else 0.375)),
             ALU.max, ALU.add)

    def counted(n, out, lo):
        sc, base = USES[n]
        ts(out, r("pL", lo, lo + 128), 1.0 / (sc * UNIT), ALU.mult, -16.0 * base, ALU.add)

    def slopes_pe():
        mm(r("pL", 256, 384), r("Ip"), r("C4"), True, False)
        mm(r("pL", 256, 383), r("S2"), r("c16", 1, 128), False, False)
        mm(r("pL", 383, 384), r("D15"), r("c16", 127, 128), False, False)
        mm(r("pL", 256, 384), r("S1"), r("c16"), False, True)

    def slopes_v(n):
        ts(r("sU%d" % n), r("pL", 256, 384), 0.0, ALU.max, 8.0, ALU.min)

    def weigh(out, src, n, lo, hi):
        return tt(r(out, lo, hi), ind(r("R9", 16 * n, 16 * n + 9), r("sU%d" % n, lo // 16, hi // 16)), r(src, lo, hi),
                  ALU.mult)

    def slot(t, k):
        return rows("dM%d" % t, 128 * (k + 1), 128 * (k + 2))

    def fold(t, m):
        d = "dM%d" % t
        send([([rows(d, 128 * k + 16, 128 * k + 144) for k in range(N)], [(q, piece(m, me)) for q in dests], allm,
               "ag%d" % t, 2)])
        arrive("ag%d" % t, len(eng) * (N - 1), [piece(m, q) for q in dests])

    def echo(t, m):
        send([([piece(m, prv(me))], [(prv(me), piece(m, prv(me)))], allm, "ec%d" % t, 0)])
        arrive("ec%d" % t, len(eng), [piece(m, me)])

    def own_piece(t, x):
        d = "dM%d" % t
        dma("s", rows(d, 0, 128), piece(x, me), "own%d" % t)
        dma("s", rows(d, 128 * N, 128 * N + 16), r(x, PW * me, PW * me + PW, p=(0, 16)), "own%d" % t)

    def neighbour(t, lo, sem):
        send([([r("nbS%d" % t, lo, lo + 128)], [((me - 1) % N, r("nbR%d" % t, lo, lo + 128))], allm, sem, 0)])
        return arrive(sem, len(eng), [r("nbR%d" % t, lo, lo + 128)])

    def acc(t, j, tr):
        return col("acc", 20 * t + 5 * j + tr)

    def diff_pe(t, src, lo, ps, first=True, second=True, cols=H):
        for c in range(cols // 512):
            a = lo + 512 * c
            if first:
                mm(r(ps, 512 * c, 512 * c + 512), r("Ip"), r(src, a, a + 512), True, False)
            if second:
                mm(r(ps, 512 * c, 512 * c + 512), r("In"), r("M%d" % t, a, a + 512), False, True)

    turn = [0]

    def size_a(t, j, tr, ps, cols=H):
        turn[0] = H - turn[0]
        act(r("junk", turn[0], turn[0] + cols), r(ps, 0, cols), AF.Abs, acc=acc(t, j, tr))

    def size_v(t, j, tr, x):
        o = acc(t, j, tr)
        op("v", lambda: V.tensor_reduce(o[0], x[0], AX.X, ALU.add, apply_absolute_value=True), [o], [x])

    def diff_v(t, d, x, lst, base, lo, hi):
        tt(r(d, lo, hi), ind(r(x), r(lst, base + lo // 16, base + hi // 16)), r("M%d" % t, lo, hi), ALU.subtract)

    def size_s(t, j, tr, d, lo, hi):
        act(r(d, lo, hi), r(d, lo, hi), AF.Abs, acc=acc(t, j, tr))

    def size_pe(d, lo, hi, first, last):
        ts(r("dP", lo, hi), r(d, lo, hi), 0.0, ALU.max)
        for a in range(lo, hi, 128):
            mm(r("pL", 128, 256), r(d, a, a + 128), r("Gn"), first and a == lo, False)
            mm(r("pL", 128, 256), r("dP", a, a + 128), r("Gp"), False, last and a == hi - 128)

    def row_sums(ps, row, weights):
        for a in range(0, W, 128):
            mm(ps, r(row, a, a + 128), r(weights), a == 0, a == W - 128)

    def greater(tr, x):
        send([([r(x), r("M1")], [(nxt, r(LAND[tr]))], allm, "fx%d" % tr, 2)])
        arrive("fx%d" % tr, len(eng), [r(LAND[tr])])

    def greater_back(tr, ps):
        act(piece("So", tr, 128), ps)
        send([([piece("So", tr, 128)], [(prv(me), piece("Si", tr, 128))], allm, "fb%d" % tr, 0)])
        arrive("fb%d" % tr, len(eng), [piece("Si", tr, 128)])

    def elect(t):
        both = (("pT", 272), ("pB", 0))
        keys, sums = [r(ps, lo, lo + 5) for ps, lo in both]
        mm(keys, r("Grp8"), r("Tc", 0, 5), True, False)
        mm(sums, r("Grp8"), r("acc", 15, 20), True, False)
        parts = [(3, r("S3"))]
        if t:
            parts = [(0, piece("Si", 0, 128))] + parts + [(1, piece("Si", 1, 128))]
            for ps, lo in both:
                mm(r(ps, lo, lo + 2), r("Grp8n"), r("accn", 0, 2), False, False)
                mm(r(ps, lo, lo + 2), r("Sm"), r("eight", 0, 2), False, False)
        for tr, x in parts:
            for ps, lo in both:
                mm(r(ps, lo + tr, lo + tr + 1), x, col("eight", 0), False, False)
        for j in range(3):
            x = r("acc", 20 * t + 5 * j, 20 * t + 5 * j + 5)
            mm(keys, r("Grp8"), x, False, j == 2)
            mm(sums, r("Grp8"), x, False, j == 2)
        for j, i in enumerate((keys, sums)):
            o = col("km", 4 * j)
            op("v", lambda o=o, i=i: V.tensor_reduce(o[0], i[0], AX.X, ALU.min), [o], [i])
        ts(r("eo"), r("base5"), col("km", 0), ALU.add, col("km", 4), ALU.subtract)
        cp(r("cU%d" % t), ind(r("Lall"), r("eo")))

    def last_trial(t, x, between=nothing):
        nb = "nbR%d" % t
        cuts = (0,) + LAST[t] + (W,)
        for j in range(3):
            diff_v(t, "d4", x, nb, 128, cuts[j], cuts[j + 1])
            if j < 2:
                size_s(t, j, 4, "d4", cuts[j], cuts[j + 1])
            if j == 0:
                between()
        lall(4, nb, 128)()
        size_v(t, 2, 4, r("d4", cuts[2], W))

    def lall(tr, name, lo):
        return lambda: cp(r("Lall", tr, 640, 5), r(name, lo, lo + 128))

    def mean_send(t):
        to = [(q, r("ivR%d" % t, 128 * k, 128 * k + 128)) for k, q in enumerate(dests)]
        send([([r("ivS%d" % t)], x, bits(eng[j::2]), "mu%d" % t, 0) for j, x in enumerate((to[:nfar], to[nfar:]))])
        arrive("mu%d" % t, len(eng) // 2 * (N - 1), [r("ivR%d" % t)])

    def mean_sum(t):
        o = r("pT", 384, 512)
        mm(o, r("I8"), r("cmu"), True, False)
        mm(o, r("ivS%d" % t), r("I8"), False, False)
        for k in range(N - 1):
            mm(o, r("ivR%d" % t, 128 * k, 128 * k + 128), r("I8"), False, k == N - 2)
        if t:
            mean_f16()
        ts(r("muU%d" % t), o, MAGIC, ALU.add, MAGIC, ALU.subtract)

    def mean_f16():
        ts(r("c16"), r("pT", 384, 512), MAGIC, ALU.add, MAGIC, ALU.subtract)

    def add_template(lo, hi):
        dma("g", r("V2", lo, hi, p=(16, 128)), r("M1", lo, hi, p=(0, 112)), "accm%d" % (lo > 0), accum_op=ALU.add)
        dma("g", r("V2", lo, hi, p=(0, 16)), r("M1", lo, hi, p=(112, 128)), "accm%d" % (lo > 0), accum_op=ALU.add)

    waits = list(zip(WAITS[:-1], WAITS[1:]))

    dma("s", rows("dG", 0, 128), r("gam"), "ldg")
    dma("a", rows("dG", 128, 144), r("gam", p=(0, 16)), "ldg")
    dma("s", r("gamI"), r("gam"), "lgam")
    dma("a", r("X0"), r("xs"), "lxs")
    dma("s", r("ewI"), r("ew"), "lew")
    own_piece(0, "xs")
    op("g", lambda: g.iota(T["iP"][:, :], [[112, 2]], 0, 1), [r("iP")], [])
    iota(r("iF"), [[1, 144]], 0, 0)
    iota(r("iB"), [[1, 128]], 0, 0)
    iota(col("fD", 1), [[0, 1]], 2050, 2)
    iota(r3("C3", 0, 18), [[0, 144]], 4096, 0)
    act(r("pT", 0, 128), r("iF", 0, 128), scale=0.0, bias=4096.0)
    act(r("pT", 128, 257), r("iF", 0, 129), scale=0.0, bias=4096.0)
    act(r("pT", 0, 256, 32), r("iF", 0, 8), scale=0.0, bias=col("fD", 1))
    send([([rows("dG", 16, 144)], [((me - 1) % N, r("nbI"))], allm, "nbg0", 0)])
    arrive("nbg0", len(eng), [r("nbI")])
    ms(r("WIN", 0, 256), LOW)
    ts(col("iC", 0), col("iP", 0), 15, ALU.bitwise_and)
    ts(r("iC", 1, 3), r("iP"), 112, ALU.bitwise_and)
    ms(r("WIN", 256, 512), LOW)
    cp(r("fC", 0, 3), r("iC", 0, 3))
    ms(r("st2", 0, 512), 2.0)
    ts(r("EQ"), r("iF", 0, 16), col("fC", 0), ALU.is_equal)
    ts(r("GT"), r("iF", 0, 16), col("fC", 0), ALU.is_gt, 128.0, ALU.mult)
    ms(r("st2", 512, H), 2.0)
    for h in range(1, 4):
        dma("s", piece("WIN", h, 512), r("WIN", 0, 512), "fill")
    dma("s", r("rhoS", 0, 5), r("rho"), "lrho")
    for a in range(16):
        o = r("VAL", 128 * a, 128 * a + 128)
        if a < NVAL_V:
            ts(o, r("iB"), col("EQ", a), ALU.mult, col("GT", a), ALU.add)
        else:
            act(o, r("iF", 0, 128), scale=col("EQ", a), bias=col("GT", a))
    cp(r("gamU"), r("gamI"))
    ts(col("TOP", 15), col("EQ", 0), -1.0, ALU.mult)
    ts(r("sel"), r("iF", 0, 128, 16), col("fC", 1), ALU.is_equal)
    send([([piece("X0", q)], [(q, slot(0, k))], two(k), "rs0", 0) for k, q in enumerate(dests)])
    arrive("rs0", 2 * (N - 1), [rows("dM0", 128, 128 * N)])
    iota(r3("C3", 18, 32), [[0, 112]], 0, 0)
    iota(r("fD", 5, 6), [[0, 1]], 0, 1)
    iota(r("fD", 6, 7), [[0, 1]], 0, int(UNIT))
    iota(r("iA"), [[0, 8], [1, 16]], 0, 0)
    iota(r("one"), [[0, 128]], 1, 0)
    iota(r("st2", H, 1664), [[0, 1664 - H]], 2, 0)
    fold(0, "M0")
    iota(r("st2", 1664, W), [[0, W - 1664]], 2, 0)
    iota(r("neg"), [[0, 128]], -1, 0)
    ident(r("In"), r("neg"))
    iota(r("acc"), [[0, 40]], 0, 0)
    iota(r("iG"), [[16, 8], [0, 16]], 0, 0)
    iota(r("fD", 2, 4), [[16, 2]], -1, 1)
    echo(0, "M0")
    late = 0 if PW * me < H else H
    early = H - late

    warp_top("G0", "VAL", "gamU", [lambda: cp(r("ewU", 0, 256), r("ewI", 0, 256)),
                                   lambda: ts(r("sel2"), r("iF", 0, 128, 16), col("fC", 2), ALU.is_equal),
                                   lall(1, "ewI", 0)])
    gather_a("dA", "X0", "ewU", 0, W)
    ts(r("Kd"), r("iB"), col("fD", 5), ALU.is_equal, col("fD", 6), ALU.mult)
    ts(r("Ip"), r("iB"), col("fD", 5), ALU.is_equal)
    ts(r("lane"), r("iA"), col("fC", 0), ALU.is_equal)
    lall(2, "ewI", 128)()
    blocks(0, [lambda: cp(r("nbR0", 0, 128), r("nbI")), lall(3, "nbI", 0)]
           + [lambda lo=lo, hi=hi: gather_v("d2", "X0", "ewU", lo, hi, 128) for lo, hi in waits[1:]])
    diff_pe(0, "X0", early, "pA", second=False)
    diff_pe(0, "dA", early, "pC", second=False)
    diff_pe(0, "X0", late, "pB", second=False)
    gather_a("d2", "X0", "ewU", 0, WAITS[1], base=128)
    gather_a("d2", "X0", "ewU", WAITS[-1], W, base=128)
    gather_a("d3", "X0", "nbR0", late, late + 512)
    act(r("Lall", 0, 640, 5), r("iF", 0, 128), scale=16.0, bias=col("fC", 0))
    act(r("Tc"), r("iF", 0, 8), scale=1.0 / 128)
    act(r("base5"), r("Lall", 0, 40, 5), scale=5.0)
    diff_pe(0, "dA", early, "pC", first=False)
    size_a(0, 0, 1, "pC")
    diff_pe(0, "X0", early, "pA", first=False)
    size_a(0, 0, 0, "pA")
    conv_turned("pL", 128, "IR", "sel2")
    diff_v(0, "d3", "X0", "nbR0", 0, early, early + 512)
    counted(0, r("iv16"), 128)
    turn_back("iv16", "pL", 384)
    ts(r("Grp8"), r("iG"), col("fC", 1), ALU.is_equal, 8.0, ALU.mult)
    cp(r("nbS0", 128, 256), r("pL", 384, 512))
    dma("s", r("payS"), r("pay"), "lpay", [neighbour(0, 128, "nb0")])
    iota(r("eight"), [[0, 8]], 8, 0)
    iota(r("st1"), [[0, W]], 1, 0)
    act(r("Gp"), r("Grp8"), scale=0.25)
    act(r("Gn"), r("Grp8"), scale=-0.125)
    diff_pe(0, "X0", late, "pB", first=False)
    diff_pe(0, "d2", early, "pC")
    diff_v(0, "d3", "X0", "nbR0", 0, early + 512, early + H)
    size_a(0, 1, 0, "pB")
    diff_pe(0, "dA", late, "pA")
    size_a(0, 0, 2, "pC")
    diff_v(0, "d3", "X0", "nbR0", 0, late + 512, late + H)
    diff_pe(0, "d2", late, "pB")
    size_a(0, 1, 1, "pA")
    diff_pe(0, "d3", late, "pC", cols=512)
    size_a(0, 1, 2, "pB")
    size_pe("d3", early, early + H, True, False)
    size_pe("d3", late + 512, late + H, False, True)
    size_a(0, 1, 3, "pC", 512)
    last_trial(0, "X0", lambda: act(r("S3"), r("pL", 128, 256)))
    act(r("R9", 4, 9), r("rhoS", 0, 5))
    for j in range(4):
        act(col("R9", j), col("rhoS", 4 - j))
    act(r("I8"), r("Ip"), scale=1.0 / N)
    for tab, sc in ((1, 32.0), (2, 1.0 / 32), (3, 1.0 / N)):
        act(r("R9", 16 * tab, 16 * tab + 9), r("R9", 0, 9), scale=sc)
    elect(0)

    warp_top("G1", "G0", "cU0", [lambda: ts(r("fD", 4, 5), col("EQ", 0), -1.0, ALU.mult, 1.0, ALU.add),
                                 lambda: ts(r("S1"), r("iB"), col("fD", 2), ALU.is_equal, col("fD", 4), ALU.mult),
                                 lambda: ts(r("S2"), r("iB"), col("fD", 3), ALU.is_equal, col("EQ", 0), ALU.mult)])
    for c, ks in enumerate(halves):
        for lo, hi in runs((far, near)[c]):
            gather_a("X1", "X0", "cU0", lo, hi)
        send([([piece("X1", dests[k])], [(dests[k], slot(1, k))], (two, four)[c](k), "rs1", 0) for k in ks])
    own_piece(1, "X1")
    arrive("rs1", 2 * nfar + 4 * (nfar - 1), [rows("dM1", 128, 128 * N)])
    ts(r("D15"), r("Ip"), col("EQ", 15), ALU.mult)
    tt(r("S1"), r("S1"), r("Ip"), ALU.subtract)
    cp(r("c16"), r("cU0"))
    ms(r("C4", 0, 127), 4.0)
    ts(col("C4", 127), col("EQ", 15), 4.0, ALU.add)
    slopes_pe()
    blocks(1, [lambda: ts(col("iC", 3), col("iP", 1), 127, ALU.bitwise_and), lall(1, "ewI", 256), lall(2, "ewI", 384),
               lambda: slopes_v(0), lambda: cp(r("ewU", 256, 512), r("ewI", 256, 512)),
               lambda: cp(col("fC", 3), col("iC", 3)), lambda: ms(r("cmu"), -3.5)])
    ts(r("Sh"), r("iB"), col("fC", 3), ALU.is_equal)
    conv_turned("pL", 128, "IR", "sel")
    gather_a("pc", "payS", "cU0", 0, H)
    gather_a("pc", "payS", "cU0", H, W)
    act(r("Grp8n"), r("Grp8"), scale=-1.0)
    act(r("I32b"), r("Ip"), scale=1.0 / 32)
    act(r("I128b"), r("Ip"), scale=1.0 / (16 * N))
    weigh("V1", "pc", 0, 0, 512)
    counted(1, r("ivS0"), 128)
    mean_send(0)
    fold(1, "MP")
    echo(1, "MP")
    weigh("V1", "pc", 0, 512, W)
    mean_sum(0)

    def shifted():
        mean_f16()
        mm(r("pL", 384, 512), r("Sh"), r("c16"), True, True)
        slopes_pe()

    def warp_out():
        cp(r("nbS1", 0, 128), r("pC", 512, 640))
        neighbour(1, 0, "nbg1")

    warp_top("G2", "G1", "muU0", [shifted, nothing, lambda: cp(r("muS"), r("pL", 384, 512))], "sel2")
    slopes_v(1)
    gather_a("tmp", "V1", "muU0", 0, H)
    gather_a("X2", "X1", "muU0", 0, W, acc=col("accn", 0))
    gather_v("M1", "MP", "muS", PW * me, PW * me + PW)
    to_all("M1", "am")
    blocks(2, [warp_out] + [lambda lo=lo, hi=hi: weigh("V2", "tmp", 1, lo, hi) for lo, hi in waits])
    gather_a("dA", "X2", "ewU", 0, W, base=256, acc=col("accn", 1))
    sums = [r("pC", 0, 128), r("pC", 512, 640)]
    conv_turned("pL", 128, "IR", "sel2")
    greater(0, "X2")
    greater(1, "dA")
    weigh("V2", "tmp", 1, WAITS[-1], H)
    counted(2, r("iv16"), 128)
    turn_back("iv16", "pL", 384)
    diff_v(1, "d3", "X2", "nbR1", 0, 0, 256)
    cp(r("nbS1", 128, 256), r("pL", 384, 512))
    neighbour(1, 128, "nb1")
    row_sums(r("pT", 384, 512), "M1", "Gn")
    gather_a("tmp", "V1", "muU0", H, W)
    gather_a("d2", "X2", "ewU", 0, H, base=384)
    act(r("Sm"), r("pT", 384, 512))
    gather_a("d2", "X2", "ewU", H, W, base=384)
    diff_v(1, "d3", "X2", "nbR1", 0, 256, W)
    diff_pe(1, "d2", 0, "pA")
    row_sums(sums[0], LAND[0], "Gp")
    diff_pe(1, "d2", H, "pB")
    size_a(1, 0, 2, "pA")
    size_s(1, 0, 3, "d3", 0, H)
    greater_back(0, sums[0])
    weigh("V2", "tmp", 1, H, W)
    row_sums(sums[1], LAND[1], "Gp")
    lall(3, "nbR1", 0)()
    size_pe("d3", H, W, True, True)
    size_a(1, 1, 2, "pB")
    greater_back(1, sums[1])
    add_template(0, H)
    add_template(H, W)
    act(r("S3"), r("pL", 128, 256))
    last_trial(1, "X2")
    elect(1)

    def slopes_3():
        cp(r("c16"), r("cU1"))
        slopes_pe()

    warp_top("G3", "G2", "cU1", [slopes_3, nothing, lambda: slopes_v(2)], "sel")
    gather_v("X3", "X2", "cU1", PW * prv(me), PW * prv(me) + PW)
    for c, ks in enumerate(halves):
        for lo, hi in runs([prv(dests[k]) for k in ks]):
            gather_a("X3", "X2", "cU1", lo, hi)
        send([([piece("X3", prv(dests[k]))], [(dests[k], piece("xq", k))], (two, four)[c](k), "ax%d" % c, 0) for k in ks])
        arrive("ax%d" % c, 2 * (c + 1) * len(ks), [piece("xq", k) for k in ks])
    last, own = PW * dests[-1], PW * me
    cuts = [(last, last + 96), (last + 96, last + 160), (last + 160, last + PW), (own, own + 160), (own + 160, own + PW)]
    blocks(3, [lambda: cp(r("glU"), r("pC", 512, 640))]
           + [lambda lo=lo, hi=hi: gather_v("P3", "payS", "glU", lo, hi) for lo, hi in cuts])
    for c, ks in enumerate(halves):
        for k in ks:
            if k < N - 2:
                gather_a("P3", "payS", "glU", PW * dests[k], PW * dests[k] + PW)
        send([([piece("P3", dests[k])], [(dests[k], piece("pq", k))], two(k), "ap%d" % c, 0) for k in ks])
        arrive("ap%d" % c, 2 * len(ks), [piece("pq", k) for k in ks])
        if c == 0:
            srcs = [piece("xq", k) for k in range(N - 1)] + [piece("X3", prv(me))]
            send([(srcs, [(prv(me), r("qM"))], allm, "aq", 2)])
            arrive("aq", len(eng), [r("qM")])
            for k, x in enumerate(srcs):
                mm(r("pB", 0, PW), r("Ip"), x, k == 0, k == N - 1)
    conv_turned("pL", 128, "IR", "sel")
    for lo, hi in zip(UC[:-1], UC[1:]):
        gather_a("U", "V2", "cU1", lo, hi)
        weigh("V3", "U", 2, lo, hi)
        if lo == 0:
            counted(3, r("ivS1"), 128)
            act(r("qSs"), r("pB", 0, PW))
            send([([r("qSs")], [(prv(me), r("qS"))], allm, "as", 0)])
            arrive("as", len(eng), [r("qS")])
            mean_send(1)
    mm(r("pA", 0, PW), r("I8"), piece("P3", me), True, False)
    for k in halves[0]:
        mm(r("pA", 0, PW), r("I8"), piece("pq", k), False, False)
    mm(r("pA", 0, PW), r("I128b"), r("qS"), False, False)
    mm(r("pA", 0, PW), r("I32b"), r("qM"), False, False)
    for k in halves[1]:
        mm(r("pA", 0, PW), r("I8"), piece("pq", k), False, k == N - 2)
    act(piece("QM", me), r("pA", 0, PW))
    to_all("QM", "aqm")
    mean_sum(1)
    slopes_pe()
    slopes_v(3)

    order = [far[(mine + j) % nfar] for j in range(1, nfar)] + served + [me]
    for k, q in enumerate(order):
        gather_a("tmp", "V3", "muU1", PW * q, PW * q + PW, olo=PW * k)
        tt(piece("U", k), ind(r("R9", 48, 57), r("sU3", 16 * q, 16 * q + 16)), piece("tmp", k), ALU.mult)
        for c, ks in enumerate(TAIL):
            if k == ks[-1]:
                send([([piece("U", i)], [(served[1 + i % nfar], piece("uq", i))], bits(eng[j::len(ks)]), "au%d" % c, 0)
                      for j, i in enumerate(ks)])
                arrive("au%d" % c, len(eng), [piece("uq", i) for i in ks])
    send([([piece("uq", i) for i in range(nfar - 1)] + [piece("U", nfar - 1)], [(mate, piece("uq", nfar - 1))], allm,
           "auf", 1)])
    arrive("auf", len(eng), [piece("uq", nfar - 1)])
    run = r("pC", 0, PW)
    tt(r("qg"), ind(r("QM"), r("muU1", 16 * me, 16 * me + 16)), piece("U", N - 1), ALU.add)
    tt(run, r("qg"), piece("uq", nfar), ALU.add)
    tt(run, run, piece("uq", nfar + 1), ALU.add)
    tt(run, run, piece("uq", nfar + 2), ALU.add)
    tt(r("ysb"), run, piece("uq", nfar - 1), ALU.add)
    dma("s", r("y"), r("ysb"), "sty")
    _emit(g, T, ops)
